import numpy as np, ml_dtypes
CORES = [48,51,52,55]
N = 4
BF = ml_dtypes.bfloat16
def gentries(a):
    return np.ascontiguousarray(a.reshape(8, 16, -1).transpose(0, 2, 1)).reshape(8, -1)
def gtable(e):
    e = np.asarray(e); return np.ascontiguousarray(e.reshape(8, -1, 16).transpose(0, 2, 1)).reshape(128, -1).astype(np.int32)
W, P, R, S, E, LM = 3072, 256, 4, 1, 1, 14
def pack(nb, x, v, z, th):
    return {"nb": np.ascontiguousarray(nb.reshape(N, 128, W)).astype(np.int32), "xd": np.ascontiguousarray(x.reshape(N, 128, W)).astype(np.float32).astype(BF),
            "pv": np.stack([gtable(a) for a in v]), "pz": np.ascontiguousarray(z.reshape(N, 128, P)).astype(np.float32).astype(BF), "th": np.repeat(th, 16, axis=1).astype(np.int32)}
def blur(rng, pat, sel, m):
    b = np.stack([pat[g][sel[:, g]] for g in range(8)], axis=1).transpose(0, 1, 3, 2)
    b = np.clip(b + rng.integers(-1, 2, b.shape) * (rng.random(b.shape) < 0.25), 0, 15)
    return np.where(np.arange(16)[:, None] < m[:, :, None, :], b, rng.integers(0, 16, b.shape))
def alike(rng, s, want):
    o = np.argsort(s, kind="stable"); n = np.bincount(s, minlength=8); b = np.add.accumulate(n) - n
    return o[np.minimum(b[want] + (rng.random(want.shape) * n[want]).astype(np.int64), len(s) - 1)]
def parts(rng):
    pat = rng.integers(0, 16, (8, 8, 16))
    s = np.where(rng.random((N, 8, W)) < 0.7, rng.integers(0, 8, (1, 8, W)), rng.integers(0, 8, (N, 8, W)))
    x = blur(rng, pat, s, rng.integers(0, 17, (N, 8, W)))
    sp = rng.integers(0, 8, (N, 8, P)); z = blur(rng, pat, sp, rng.integers(0, 17, (N, 8, P)))
    nb = rng.integers(0, W, (N, 8, 16, W)); v = rng.integers(0, W, (N, 8, P))
    for q in range(N):
        for g in range(8):
            w = alike(rng, s[q, g], np.broadcast_to(s[q, g], (16, W)))
            nb[q, g] = np.where(rng.random((16, W)) < 0.5, w, nb[q, g])
            v[q, g] = np.where(rng.random(P) < 0.6, alike(rng, s[q, g], sp[q, g]), v[q, g])
    th = np.stack([rng.integers(40, 91, (N, 8)), rng.integers(25, 76, (N, 8))], axis=-1)
    return nb, x, v, z, th
def setup_inputs(rng):
    return pack(*parts(rng))
def uneven(rng, shape, n):
    a = np.minimum((n * rng.random(shape) ** 3).astype(np.int64), n - 1)
    return np.where(rng.random(shape[:-1] + (1,)) < 0.5, a, n - 1 - a)
def setup_inputs_spread(rng):
    def digits(n):
        top = 1 << rng.integers(0, 5, (N, 8, 1, n)); a = np.minimum((rng.random((N, 8, 16, n)) * top).astype(np.int64), 15)
        return np.where(rng.random((N, 8, 1, n)) < 0.5, a, 15 - a)
    return pack(uneven(rng, (N, 8, 16, W), W), digits(W), uneven(rng, (N, 8, P), W), digits(P), rng.integers(0, 242, (N, 8, 2)))
def setup_inputs_ends(rng):
    def digits(n):
        return np.where(rng.random((N, 8, 1, n)) < 0.5, 15 * rng.integers(0, 2, (N, 8, 1, n)), 15 * rng.integers(0, 2, (N, 8, 16, n)))
    x = digits(W); x[..., 0] = 0; x[..., W - 1] = 15; x[:, 1:6:2, :, 0] = 15; x[:, 1:6:2, :, W - 1] = 0
    z = digits(P); z[..., 0] = 0; z[..., 1] = 15; z[..., P - 2] = 15; z[..., P - 1] = 0
    nb = np.where(rng.random((N, 8, 16, W)) < 0.25, rng.integers(0, W, (N, 8, 16, W)), (W - 1) * rng.integers(0, 2, (N, 8, 16, W)))
    nb[:, 7, :, W - 1] = W - 1
    v = np.where(rng.random((N, 8, P)) < 0.25, rng.integers(0, W, (N, 8, P)), (W - 1) * rng.integers(0, 2, (N, 8, P)))
    v[..., 0] = 0; v[..., 1] = W - 1; v[..., P - 2] = W - 1; v[..., P - 1] = W - 1
    pairs = np.array([[0, 0], [0, 241], [241, 0], [241, 241]])
    th = pairs[np.argsort(rng.random((N, 8)), axis=1) & 3]; th[N - 1] = pairs[np.array([0, 3, 2, 1, 0, 2, 3, 1])]; th[:, 2] = np.array([120, 121])
    return pack(nb, x, v, z, th)
def setup_inputs_corners(rng):
    M = P // 4; nb = np.zeros((N, 8, 16, W), np.int64); x = np.zeros((N, 8, 16, W), np.int64); v = np.zeros((N, 8, P), np.int64); z = np.zeros((N, 8, 16, P), np.int64)
    th = np.zeros((N, 8, 2), np.int64); th[..., 0] = 40; th[..., 1] = 24
    rows = np.arange(16)[:, None]
    for q in range(N):
        for g in range(8):
            zz = rng.integers(4, 12, 16)[:, None]; o = rng.permutation(W); place = o[:P]; cont = o[P:P + 16 * M].reshape(M, 16); good = o[P + 16 * M::2]; miss = o[P + 16 * M + 1::2]
            lw = rng.choice(np.array([0, 1, 2, 7, LM - 1, LM, LM + 1, 15, 16]), P); lv = np.minimum(lw, LM)[:M]; case = rng.permutation(np.arange(M) & 7)
            d = np.zeros(W, np.int64); d[good] = rng.choice(np.array([0, 1, 23]), len(good)); d[miss] = rng.choice(np.array([24, 24, 25, 39, 40]), len(miss))
            d[cont] = rng.choice(np.array([40, 40, 41, 54, 55, 56]), (M, 16)); j = np.flatnonzero(case == 0); d[cont[j, lv[j]]] = 39
            sign = 1 - 2 * rng.integers(0, 2, (16, W)); diff = (d >> 4) + (np.argsort(rng.random((16, W)), axis=0) < (d & 15))
            diff[:, place] = np.where(rows < lw, rng.integers(0, 2, (16, P)), np.where(rows == lw, 2, rng.integers(0, 5, (16, P))))
            x[q, g] = zz + sign * diff
            w = rng.random((16, W)); b = np.where(w < 0.15, np.arange(W), np.where(w < 0.25, 0, np.where(w < 0.35, W - 1, rng.integers(0, W, (16, W)))))
            b[:, place[:M]] = cont.T
            for e in range(E + 1): b[(lv + e)[:, None], cont] = rng.choice(miss, (M, 16))
            last = (lv + 15) & 15
            for c, e, k in ((1, 0, last), (2, 0, lv), (3, 1, last), (4, E, lv), (6, 0, last), (7, 0, 0 * lv + 15), (7, 0, 0 * lv)):
                j = np.flatnonzero(case == c); b[lv[j] + e, cont[j, k[j]]] = rng.choice(good, len(j))
            j = np.flatnonzero(case == 6); b[(lv[j] + 1)[:, None], cont[j]] = rng.choice(good, (len(j), 16))
            nb[q, g] = b
            pl = place.copy(); n = P - M; pl[M:] = np.where(rng.random(n) < 0.25, rng.choice(place[:M], n), pl[M:]); pl[P - 1] = W - 1; pl[P - 2] = 0
            t = np.repeat(zz, P, axis=1); t[:, M:] = np.where(rng.random(n) < 0.5, np.clip(zz + rng.integers(-3, 4, (16, n)), 0, 15), rng.integers(0, 16, (16, n)))
            r = rng.permutation(P); v[q, g] = pl[r]; z[q, g] = t[:, r]
    th[1, :, 0] = 0; th[N - 1, :4] = np.array([[0, 0], [0, 241], [241, 0], [241, 241]])
    return pack(nb, x, v, z, th)
def setup_inputs_crowd(rng):
    nb, x, v, z, th = parts(rng)
    v[:, 0] = rng.integers(0, W, (N, 1)); v[:, 1] = rng.integers(0, W - 1, (N, 1))
    for q in range(N): v[q, 1, rng.integers(0, P)] = W - 1
    v[:, 2] = rng.choice(np.array([0, 3, W // 2, W - 1]), (N, P)); v[:, 3] = np.repeat(v[:, 3, :P // 2], 2, axis=1)
    nb[:, 4, :15] = rng.integers(0, W, (N, 1, 1)); nb[:, 5] = nb[:, 5, :1]
    v[:, 6] = rng.integers(0, W, (N, 1)); z[:, 6] = z[:, 6, :, :1]; v[:, 7] = W - 1
    th[0, :, 0] = 0; th[1, :, 0] = 0; th[1, 7, 0] = 1
    x[1, 7, 15] = np.minimum(x[1, 7, 15], 14); z[1, 7, 15] = 15; j = rng.integers(0, P); u = rng.integers(0, W - 1)
    nb[1, 7, :, v[1, 7, j]] = u; z[1, 7, :, j] = x[1, 7, :, u]
    th[2, :7, 0] = 241; th[2, 7, 0] = 0
    return pack(nb, x, v, z, th)
def setup_inputs_calm(rng):
    M = P - P // 8; rows = np.arange(16)[:, None]
    nb = rng.integers(0, W, (N, 8, 16, W)); x = rng.integers(0, 16, (N, 8, 16, W))
    n = np.argsort(rng.random((8, W)), axis=1)[:, :(R + 1) * M].reshape(8, R + 1, M)
    th = np.zeros((N, 8, 2), np.int64); th[..., 0] = rng.integers(16, 33, (N, 8))
    z0 = np.clip(rng.integers(0, 16, (8, 16, M)) + rng.integers(-1, 2, (N, 8, 16, M)), 0, 15); z = z0
    at = np.where(rows < rng.integers(0, 17, (N, 8, 1, M)), np.clip(z + rng.integers(-1, 2, z.shape), 0, 15), rng.integers(0, 16, z.shape))
    o = rng.permutation(N); want = np.zeros((R - 1, N), np.int64)
    for t in range(R - 1): want[t, o] = (np.arange(N) + t) & 3
    want[0, o[0]] = 8 * P; want[0, o[1]] = 8 * P - 1
    weight = 1 + (np.arange(M) < P - M).astype(np.int64); a = np.zeros(N, np.int64)
    for t in range(R):
        if t > 0: z = np.roll(z, S, axis=0)
        near = (np.abs(at - z) <= 1).astype(np.int64)
        l = np.minimum(np.add.reduce(np.multiply.accumulate(near, axis=2), axis=2), LM)
        for q in range(N):
            for g in range(8):
                x[q, g][:, n[g, t]] = at[q, g]; nb[q, g][l[q, g], n[g, t]] = n[g, t + 1]
                if t < R - 1: nb[q, g][15, n[g, t]] = n[g, t + 1]
        fail = rng.random((N, 8, M)) < 0.4; over = np.where(rng.random((N, 8, M)) < 0.5, 0, rng.integers(0, 8, (N, 8, M)))
        if t < R - 1:
            over = 0 * over
            for q in range(N):
                k = int(want[t, q]); j = rng.permutation(8 * (2 * M - P))[:min(k, 8 * P - k)]
                fail[q] = k > 3; fail[q, j & 7, P - M + (j >> 3)] = k < 4
        h = th[..., 0][:, :, None] + (a & 15)[:, None, None]
        under = np.where(rng.random((N, 8, M)) < 0.5, 0, rng.integers(0, 16, (N, 8, M)))
        need = np.where(fail, h + over, h - 1 - under)[:, :, None, :]
        m = rng.integers(0, 10, (N, 8, 1, M)); base = need // (16 - m)
        place = np.argsort(np.argsort(rng.random(z.shape) + 2 * (rows < m), axis=2), axis=2)
        diff = np.where(rows >= m, base + (place < need - base * (16 - m)), 0)
        come = z + np.where(z < 8, diff, -diff)
        a = np.add.reduce((fail * weight).reshape(N, -1), axis=1)
        z = np.where(fail[:, :, None, :], np.abs(z - at), z); at = come
    v = np.zeros((N, 8, P), np.int64); zp = np.zeros((N, 8, 16, P), np.int64); who = np.concatenate([np.arange(M), np.arange(P - M)])
    for q in range(N):
        for g in range(8):
            x[q, g][:, n[g, R]] = at[q, g]
            r = who[rng.permutation(P)]; v[q, g] = n[g, 0][r]; zp[q, g] = z0[q, g][:, r]
    return pack(nb, x, v, zp, th)
def check_inputs(d):
    bad = []
    for k, hi in (("nb", W - 1), ("xd", 15), ("pv", W - 1), ("pz", 15), ("th", 241)):
        a = np.asarray(d[k]).astype(np.float64)
        if not (np.min(a) >= 0 and np.max(a) <= hi): bad.append("range of " + k)
        if np.any(a != np.floor(a)): bad.append("whole numbers of " + k)
    t = np.asarray(d["th"]).reshape(N, 8, 16, 2)
    if np.any(t != t[:, :, :1]): bad.append("rows of a group alike in th")
    return bad
def dist(x, z, u):
    s = np.zeros(u.shape, np.int64)
    for p in range(16):
        s = s + np.abs(np.take_along_axis(x[:, :, p], u.reshape(N, 8, -1), 2).reshape(u.shape) - z[:, :, p][:, :, None, :])
    return s
def reference(nb, xd, pv, pz, th):
    c = nb.astype(np.int64).reshape(N, 8, 16, W); x = xd.astype(np.float32).astype(np.int64).reshape(N, 8, 16, W)
    v = np.stack([gentries(a) for a in pv]).astype(np.int64); z = pz.astype(np.float32).astype(np.int64).reshape(N, 8, 16, P)
    h = th.astype(np.int64).reshape(N, 8, 16, 2)[:, :, 0]; a = np.zeros(N, np.int64)
    for t in range(R):
        if t > 0: v = np.roll(v, S, axis=0); z = np.roll(z, S, axis=0)
        xv = np.take_along_axis(x, v[:, :, None, :], 3); con = np.take_along_axis(c, v[:, :, None, :], 3)
        near = (np.abs(xv - z) <= 1).astype(np.int64)
        l = np.minimum(np.add.reduce(np.multiply.accumulate(near, axis=2), axis=2), LM)
        tl = np.take_along_axis(con, l[:, :, None, :], 2)
        ok = dist(x, z, tl)[:, :, 0] < h[:, :, 0, None] + (a & 15)[:, None, None]
        new = np.where(ok, tl[:, :, 0], con[:, :, 15]); todo = ~ok; fixed = np.zeros(ok.shape, bool)
        order = (l[:, :, None, :] + np.arange(16)[:, None]) & 15
        for e in range(E + 1):
            cand = np.take_along_axis(c.reshape(N, 8, 16 * W), ((l + e)[:, :, None, :] * W + con).reshape(N, 8, -1), 2).reshape(N, 8, 16, P)
            hit = np.take_along_axis(dist(x, z, cand) < h[:, :, 1, None, None], order, 2); cand = np.take_along_axis(cand, order, 2)
            got = todo & np.any(hit, axis=2)
            new = np.where(got, np.take_along_axis(cand, np.argmax(hit, axis=2)[:, :, None, :], 2)[:, :, 0], new)
            fixed = fixed | got; todo = todo & ~got
        a = np.add.reduce((~ok).astype(np.int64).reshape(N, -1), axis=1)
        for q in range(N):
            for g in range(8):
                i = np.flatnonzero(fixed[q, g]); u, k = np.unique(v[q, g, i], return_index=True); i = i[k]
                c[q, g][l[q, g][i], u] = new[q, g][i]
                if t < R - 1:
                    u, i = np.unique(v[q, g], return_index=True)
                    x[q, g][:, u] = (xv[q, g][:, i] + z[q, g][:, i]) >> 1
        z = np.where(todo[:, :, None, :], np.abs(z - xv), z); v = new
    return {"ynb": c.reshape(N, 128, W).astype(np.float32), "yv": np.stack([gtable(b) for b in v]).astype(np.float32), "yz": z.reshape(N, 128, P).astype(np.float32).astype(BF)}

@@ -1,0 +1,538 @@
+import math
+from concourse.mybir import dt, AluOpType, AxisListType, ActivationFunctionType
+
+W = 3072
+LN2 = math.log(2.0)
+WT = W + 256
+
+SCRATCH = {
+    "nbI": ("sbuf", [128, W], "int32"), "nbS": ("sbuf", [128, WT], "float32"), "xdS": ("sbuf", [128, WT], "bfloat16"),
+    "idW": ("sbuf", [128, W], "float32"), "yn": ("sbuf", [128, WT], "float32"),
+    "E30": ("sbuf", [128, 16, 256], "bfloat16"), "E31": ("sbuf", [128, 16, 256], "bfloat16"),
+    "Wt": ("sbuf", [128, 2, 256], "bfloat16"), "TRI": ("sbuf", [128, 16, 16], "bfloat16"),
+}
+
+
+def _decl():
+    for names, cols, d in (("maskE zE xg", 4096, "bfloat16"), ("mk", 4096, "float16"), ("dd", 8192, "bfloat16"), ("LQ", 2048, "bfloat16"),
+                           ("dz adz nn nm Pb m2 ohb dlt d0 hb2 cb crb xi xn", 256, "bfloat16"), ("hw fi", 512, "bfloat16"),
+                           ("VB0 VB1 VB2 VB3 co hc lc", 256, "float16"), ("fc pk0 pk1 pk2 pk3", 512, "float16"), ("conF wv rr", 256, "float32"),
+                           ("conU", 256, "uint16"), ("cU", 512, "uint16"), ("TLu offA offR", 16, "uint16"),
+                           ("vS rp q1 o1 o2 o3 yvS tr trS", 16, "float32"), ("pvI", 16, "int32"),
+                           ("thI", 2, "int32"), ("thF", 2, "float32"), ("bB", 1, "float32"), ("Hc hs", 4, "float32"),
+                           ("hsb", 4, "bfloat16"), ("hi0 hi1", 4, "int32"), ("pI pB", 8, "int32"), ("pC", 32, "float32"),
+                           ("ones ZZ ta tb ZB0", 144, "bfloat16"), ("ZFe ZFo ZFa ZF0", 144, "float16"),
+                           ("BLKb D0 D1 D2 CA CB D0n mt M1 M2 M2a In Ih B7 AW VW ALT KE KO", 128, "bfloat16"),
+                           ("BF1 BFh BF15", 128, "float16"),
+                           ("VL0 VL1 VL2 VL3 VN0 VN1 VN2 VN3", 16, "uint16"), ("z0 z1 z2 z3 zn0 zn1 zn2 zn3", 256, "bfloat16")):
+        for n in names.split():
+            SCRATCH[n] = ("sbuf", [128, cols], d)
+    for b in range(8):
+        SCRATCH["ps%d" % b] = ("psum", [128, 512], "float32")
+
+
+_decl()
+DMAS = ["pv", "pz", "th", "xa", "xb", "n0", "n1", "n2", "n3", "y0", "y1", "y2", "y3", "yv", "yz0", "yz1"]
+SEMAPHORES = ["sV", "sS", "sP", "sG", "loc"] + ["d_" + d for d in DMAS] + ["a%s%d" % (n, t) for n in ("l", "y", "z", "v") for t in range(4)]
+
+
+def rank_program(g, core, T, topo):
+    rank = T.rank_of(core)
+    if rank is None:
+        return
+    A, F = AluOpType, ActivationFunctionType
+    ENG = {"V": g.vector, "S": g.scalar, "P": g.tensor, "G": g, "Y": g.sync}
+    cnt = {"sV": 0, "sS": 0, "sP": 0, "sG": 0}
+    known = {q: {} for q in ENG}
+    snap = {}
+    rec = {}
+
+    def need(q, name, lo, hi, wr, out):
+        ps = name[:2] == "ps"
+        for (a, b, q2, s, c, w2) in rec.get(name, ()):
+            if (ps and q2 != q) or (a < hi and lo < b and (wr or w2)):
+                if out.get(s, 0) < c:
+                    out[s] = c
+
+    def note(q, name, lo, hi, s, c, wr):
+        keep = []
+        for x in rec.get(name, []):
+            inside = lo <= x[0] and x[1] <= hi
+            if inside and (wr or (x[2] == q and not x[5] and x[3] == s)):
+                continue
+            keep.append(x)
+        keep.append((lo, hi, q, s, c, wr))
+        rec[name] = keep
+
+    def waits(q, deps):
+        k = known[q]
+        for s in sorted(deps, key=lambda s: -len(snap.get((s, deps[s]), ()))):
+            c = deps[s]
+            if k.get(s, 0) >= c:
+                continue
+            ENG[q].wait_ge(T.sem[s], c)
+            for s2, c2 in snap.get((s, c), {}).items():
+                if k.get(s2, 0) < c2:
+                    k[s2] = c2
+            k[s] = max(k.get(s, 0), c)
+
+    def op(q, emit, reads, writes, sem=None, inc=1):
+        deps = {}
+        for x in reads:
+            need(q, x[1], x[2], x[3], False, deps)
+        for x in writes:
+            need(q, x[1], x[2], x[3], True, deps)
+        waits(q, deps)
+        r = emit(ENG[q])
+        if sem is None:
+            s = "s" + q
+            cnt[s] += 1
+            c = cnt[s]
+        else:
+            s, c = sem, inc
+        r.then_inc(T.sem[s], inc)
+        snap[(s, c)] = dict(known[q])
+        for x in reads:
+            note(q, x[1], x[2], x[3], s, c, False)
+        for x in writes:
+            note(q, x[1], x[2], x[3], s, c, True)
+
+    def X(n, a=0, b=None, st=1):
+        if b is None:
+            b = SCRATCH[n][1][1]
+        return (T[n][:, a:b:st] if st > 1 else T[n][:, a:b], n, a, b)
+
+    def IND(win, off):
+        return (win[0].indirect(off[0]), win, off)
+
+    def rd(x):
+        return [x[1], x[2]] if len(x) == 3 else [x]
+
+    def tt(out, a, b, o):
+        op("V", lambda e: e.tensor_tensor(out[0], a[0], b[0], o), rd(a) + rd(b), [out])
+
+    def ts(out, a, s1, o0, s2=None, o1=None):
+        reads = rd(a)
+        v1, v2 = s1, s2
+        if isinstance(s1, tuple):
+            reads = reads + [s1]; v1 = s1[0]
+        if isinstance(s2, tuple):
+            reads = reads + [s2]; v2 = s2[0]
+        if o1 is None:
+            op("V", lambda e: e.tensor_scalar(out[0], a[0], v1, None, o0), reads, [out])
+        else:
+            op("V", lambda e: e.tensor_scalar(out[0], a[0], v1, v2, o0, o1), reads, [out])
+
+    def cp(out, a):
+        if len(out) == 3:
+            op("V", lambda e: e.tensor_copy(out[0], a[0]), rd(a) + [out[2]], [out[1]])
+        else:
+            op("V", lambda e: e.tensor_copy(out[0], a[0]), rd(a), [out])
+
+    def act(out, a, f, bias=None, scale=None, acc=None):
+        kw = {}
+        reads, writes = rd(a), [out]
+        for nm, v in (("bias", bias), ("scale", scale)):
+            if v is not None:
+                if isinstance(v, tuple):
+                    reads = reads + [v]; kw[nm] = v[0]
+                else:
+                    kw[nm] = v
+        if acc is not None:
+            writes = writes + [acc]; kw["accum_out"] = acc[0]
+        op("S", lambda e: e.activation(out[0], a[0], f, **kw), reads, writes)
+
+    def scp(out, a):
+        act(out, a, F.Copy)
+
+    def mms(items):
+        deps = {}
+        for (o, l, r) in items:
+            need("P", o[1], o[2], o[3], True, deps)
+            need("P", l[1], l[2], l[3], False, deps)
+            need("P", r[1], r[2], r[3], False, deps)
+        waits("P", deps)
+        n = len(items)
+        for j, (o, l, r) in enumerate(items):
+            g.tensor.matmul(o[0], l[0], r[0], j == 0, j == n - 1).then_inc(T.sem.sP, 1)
+        cnt["sP"] += n
+        c = cnt["sP"]
+        snap[("sP", c)] = dict(known["P"])
+        for (o, l, r) in items:
+            note("P", l[1], l[2], l[3], "sP", c, False)
+            note("P", r[1], r[2], r[3], "sP", c, False)
+        for (o, l, r) in items:
+            note("P", o[1], o[2], o[3], "sP", c, True)
+
+    def dma(q, out, oacc, in_, iacc, name):
+        op(q, lambda e: e.dma_start(out, in_), iacc, oacc, sem="d_" + name, inc=16)
+
+    def iota(x, pat, base, cm):
+        kw = {} if SCRATCH[x[1]][2] == "int32" else {"allow_small_or_imprecise_dtypes": True}
+        op("G", lambda e: e.iota(x[0], pat, base, cm, **kw), [], [x])
+
+    def sel(out, a, pat, o, base, cm):
+        op("G", lambda e: e.affine_select(out[0], a[0], pat, o, 0.0, base, cm), [a], [out])
+
+    C4, H2 = W // 4, W // 2
+    dma("Y", T.pvI[:, :], [X("pvI")], T.pv[:, :], [], "pv")
+    dma("Y", T.thI[:, :], [X("thI")], T.th[:, :], [], "th")
+    dma("S", T.z0[:, :], [X("z0")], T.pz[:, :], [], "pz")
+    dma("Y", T.xdS[:, 0:H2], [X("xdS", 0, H2)], T.xd[:, 0:H2], [], "xa")
+    dma("S", T.xdS[:, H2:W], [X("xdS", H2, W)], T.xd[:, H2:W], [], "xb")
+    for j in range(4):
+        a, b = j * C4, (j + 1) * C4
+        dma("Y" if j % 2 == 0 else "S", T.nbI[:, a:b], [X("nbI", a, b)], T.nb[:, a:b], [], "n%d" % j)
+
+    pc = lambda j: X("pC", j, j + 1)
+    iota(X("pI", 0, 1), [[1, 1]], 0, 1)
+    op("V", lambda e: e.memset(T.ones[:, :], 1.0), [], [X("ones")])
+    op("V", lambda e: e.memset(T.AW[:, :], 1.0 / 32), [], [X("AW")])
+    ts(X("pI", 1, 2), X("pI", 0, 1), 15, A.bitwise_and)
+    cp(pc(0), X("pI", 1, 2))
+    for b in range(4):
+        ts(X("pB", b, b + 1), X("pI", 1, 2), b, A.arith_shift_right, 1, A.bitwise_and)
+    cp(X("pC", 1, 5), X("pB", 0, 4))
+    for b in range(4):
+        ts(pc(5 + b), pc(1 + b), 2.0 ** -(1 << b) - 1.0, A.mult, 1.0, A.add)
+    tt(pc(9), pc(5), pc(6), A.mult)
+    tt(pc(10), pc(7), pc(8), A.mult)
+    tt(pc(11), pc(9), pc(10), A.mult)
+    ts(pc(13), pc(0), 14.0, A.is_lt)
+    ts(pc(14), pc(0), 14.0, A.is_equal)
+    ts(pc(15), pc(0), 15.0, A.is_equal)
+    ts(pc(16), pc(11), 32768.0, A.mult)
+    tt(pc(17), pc(16), pc(13), A.mult)
+    tt(pc(18), pc(17), pc(14), A.subtract)
+    ts(pc(19), pc(15), 1.0e9, A.mult)
+    tt(pc(20), pc(18), pc(19), A.add)
+    ts(pc(21), pc(1), -2.0, A.mult, 1.0, A.add)
+    tt(pc(22), pc(21), pc(13), A.mult)
+    ts(pc(23), pc(15), -1.0, A.mult, 1.0, A.add)
+    ts(pc(28), pc(0), -LN2, A.mult)
+    ts(pc(29), pc(0), -LN2, A.mult, -16.0 * LN2, A.add)
+    ts(pc(24), pc(1), -1.0, A.mult, 1.0, A.add)
+    ts(pc(25), pc(0), 0.0, A.is_equal)
+    ts(pc(26), pc(25), 4096.0, A.mult)
+    sel(X("ta", 0, 128), X("ones", 0, 128), [[-16, 8], [0, 16]], A.is_ge, 0, 1)
+    sel(X("BLKb"), X("ta", 0, 128), [[16, 8], [0, 16]], A.is_ge, 15, -1)
+    for n, j in (("VW", 17), ("ALT", 22)):
+        ts(X(n), X("BLKb"), pc(j), A.mult)
+    for n, b in (("D0", 0), ("D2", 2), ("CA", -15), ("CB", -14), ("D1", 1)):
+        sel(X(n), X("BLKb"), [[-1, 128]], A.is_equal, b, 1)
+    ts(X("In"), X("D0"), -1.0, A.mult)
+    ts(X("D0n"), X("D0"), pc(23), A.mult)
+    tt(X("KE"), X("D0n"), X("ALT"), A.add)
+    tt(X("KO"), X("D0n"), X("ALT"), A.subtract)
+    tt(X("mt"), X("CA"), X("D0n"), A.subtract)
+    tt(X("M2a"), X("D2"), X("CB"), A.add)
+    tt(X("M2"), X("M2a"), X("mt"), A.add)
+    tt(X("M1"), X("D1"), X("mt"), A.add)
+    sel(X("ta"), X("ones"), [[-16, 9], [0, 16]], A.is_ge, 0, 1)
+    sel(X("tb"), X("ta"), [[16, 9], [0, 16]], A.is_ge, 15, -1)
+    sel(X("ZZ"), X("tb"), [[0, 9], [1, 16]], A.is_equal, -15, 0)
+    iota(X("rr"), [[0, 16], [1, 16]], 0, 0)
+    iota(X("tr"), [[16, 16]], W - 1536, 0)
+    iota(X("idW"), [[1, W]], -1536, 0)
+    cp(X("VL0"), X("pvI"))
+
+    def more_consts():
+        ts(X("ZFe"), X("ZZ"), pc(24), A.mult)
+        ts(X("ZFo"), X("ZZ"), pc(1), A.mult)
+        cp(X("ZFa"), X("ZZ"))
+        ts((T.TRI[:, :, :], "TRI", 0, 256), X("rr"), pc(0), A.is_gt)
+        ts(X("ZF0"), X("ZZ"), pc(25), A.mult)
+        ts(X("ZB0"), X("ZZ"), pc(26), A.mult)
+        ts(X("Ih"), X("D0"), 0.5, A.mult)
+        ts(X("B7"), X("BLKb"), 0.4375, A.mult)
+        cp(X("BF1"), X("BLKb"))
+        ts(X("BFh"), X("BLKb"), 0.5, A.mult)
+        ts(X("BF15"), X("BLKb"), pc(15), A.mult)
+        ts(X("trS"), X("tr"), pc(0), A.add)
+        cp(X("thF"), X("thI"))
+        cp(X("Hc", 0, 1), X("thF", 0, 1))
+        ts(X("bB"), X("thF", 1, 2), 2.0, A.mult, -1.0, A.add)
+
+    nxt = T.cores[(rank + 1) % len(T.cores)]
+    prv = T.cores[(rank - 1) % len(T.cores)]
+    adr = topo.addr(nxt)
+    eng = topo.engines(core, nxt)
+    half = len(eng) // 2
+    msk = sum(1 << e for e in eng[:half])
+    n_in = len(topo.engines(prv, core)) // 2
+    loc = [0]
+
+    def send(dst, src, sem):
+        deps = {}
+        need("G", src[1], src[2], src[3], False, deps)
+        waits("G", deps)
+        g.remote_dma(dst, src[0], T.sem[sem], T.sem.loc, adr[1], adr[0], msk)
+        loc[0] += half
+
+    def arrive(t):
+        rec["VL%d" % t] = [(0, 16, "R", "al%d" % t, n_in, True)]
+        rec["VB%d" % t] = [(0, 256, "R", "av%d" % t, n_in, True)]
+        rec["z%d" % t] = [(0, 128, "R", "ay%d" % t, n_in, True), (128, 256, "R", "az%d" % t, n_in, True)]
+
+    def expand(copy, dst, src, i0, i1):
+        a, b = 16 * i0, 16 * i1
+        copy(X(dst, a, b, 16), X(src, i0, i1))
+        for k in (8, 4, 2, 1):
+            copy(X(dst, a + k, b, 2 * k), X(dst, a, b, 2 * k))
+
+    def targets(t, c):
+        expand(scp, "zE", "z%d" % t, 64 * c, 64 * c + 64)
+
+    def ind_x(off):
+        return IND(X("xdS", 0, W), off)
+
+    def ind_n(off):
+        return IND(X("nbS", 0, W), off)
+
+    def erow(E, q):
+        return (T[E][:, q, 0:256 - 16 * q], E, 256 * q, 240 * q + 256)
+
+    def count(ps, lhs, E):
+        mms([(X(ps, 16 * q, 256), lhs(q), erow(E, q)) for q in range(16)])
+
+    def to_list(ps, src):
+        mms([(X(ps, 480, 496), X("ZB0", 15 - r, 143 - r), X(src, r, 256, 16)) for r in range(16)])
+
+    def place(ps, src, out):
+        tt(X("o1"), X(ps, 480, 496), X(src), A.add)
+        tt(X("o2"), X("o1"), X("trS"), A.min)
+        ts(X(out), X("o2"), 1536.0, A.add)
+
+    def new_contacts():
+        nw = X("ps0", 0, 256)
+        tt(nw, nw, X("conF"), A.subtract)
+        tt(nw, nw, X("ohb"), A.mult)
+        tt(X("wv"), nw, X("conF"), A.add)
+
+    for t in range(4):
+        VL, VB, z, E, pk = "VL%d" % t, "VB%d" % t, "z%d" % t, "E3%d" % (t % 2), "pk%d" % t
+        last = t == 3
+
+        if t == 0:
+            targets(0, 0)
+        tt(X("dz"), ind_x(X(VL)), X(z), A.subtract)
+        ts(X("nn"), X("dz"), 1.0, A.is_gt)
+        ts(X("nm"), X("dz"), -1.0, A.is_lt)
+        mms([(X("ps6", 0, 256), X("VW"), X("nn")), (X("ps6", 0, 256), X("VW"), X("nm"))])
+        act(X("adz"), X("dz"), F.Abs)
+        mms([(X("ps5", 0, 256), X("D0"), X("adz")), (X("ps5", 0, 256), X("In"), X(z))])
+        if not last:
+            ts(X("xi"), X("dz"), 0.5, A.mult, 191.75, A.add)
+            mms([(X("ps5", 256, 512), X("D0"), X("xi")), (X("ps5", 256, 512), X("D0"), X(z))])
+        if t > 0:
+            new_contacts()
+            place("ps2", "o3", "offR")
+        else:
+            targets(0, 1)
+        targets(t, 2)
+        scp(X("dlt"), X("ps5", 0, 256))
+        if not last:
+            act(X("xn"), X("ps5", 256, 512), F.Copy, bias=-192.0)
+        ts(X("Pb"), X("ps6", 0, 256), pc(20), A.is_lt)
+        mms([(X("ps1", 0, 256), X("M2"), X("Pb"))])
+        mms([(X("ps1", 256, 512), X("M1"), X("Pb"))])
+        mms([(X("ps6", 0, 256), X("KE"), X("Pb"))])
+        mms([(X("ps6", 256, 512), X("KO"), X("Pb"))])
+        scp(X("m2"), X("ps1", 0, 256))
+        ts(X("vS"), X(VL), -1536.0, A.add)
+        if t == 0:
+            more_consts()
+            for j in range(4):
+                a, b = j * C4, (j + 1) * C4
+                ts(X("nbS", a, b), X("nbI", a, b), -1536.0, A.add)
+        else:
+            cp(IND(X("nbS", 0, WT), X("offR")), X("wv"))
+        ts(X("conU"), ind_n(X(VL)), 1536.0, A.add)
+        expand(cp, "maskE", "m2", 0, 64)
+        for c in range(1, 4):
+            expand(scp, "maskE", "m2", 64 * c, 64 * c + 64)
+            if c == 1:
+                act(X("conF"), ind_n(X(VL)), F.Copy)
+
+        def gather_nb(c):
+            s = 1024 * c
+            tt(X("mk", s, s + 1024), ind_n(X("conU", 64 * c, 64 * c + 64)), X("maskE", s, s + 1024), A.mult)
+            for par, zz in ((0, "ZFe"), (1, "ZFo")):
+                col = par * 128 + (c % 2) * 64
+                mms([(X("ps%d" % (3 + c // 2), col, col + 64), X(zz, 15 - k, 143 - k), X("mk", s + k, s + 1024, 16))
+                     for k in range(16)])
+
+        def lists(h):
+            ts(X("cU", 256 * h, 256 * h + 256), X("ps%d" % (3 + h), 0, 256), 1536.0, A.add)
+
+        gather_nb(0)
+        gather_nb(1)
+        tt(X("co"), X("ps1", 256, 512), X("conF"), A.mult)
+        cp(X("ohb"), X("ps1", 256, 512))
+        mms([(X("ps2", 0, 16), X("ZFa", 15 - r, 143 - r), X("co", r, 256, 16)) for r in range(16)])
+        for par in range(2):
+            act((T.Wt[:, :, 128 * par:128 * par + 128], "Wt", 0, 512), X("ps6", 256 * par, 256 * par + 256), F.Exp,
+                bias=pc(28 + par), scale=-16.0 * LN2)
+        gather_nb(2)
+        lists(0)
+        ts(X("TLu"), X("ps2", 0, 16), 1536.0, A.add)
+        gather_nb(3)
+        targets(t, 3)
+
+        def dsum(c, par):
+            s = 1024 * (2 * c + par)
+            col = par * 128 + (c % 2) * 64
+            mms([(X("ps%d" % (5 + c // 2), col, col + 64), X("ZZ", 15 - k, 143 - k), X("dd", s + k, s + 1024, 16)) for k in range(16)])
+
+        def ccols(c, par):
+            col = 256 * (c // 2) + par * 128 + (c % 2) * 64
+            return X("cU", col, col + 64)
+
+        def raw(c):
+            act(X("xg", 1024 * c, 1024 * c + 1024), ind_x(ccols(c, 1)), F.Copy)
+
+        def raw_sub(c):
+            for b in range(2):
+                a0 = 1024 * c + 512 * b
+                mms([(X("ps%d" % b), X("D0"), X("xg", a0, a0 + 512)), (X("ps%d" % b), X("In"), X("zE", a0, a0 + 512))])
+
+        def raw_abs(c):
+            s = 1024 * (2 * c + 1)
+            for b in range(2):
+                act(X("dd", s + 512 * b, s + 512 * b + 512), X("ps%d" % b), F.Abs)
+            dsum(c, 1)
+
+        def cand(c, par):
+            s = 1024 * (2 * c + par)
+            tt(X("dd", s, s + 1024), ind_x(ccols(c, par)), X("zE", 1024 * c, 1024 * c + 1024), A.subtract)
+            act(X("dd", s, s + 1024), X("dd", s, s + 1024), F.Abs)
+            dsum(c, par)
+
+        def pairs():
+            if t == 0:
+                cp(X(VB), IND(X("idW"), X(VL)))
+            for q in range(16):
+                ts(erow(E, q), X(VB, 16 * q, 256), X("vS", q, q + 1), A.is_equal)
+            diag = (T[E][:, :, 0:16], E, 0, 4096)
+            tt(diag, diag, (T.TRI[:, :, :], "TRI", 0, 256), A.mult)
+
+        def relu(h):
+            act(X("ps%d" % (5 + h), 0, 256), X("ps%d" % (5 + h), 0, 256), F.Relu, bias=X("bB"), scale=-2.0)
+
+        raw(0)
+        raw_sub(0)
+        raw(1)
+        cand(0, 0)
+        raw_abs(0)
+        raw_sub(1)
+        lists(1)
+        pairs()
+        if not last:
+            count("ps2", lambda q: X("BLKb"), E)
+        raw(2)
+        tt(X("d0"), ind_x(X("TLu")), X(z), A.subtract)
+        act(X("d0"), X("d0"), F.Abs)
+        mms([(X("ps7", 256, 512), X("BLKb"), X("d0"))])
+        raw_abs(1)
+        raw_sub(2)
+        cand(1, 0)
+        if not last:
+            scp(X("cb"), X("ps2", 0, 256))
+            to_list("ps2", "cb")
+        cand(2, 0)
+        raw_abs(2)
+        hb = X("ps7", 256, 512)
+        ts(hb, hb, X("Hc", t, t + 1), A.is_lt, 2.0, A.mult)
+        tt(X("hc"), hb, X("co"), A.mult)
+        relu(0)
+        act(X("hb2"), hb, F.Copy, acc=X("hs", t, t + 1))
+        cand(3, 0)
+
+        def tail_a(h):
+            tt(X("hw", 256 * h, 256 * h + 256), X("ps%d" % (5 + h), 0, 256), (T.Wt[:, h, :], "Wt", 256 * h, 256 * h + 256), A.min)
+            s = X("ps7", 128 * h, 128 * h + 128)
+            mms([(s, X("B7"), X("hw", 256 * h, 256 * h + 128)), (s, X("B7"), X("hw", 256 * h + 128, 256 * h + 256)),
+                 (s, X("Ih"), X("hb2", 128 * h, 128 * h + 128))])
+
+        def tail_b(h):
+            a, b = 128 * h, 128 * h + 128
+            s = X("ps7", a, b)
+            for par in range(2):
+                u = 256 * h + 128 * par
+                tt(X("fi", u, u + 128), X("hw", u, u + 128), s, A.is_gt)
+            tt(X("fc", 256 * h, 256 * h + 256), X("ps%d" % (3 + h), 0, 256), X("fi", 256 * h, 256 * h + 256), A.mult)
+            lo = X("ps1", 256 + a, 256 + b)
+            ts(lo, s, 0.0, A.is_equal)
+            tt(X("lc", a, b), lo, X("conF", a, b), A.mult)
+            o = X("ps0", a, b)
+            mms([(o, X("BFh"), X("hc", a, b)), (o, X("BF1"), X("fc", 256 * h, 256 * h + 128)),
+                 (o, X("BF1"), X("fc", 256 * h + 128, 256 * h + 256)), (o, X("BF15"), X("lc", a, b))])
+            tt(lo, lo, X("dlt", a, b), A.mult)
+            zn = X("zn%d" % t, a, b)
+            tt(zn, lo, X(z, a, b), A.add)
+            if not last:
+                send(T["z%d" % (t + 1)][:, a:b], zn, ("ay%d" if h == 0 else "az%d") % (t + 1))
+            else:
+                dma("Y", T.yz[:, a:b], [], zn[0], [zn], "yz%d" % h)
+            tt(X(pk, 256 + a, 256 + b), s, X("hb2", a, b), A.is_gt)
+
+        def weigh(qs, on_scalar):
+            for q in qs:
+                if on_scalar:
+                    act(X("LQ", 128 * q, 128 * q + 128), X("BLKb"), F.Copy, scale=X("rp", q, q + 1))
+                else:
+                    ts(X("LQ", 128 * q, 128 * q + 128), X("BLKb"), X("rp", q, q + 1), A.mult)
+
+        tail_a(0)
+        cand(3, 1)
+        relu(1)
+        if last:
+            act(X("yn", 0, W), X("nbS", 0, W), F.Copy, bias=1536.0)
+        tail_b(0)
+        if not last:
+            place("ps2", "vS", "offA")
+            scp(X("hsb", t, t + 1), X("hs", t, t + 1))
+            mms([(X("ps4", 256, 257), X("AW"), X("hsb", t, t + 1))])
+        tail_a(1)
+        cp(X(pk, 0, 128), X("ps0", 0, 128))
+        tail_b(1)
+        cp(X(pk, 128, 256), X("ps0", 128, 256))
+        mms([(X("ps5", 256, 288), X("ZF0", 15 - r, 143 - r), X(pk, r, 512, 16)) for r in range(16)])
+        if not last:
+            ts(X("hi0", t, t + 1), X("ps4", 256, 257), -1.0, A.mult, 2048.0, A.add)
+            ts(X("hi1", t, t + 1), X("hi0", t, t + 1), 15, A.bitwise_and)
+            tt(X("Hc", t + 1, t + 2), X("hi1", t, t + 1), X("thF", 0, 1), A.add)
+        ts(X("VN%d" % t if not last else "yvS"), X("ps5", 256, 272), 1536.0, A.add)
+        if not last:
+            send(T["VL%d" % (t + 1)][:, :], X("VN%d" % t), "al%d" % (t + 1))
+            send(T["VB%d" % (t + 1)][:, :], X(pk, 0, 256), "av%d" % (t + 1))
+            arrive(t + 1)
+            targets(t + 1, 0)
+        else:
+            dma("Y", T.yv[:, :], [], T.yvS[:, :], [X("yvS")], "yv")
+        scp(X("rp"), X("ps5", 272, 288))
+        weigh(range(0, 10), False)
+        weigh(range(10, 16), True)
+        count("ps2", lambda q: X("LQ", 128 * q, 128 * q + 128), E)
+        if not last:
+            cp(IND(X("xdS", 0, WT), X("offA")), X("xn"))
+            targets(t + 1, 1)
+        ts(X("q1"), X("rp"), -4096.0, A.mult, 4096.0, A.add)
+        tt(X("o3"), X("q1"), X("vS"), A.add)
+        scp(X("crb"), X("ps2", 0, 256))
+        to_list("ps2", "crb")
+    new_contacts()
+    place("ps2", "o3", "offR")
+    ot = IND(X("yn", 0, WT), X("offR"))
+    op("V", lambda e: e.tensor_scalar(ot[0], T.wv[:, :], 1.0, 1536.0, A.mult, A.add), [X("wv"), ot[2]], [ot[1]])
+
+    for j in range(4):
+        a, b = j * C4, (j + 1) * C4
+        dma("Y" if j % 2 == 0 else "S", T.ynb[:, a:b], [], T.yn[:, a:b], [X("yn", a, b)], "y%d" % j)
+    fin = {s: cnt[s] for s in cnt}
+    for d in DMAS:
+        fin["d_" + d] = 16
+    fin["loc"] = loc[0]
+    for s in fin:
+        if known["G"].get(s, 0) < fin[s]:
+            g.wait_ge(T.sem[s], fin[s])

@@ -1,39 +1,56 @@
-import math
+from concourse.bass import DstId, RemoteDMATransfer
 from concourse.mybir import dt, AluOpType, AxisListType, ActivationFunctionType
 
 W = 3072
-LN2 = math.log(2.0)
 WT = W + 256
+OFF = 1536.0
+U = 4096.0
+SEG = 34
+NK = 8 * SEG
+ON_SCALAR = (6, 2)
+CYCLE, GATHER, SCATTER, HOP, DMA_LAG, DMA_RATE, WAY = 0.83, 1.3, 3.1, 280.0, 2500.0, 190.0, 4500.0
+PASSES, FIRST, BANK = 4, 0.0, 100.0
 
 SCRATCH = {
     "nbI": ("sbuf", [128, W], "int32"), "nbS": ("sbuf", [128, WT], "float32"), "xdS": ("sbuf", [128, WT], "bfloat16"),
     "idW": ("sbuf", [128, W], "float32"), "yn": ("sbuf", [128, WT], "float32"),
-    "E30": ("sbuf", [128, 16, 256], "bfloat16"), "E31": ("sbuf", [128, 16, 256], "bfloat16"),
-    "Wt": ("sbuf", [128, 2, 256], "bfloat16"), "TRI": ("sbuf", [128, 16, 16], "bfloat16"),
+    "E": ("sbuf", [128, 16, 256], "bfloat16"), "TRI": ("sbuf", [128, 16, 16], "bfloat16"),
+    "px": ("psum", [128, 16, 32], "float32"),
 }
+PART = {}
 
 
 def _decl():
-    for names, cols, d in (("maskE zE xg", 4096, "bfloat16"), ("mk", 4096, "float16"), ("dd", 8192, "bfloat16"), ("LQ", 2048, "bfloat16"),
-                           ("dz adz nn nm Pb m2 ohb dlt d0 hb2 cb crb xi xn", 256, "bfloat16"), ("hw fi", 512, "bfloat16"),
-                           ("VB0 VB1 VB2 VB3 co hc lc", 256, "float16"), ("fc pk0 pk1 pk2 pk3", 512, "float16"), ("conF wv rr", 256, "float32"),
-                           ("conU", 256, "uint16"), ("cU", 512, "uint16"), ("TLu offA offR", 16, "uint16"),
-                           ("vS rp q1 o1 o2 o3 yvS tr trS", 16, "float32"), ("pvI", 16, "int32"),
-                           ("thI", 2, "int32"), ("thF", 2, "float32"), ("bB", 1, "float32"), ("Hc hs", 4, "float32"),
-                           ("hsb", 4, "bfloat16"), ("hi0 hi1", 4, "int32"), ("pI pB", 8, "int32"), ("pC", 32, "float32"),
-                           ("ones ZZ ta tb ZB0", 144, "bfloat16"), ("ZFe ZFo ZFa ZF0", 144, "float16"),
-                           ("BLKb D0 D1 D2 CA CB D0n mt M1 M2 M2a In Ih B7 AW VW ALT KE KO", 128, "bfloat16"),
-                           ("BF1 BFh BF15", 128, "float16"),
-                           ("VL0 VL1 VL2 VL3 VN0 VN1 VN2 VN3", 16, "uint16"), ("z0 z1 z2 z3 zn0 zn1 zn2 zn3", 256, "bfloat16")):
+    for names, cols, d in (("mk", 4096, "float16"), ("dd xg", 8192, "bfloat16"),
+                           ("zz0 zz1 zz2 zz3 z40 z41 m40 m41", 512, "bfloat16"),
+                           ("dz far Pb xi xn d0 cb crb zn0 zn1 zn2 zn3 ta tb tc", 256, "bfloat16"),
+                           ("VB0 VB1 VB2 VB3 VO0 VO1 VO2 VO3 con co", 256, "float16"),
+                           ("TT A1 no Vm rr", 256, "float32"), ("Tt", 256, "uint16"), ("cU", 512, "uint16"),
+                           ("WP TH RST R0 R1 ones", NK, "bfloat16"), ("sc0 sc1", NK, "float32"), ("w34 k34 t34 u34", SEG, "float32"),
+                           ("VL0 VL1 VL2 VL3 VN0 VN1 VN2 VN3 TLu offA offR zo", 16, "uint16"), ("Lg LP LL", 8, "uint16"),
+                           ("vS o2 o3 yvS ii trS zf zg", 16, "float32"), ("pvI vi vc pr", 16, "int32"), ("sg", 16, "bfloat16"),
+                           ("thI", 2, "int32"), ("thF", 2, "float32"), ("Hc", 4, "float32"), ("hs", 8, "float32"),
+                           ("hi0 hi1", 4, "int32"), ("pI pB iI", 8, "int32"), ("pC", 32, "float32"), ("iF", 8, "float32"),
+                           ("ZZ ZB", 144, "bfloat16"), ("ZFe ZFo ZFa", 144, "float16"),
+                           ("BLK D0 D1 D2 CA CB D0n mt M1 M2 M2a In LT NEG Sp Sm LQ crc", 128, "bfloat16"),
+                           ("I16 N16 W00 W01 W10 W11", 128, "float16"), ("I32 MD on32", 128, "float32"), ("CMP", 64, "float32"),
+                           ("b8 b80", 8, "bfloat16"), ("b8h r15", 8, "float16"), ("b8f", 8, "float32"), ("SelP", 16, "float16")):
         for n in names.split():
-            SCRATCH[n] = ("sbuf", [128, cols], d)
-    for b in range(8):
-        SCRATCH["ps%d" % b] = ("psum", [128, 512], "float32")
+            if cols > 32:
+                SCRATCH[n] = ("sbuf", [128, cols], d)
+            else:
+                home = "few_" + d
+                at = SCRATCH[home][1][1] if home in SCRATCH else 0
+                PART[n] = (home, at, cols)
+                SCRATCH[home] = ("sbuf", [128, at + (cols + 15) // 16 * 16], d)
+    for b in "pK pD0 pD1 pS0 pS1 pM pN".split():
+        SCRATCH[b] = ("psum", [128, 512], "float32")
 
 
 _decl()
-DMAS = ["pv", "pz", "th", "xa", "xb", "n0", "n1", "n2", "n3", "y0", "y1", "y2", "y3", "yv", "yz0", "yz1"]
-SEMAPHORES = ["sV", "sS", "sP", "sG", "loc"] + ["d_" + d for d in DMAS] + ["a%s%d" % (n, t) for n in ("l", "y", "z", "v") for t in range(4)]
+DMAS = ["pv", "pz", "th", "xa", "xb", "n0", "n1", "n2", "n3", "n4", "y0", "y1", "y2", "y3", "yv", "yz0", "yz1"]
+SEMAPHORES = (["sV", "sS", "sP", "sG", "loc"] + ["d_" + d for d in DMAS] + ["d_z%d%d" % (t, h) for t in range(4) for h in range(2)]
+              + ["a%s%d%d" % (n, t, h) for n in "lzv" for t in range(1, 4) for h in range(2)])
 
 
 def rank_program(g, core, T, topo):
@@ -48,8 +65,10 @@ def rank_program(g, core, T, topo):
     rec = {}
 
     def need(q, name, lo, hi, wr, out):
-        ps = name[:2] == "ps"
+        ps = name in SCRATCH and SCRATCH[name][0] == "psum"
         for (a, b, q2, s, c, w2) in rec.get(name, ()):
+            if ps and q == q2 == "P":
+                continue
             if (ps and q2 != q) or (a < hi and lo < b and (wr or w2)):
                 if out.get(s, 0) < c:
                     out[s] = c
@@ -76,31 +95,127 @@ def rank_program(g, core, T, topo):
                     k[s2] = c2
             k[s] = max(k.get(s, 0), c)
 
-    def op(q, emit, reads, writes, sem=None, inc=1):
-        deps = {}
-        for x in reads:
-            need(q, x[1], x[2], x[3], False, deps)
-        for x in writes:
-            need(q, x[1], x[2], x[3], True, deps)
-        waits(q, deps)
-        r = emit(ENG[q])
-        if sem is None:
+    calls = []
+    seen = {}
+    lift = [0.0]
+
+    def call(q, run, reads, writes, ns, lag=0.0, adds=False, nbytes=0):
+        me = len(calls) + (1 if nbytes else 0)
+        deps = set()
+        for xs, wr in ((reads, False), (writes, True)):
+            for x in xs:
+                for (a, b, c, w2, ad) in seen.get(x[1], ()):
+                    if a < x[3] and x[2] < b and (wr or w2) and not (wr and adds and ad):
+                        deps.add(c)
+        for xs, wr in ((reads, False), (writes, True)):
+            for x in xs:
+                old = seen.get(x[1], [])
+                if wr and not adds:
+                    old = [y for y in old if not (x[2] <= y[0] and y[1] <= x[3])]
+                seen[x[1]] = old + [(x[2], x[3], me, wr, wr and adds)]
+        deps.discard(me)
+        uses = [q] + sorted({x[1] for x in reads + writes if in_psum(x)})
+        calls.append({"uses": uses, "run": run, "deps": deps, "ns": ns, "lag": lag})
+        if nbytes:
+            calls.append({"uses": ["engines"], "run": lambda: None, "deps": {me - 1}, "ns": nbytes / DMA_RATE, "lag": 0.0})
+
+    def place_calls(rank_of, before, after, delay):
+        n = len(calls)
+        left = [len(b) for b in before]
+        at = [0.0] * n
+        busy = {}
+        ready = [j for j in range(n) if left[j] == 0]
+        while ready:
+            j = min(ready, key=rank_of)
+            ready.remove(j)
+            c = calls[j]
+            s, moved = at[j], True
+            while moved:
+                moved = False
+                for u in c["uses"]:
+                    taken = busy.setdefault(u, [])
+                    lo, hi = 0, len(taken)
+                    while lo < hi:
+                        mid = (lo + hi) // 2
+                        if taken[mid][1] <= s:
+                            lo = mid + 1
+                        else:
+                            hi = mid
+                    if lo < len(taken) and taken[lo][0] < s + c["ns"]:
+                        s, moved = taken[lo][1], True
+            at[j] = s
+            for u in c["uses"]:
+                taken = busy[u]
+                k = len(taken)
+                while k and taken[k - 1][0] > s:
+                    k -= 1
+                taken.insert(k, (s, s + c["ns"] + (BANK if u in SCRATCH else 0.0)))
+            for u in after[j]:
+                at[u] = max(at[u], s + c["ns"] + delay(j, u))
+                left[u] -= 1
+                if left[u] == 0:
+                    ready.append(u)
+        return at
+
+    def plan():
+        n = len(calls)
+        deps = [sorted(c["deps"]) for c in calls]
+        users = [[] for c in calls]
+        for j in range(n):
+            for d in deps[j]:
+                users[d].append(j)
+        key = list(range(n))
+        best = None
+        for turn_ in range(PASSES):
+            fw = place_calls(lambda j: key[j], deps, users, lambda a, b: calls[a]["lag"] + HOP)
+            end = max(fw[j] + calls[j]["ns"] for j in range(n))
+            if best is None or end < best[0]:
+                best = (end, fw)
+            bw = place_calls(lambda j: -(fw[j] + calls[j]["ns"]), users, deps, lambda a, b: calls[b]["lag"] + HOP)
+            key = [-(bw[j] + calls[j]["ns"]) for j in range(n)]
+        return sorted(range(n), key=lambda j: (best[1][j], j))
+
+    def kind(x):
+        return SCRATCH[PART[x[1]][0] if x[1] in PART else x[1]]
+
+    def in_psum(x):
+        return kind(x)[0] == "psum"
+
+    def ns(out, a, two=False):
+        if len(out) == 3:
+            return 50.0 + 16 * out[2][4] * SCATTER
+        if len(a) == 3:
+            return 50.0 + out[4] * GATHER
+        narrow = all(kind(x)[2] in ("bfloat16", "float16", "uint16") for x in (out, a))
+        return max(55.0, 35.0 + out[4] * CYCLE * (2.0 if two else 0.5 if narrow else 1.0))
+
+    def op(q, emit, reads, writes, t):
+        def run():
+            deps = {}
+            for x in reads:
+                need(q, x[1], x[2], x[3], False, deps)
+            for x in writes:
+                need(q, x[1], x[2], x[3], True, deps)
+            waits(q, deps)
             s = "s" + q
             cnt[s] += 1
             c = cnt[s]
-        else:
-            s, c = sem, inc
-        r.then_inc(T.sem[s], inc)
-        snap[(s, c)] = dict(known[q])
-        for x in reads:
-            note(q, x[1], x[2], x[3], s, c, False)
-        for x in writes:
-            note(q, x[1], x[2], x[3], s, c, True)
+            emit(ENG[q]).then_inc(T.sem[s], 1)
+            snap[(s, c)] = dict(known[q])
+            for x in reads:
+                note(q, x[1], x[2], x[3], s, c, False)
+            for x in writes:
+                note(q, x[1], x[2], x[3], s, c, True)
+        call(q, run, reads, writes, t)
 
-    def X(n, a=0, b=None, st=1):
+    def X(n, a=0, b=None, st=1, p=128):
+        home, at, cols = PART[n] if n in PART else (n, 0, SCRATCH[n][1][1])
         if b is None:
-            b = SCRATCH[n][1][1]
-        return (T[n][:, a:b:st] if st > 1 else T[n][:, a:b], n, a, b)
+            b = cols
+        return (T[home][0:p, at + a:at + b:st] if st > 1 else T[home][0:p, at + a:at + b], n, a, b, len(range(a, b, st)))
+
+    def PX(a, b, c0=0, c1=32):
+        return (T.px[:, a:b, c0:c1], "px", 32 * a, 32 * b, (b - a) * (c1 - c0))
 
     def IND(win, off):
         return (win[0].indirect(off[0]), win, off)
@@ -108,8 +223,12 @@ def rank_program(g, core, T, topo):
     def rd(x):
         return [x[1], x[2]] if len(x) == 3 else [x]
 
+    def wr(out):
+        return ([out[2]], [out[1]]) if len(out) == 3 else ([], [out])
+
     def tt(out, a, b, o):
-        op("V", lambda e: e.tensor_tensor(out[0], a[0], b[0], o), rd(a) + rd(b), [out])
+        two = len(a) > 3 and not in_psum(a) and not in_psum(b)
+        op("V", lambda e: e.tensor_tensor(out[0], a[0], b[0], o), rd(a) + rd(b) + wr(out)[0], wr(out)[1], ns(out, a, two))
 
     def ts(out, a, s1, o0, s2=None, o1=None):
         reads = rd(a)
@@ -119,15 +238,15 @@ def rank_program(g, core, T, topo):
         if isinstance(s2, tuple):
             reads = reads + [s2]; v2 = s2[0]
         if o1 is None:
-            op("V", lambda e: e.tensor_scalar(out[0], a[0], v1, None, o0), reads, [out])
+            op("V", lambda e: e.tensor_scalar(out[0], a[0], v1, None, o0), reads, [out], ns(out, a))
         else:
-            op("V", lambda e: e.tensor_scalar(out[0], a[0], v1, v2, o0, o1), reads, [out])
+            op("V", lambda e: e.tensor_scalar(out[0], a[0], v1, v2, o0, o1), reads, [out], ns(out, a))
 
     def cp(out, a):
-        if len(out) == 3:
-            op("V", lambda e: e.tensor_copy(out[0], a[0]), rd(a) + [out[2]], [out[1]])
-        else:
-            op("V", lambda e: e.tensor_copy(out[0], a[0]), rd(a), [out])
+        op("V", lambda e: e.tensor_copy(out[0], a[0]), rd(a) + wr(out)[0], wr(out)[1], ns(out, a))
+
+    def fill(x, v):
+        op("V", lambda e: e.memset(x[0], v), [], [x], ns(x, x))
 
     def act(out, a, f, bias=None, scale=None, acc=None):
         kw = {}
@@ -140,148 +259,226 @@ def rank_program(g, core, T, topo):
                     kw[nm] = v
         if acc is not None:
             writes = writes + [acc]; kw["accum_out"] = acc[0]
-        op("S", lambda e: e.activation(out[0], a[0], f, **kw), reads, writes)
+        t = 65.0 + out[4] * GATHER if len(a) == 3 else max(60.0, 40.0 + out[4] * CYCLE)
+        op("S", lambda e: e.activation(out[0], a[0], f, **kw), reads, writes, t)
 
     def scp(out, a):
         act(out, a, F.Copy)
 
-    def mms(items):
-        deps = {}
-        for (o, l, r) in items:
-            need("P", o[1], o[2], o[3], True, deps)
-            need("P", l[1], l[2], l[3], False, deps)
-            need("P", r[1], r[2], r[3], False, deps)
-        waits("P", deps)
-        n = len(items)
-        for j, (o, l, r) in enumerate(items):
-            g.tensor.matmul(o[0], l[0], r[0], j == 0, j == n - 1).then_inc(T.sem.sP, 1)
-        cnt["sP"] += n
-        c = cnt["sP"]
-        snap[("sP", c)] = dict(known["P"])
-        for (o, l, r) in items:
-            note("P", l[1], l[2], l[3], "sP", c, False)
-            note("P", r[1], r[2], r[3], "sP", c, False)
-        for (o, l, r) in items:
-            note("P", o[1], o[2], o[3], "sP", c, True)
+    parts = {}
 
-    def dma(q, out, oacc, in_, iacc, name):
-        op(q, lambda e: e.dma_start(out, in_), iacc, oacc, sem="d_" + name, inc=16)
+    def mms(items, start=True, stop=True, part=None):
+        if part is not None:
+            parts[part] = parts.get(part, 0) + 1
+
+        def run():
+            deps = {}
+            for (o, l, r) in items:
+                need("P", o[1], o[2], o[3], True, deps)
+                need("P", l[1], l[2], l[3], False, deps)
+                need("P", r[1], r[2], r[3], False, deps)
+            waits("P", deps)
+            n = len(items)
+            end = stop
+            if part is not None:
+                parts[part] -= 1
+                end = stop and parts[part] == 0
+            for j, (o, l, r) in enumerate(items):
+                g.tensor.matmul(o[0], l[0], r[0], start and j == 0, end and j == n - 1).then_inc(T.sem.sP, 1)
+            cnt["sP"] += n
+            c = cnt["sP"]
+            snap[("sP", c)] = dict(known["P"])
+            for (o, l, r) in items:
+                note("P", l[1], l[2], l[3], "sP", c, False)
+                note("P", r[1], r[2], r[3], "sP", c, False)
+            for (o, l, r) in items:
+                note("P", o[1], o[2], o[3], "sP", c, True)
+        t = sum(max(min(64, l[4]), r[4]) * (4 if kind(l)[2] == "float32" else 1) for (o, l, r) in items) * CYCLE / 2
+        call("P", run, [x for it in items for x in it[1:]], [it[0] for it in items], t, adds=part is not None)
+
+    dsem = {}
+
+    def dmas(q, name, items, nbytes):
+        s = "d_" + name
+        outs = [o for o, x in items if isinstance(o, tuple)]
+        ins = [x for o, x in items if isinstance(x, tuple)]
+
+        def run():
+            deps = {}
+            for o in outs:
+                need(q, o[1], o[2], o[3], True, deps)
+            for x in ins:
+                need(q, x[1], x[2], x[3], False, deps)
+            waits(q, deps)
+            for o, x in items:
+                ENG[q].dma_start(o[0] if isinstance(o, tuple) else o, x[0] if isinstance(x, tuple) else x).then_inc(T.sem[s], 16)
+            c = dsem[s] = 16 * len(items)
+            snap[(s, c)] = dict(known[q])
+            for x in ins:
+                note(q, x[1], x[2], x[3], s, c, False)
+            for o in outs:
+                note(q, o[1], o[2], o[3], s, c, True)
+        call(q, run, ins, outs, 60.0 * len(items), lag=DMA_LAG, nbytes=nbytes)
 
     def iota(x, pat, base, cm):
-        kw = {} if SCRATCH[x[1]][2] == "int32" else {"allow_small_or_imprecise_dtypes": True}
-        op("G", lambda e: e.iota(x[0], pat, base, cm, **kw), [], [x])
+        kw = {} if x[1][-1] == "I" else {"allow_small_or_imprecise_dtypes": True}
+        op("G", lambda e: e.iota(x[0], pat, base, cm, **kw), [], [x], 130.0 + 2 * CYCLE * x[4])
 
     def sel(out, a, pat, o, base, cm):
-        op("G", lambda e: e.affine_select(out[0], a[0], pat, o, 0.0, base, cm), [a], [out])
+        op("G", lambda e: e.affine_select(out[0], a[0], pat, o, 0.0, base, cm), [a], [out], 170.0 + 2 * CYCLE * out[4])
 
-    C4, H2 = W // 4, W // 2
-    dma("Y", T.pvI[:, :], [X("pvI")], T.pv[:, :], [], "pv")
-    dma("Y", T.thI[:, :], [X("thI")], T.th[:, :], [], "th")
-    dma("S", T.z0[:, :], [X("z0")], T.pz[:, :], [], "pz")
-    dma("Y", T.xdS[:, 0:H2], [X("xdS", 0, H2)], T.xd[:, 0:H2], [], "xa")
-    dma("S", T.xdS[:, H2:W], [X("xdS", H2, W)], T.xd[:, H2:W], [], "xb")
-    for j in range(4):
-        a, b = j * C4, (j + 1) * C4
-        dma("Y" if j % 2 == 0 else "S", T.nbI[:, a:b], [X("nbI", a, b)], T.nb[:, a:b], [], "n%d" % j)
+    H2 = W // 2
+    PIECES = (0, 768, 1536, 2304, 2816, W)
+    lift[0] = 1.0e6
+    dmas("Y", "pv", [(X("pvI"), T.pv[:, :])], 8192)
+    dmas("S", "pz", [(X("zz0", 0, 256), T.pz[:, :])], 65536)
+    dmas("Y", "xa", [(X("xdS", 0, H2), T.xd[:, 0:H2])], 256 * H2)
+    dmas("S", "xb", [(X("xdS", H2, W), T.xd[:, H2:W])], 256 * H2)
+    dmas("Y", "th", [(X("thI"), T.th[:, :])], 1024)
+    lift[0] = 0.5e6
+    for j in range(5):
+        a, b = PIECES[j], PIECES[j + 1]
+        dmas("Y" if j % 2 == 0 else "S", "n%d" % j, [(X("nbI", a, b), T.nb[:, a:b])], 512 * (b - a))
+    lift[0] = 0.0
+
+    def replicate(t, h):
+        src = X("zz%d" % t, 128 * h, 128 * h + 128)
+        dmas("Y", "z%d%d" % (t, h), [(X("z4%d" % h, 128 * c, 128 * c + 128), src) for c in range(4)], 4 * 32768)
 
     pc = lambda j: X("pC", j, j + 1)
+    one = X("ones", 0, 128)
     iota(X("pI", 0, 1), [[1, 1]], 0, 1)
-    op("V", lambda e: e.memset(T.ones[:, :], 1.0), [], [X("ones")])
-    op("V", lambda e: e.memset(T.AW[:, :], 1.0 / 32), [], [X("AW")])
+    fill(X("ones"), 1.0)
+    fill(X("on32"), 1.0)
+    fill(X("RST"), 1.0)
+    fill(X("tc", 0, 144), U)
+    fill(X("RST", 0, NK, SEG), 0.0)
+    fill(pc(19), -1.0)
+    fill(pc(20), 1.0)
+    fill(pc(21), -60.0 * U)
+    sel(X("ta", 0, 128), one, [[-16, 8], [0, 16]], A.is_ge, 0, 1)
+    sel(X("BLK"), X("ta", 0, 128), [[16, 8], [0, 16]], A.is_ge, 15, -1)
+    sel(X("ta", 128, 256), X("BLK"), [[1, 128]], A.is_ge, 0, -1)
+    sel(X("LT"), X("ta", 128, 256), [[0, 8], [-1, 16]], A.is_ge, 14, 0)
+    for n, b in (("D0", 0), ("D2", 2), ("CA", -15), ("CB", -14), ("D1", 1)):
+        sel(X(n), X("BLK"), [[-1, 128]], A.is_equal, b, 1)
+    sel(X("Sp"), one, [[-1, 128]], A.is_equal, 16, 1)
+    sel(X("Sm"), one, [[-1, 128]], A.is_equal, -16, 1)
+    sel(X("ZB", p=8), X("tc", 0, 144, p=8), [[1, 144]], A.is_equal, -15, -16)
+    sel(X("ta", 0, 144), X("ones", 0, 144), [[-16, 9], [0, 16]], A.is_ge, 0, 1)
+    sel(X("tb", 0, 144), X("ta", 0, 144), [[16, 9], [0, 16]], A.is_ge, 15, -1)
+    sel(X("ZZ"), X("tb", 0, 144), [[0, 9], [1, 16]], A.is_equal, -15, 0)
+    iota(X("rr"), [[0, 16], [1, 16]], 0, 0)
+    iota(X("iI"), [[SEG, 8]], SEG - 1, 0)
+    iota(X("iF"), [[2, 8]], 0, 0)
+    iota(X("ii"), [[16, 16]], 0, 0)
+    iota(X("w34"), [[-16, 2], [-1, 17]], 47, 0)
+    iota(X("k34"), [[0, 2], [1, 17]], 0, 0)
+    for j in range(4):
+        iota(X("idW", 768 * j, 768 * j + 768), [[1, 768]], 768 * j - int(OFF), 0)
+
     ts(X("pI", 1, 2), X("pI", 0, 1), 15, A.bitwise_and)
     cp(pc(0), X("pI", 1, 2))
-    for b in range(4):
-        ts(X("pB", b, b + 1), X("pI", 1, 2), b, A.arith_shift_right, 1, A.bitwise_and)
-    cp(X("pC", 1, 5), X("pB", 0, 4))
-    for b in range(4):
-        ts(pc(5 + b), pc(1 + b), 2.0 ** -(1 << b) - 1.0, A.mult, 1.0, A.add)
-    tt(pc(9), pc(5), pc(6), A.mult)
-    tt(pc(10), pc(7), pc(8), A.mult)
-    tt(pc(11), pc(9), pc(10), A.mult)
-    ts(pc(13), pc(0), 14.0, A.is_lt)
-    ts(pc(14), pc(0), 14.0, A.is_equal)
-    ts(pc(15), pc(0), 15.0, A.is_equal)
-    ts(pc(16), pc(11), 32768.0, A.mult)
-    tt(pc(17), pc(16), pc(13), A.mult)
-    tt(pc(18), pc(17), pc(14), A.subtract)
-    ts(pc(19), pc(15), 1.0e9, A.mult)
-    tt(pc(20), pc(18), pc(19), A.add)
-    ts(pc(21), pc(1), -2.0, A.mult, 1.0, A.add)
-    tt(pc(22), pc(21), pc(13), A.mult)
-    ts(pc(23), pc(15), -1.0, A.mult, 1.0, A.add)
-    ts(pc(28), pc(0), -LN2, A.mult)
-    ts(pc(29), pc(0), -LN2, A.mult, -16.0 * LN2, A.add)
-    ts(pc(24), pc(1), -1.0, A.mult, 1.0, A.add)
-    ts(pc(25), pc(0), 0.0, A.is_equal)
-    ts(pc(26), pc(25), 4096.0, A.mult)
-    sel(X("ta", 0, 128), X("ones", 0, 128), [[-16, 8], [0, 16]], A.is_ge, 0, 1)
-    sel(X("BLKb"), X("ta", 0, 128), [[16, 8], [0, 16]], A.is_ge, 15, -1)
-    for n, j in (("VW", 17), ("ALT", 22)):
-        ts(X(n), X("BLKb"), pc(j), A.mult)
-    for n, b in (("D0", 0), ("D2", 2), ("CA", -15), ("CB", -14), ("D1", 1)):
-        sel(X(n), X("BLKb"), [[-1, 128]], A.is_equal, b, 1)
+    for j, (sh, m) in enumerate(((0, 1), (0, 3), (2, 1), (3, 1), (4, 1))):
+        ts(X("pB", j, j + 1), X("pI", 0, 1), sh, A.arith_shift_right, m, A.bitwise_and)
+    cp(X("pC", 1, 6), X("pB", 0, 5))
+    ts(pc(6), pc(0), 14.0, A.not_equal, 2.0, A.mult)
+    ts(pc(7), pc(6), -1.0, A.add)
+    ts(pc(8), pc(0), 15.0, A.is_equal)
+    ts(pc(9), pc(0), 15.0, A.is_lt)
+    ts(pc(10), pc(1), -1.0, A.mult, 1.0, A.add)
+    ts(pc(11), pc(5), -1.0, A.mult, 1.0, A.add)
+    cp(X("VL0"), X("pvI"))
     ts(X("In"), X("D0"), -1.0, A.mult)
-    ts(X("D0n"), X("D0"), pc(23), A.mult)
-    tt(X("KE"), X("D0n"), X("ALT"), A.add)
-    tt(X("KO"), X("D0n"), X("ALT"), A.subtract)
+    ts(X("D0n"), X("D0"), pc(9), A.mult)
     tt(X("mt"), X("CA"), X("D0n"), A.subtract)
     tt(X("M2a"), X("D2"), X("CB"), A.add)
     tt(X("M2"), X("M2a"), X("mt"), A.add)
     tt(X("M1"), X("D1"), X("mt"), A.add)
-    sel(X("ta"), X("ones"), [[-16, 9], [0, 16]], A.is_ge, 0, 1)
-    sel(X("tb"), X("ta"), [[16, 9], [0, 16]], A.is_ge, 15, -1)
-    sel(X("ZZ"), X("tb"), [[0, 9], [1, 16]], A.is_equal, -15, 0)
-    iota(X("rr"), [[0, 16], [1, 16]], 0, 0)
-    iota(X("tr"), [[16, 16]], W - 1536, 0)
-    iota(X("idW"), [[1, W]], -1536, 0)
-    cp(X("VL0"), X("pvI"))
-
-    def more_consts():
-        ts(X("ZFe"), X("ZZ"), pc(24), A.mult)
-        ts(X("ZFo"), X("ZZ"), pc(1), A.mult)
-        cp(X("ZFa"), X("ZZ"))
-        ts((T.TRI[:, :, :], "TRI", 0, 256), X("rr"), pc(0), A.is_gt)
-        ts(X("ZF0"), X("ZZ"), pc(25), A.mult)
-        ts(X("ZB0"), X("ZZ"), pc(26), A.mult)
-        ts(X("Ih"), X("D0"), 0.5, A.mult)
-        ts(X("B7"), X("BLKb"), 0.4375, A.mult)
-        cp(X("BF1"), X("BLKb"))
-        ts(X("BFh"), X("BLKb"), 0.5, A.mult)
-        ts(X("BF15"), X("BLKb"), pc(15), A.mult)
-        ts(X("trS"), X("tr"), pc(0), A.add)
-        cp(X("thF"), X("thI"))
-        cp(X("Hc", 0, 1), X("thF", 0, 1))
-        ts(X("bB"), X("thF", 1, 2), 2.0, A.mult, -1.0, A.add)
+    for n, src, j in (("W00", "D0", 11), ("W11", "D0", 5), ("W01", "Sp", 11), ("W10", "Sm", 5)):
+        ts(X(n), X(src), pc(j), A.mult)
+    ts(pc(12), pc(2), 32.0, A.mult, pc(4), A.add)
+    ts(pc(13), pc(3), 16.0, A.mult, pc(12), A.add)
+    ts(X("LP"), X("iF"), pc(13), A.add)
+    ts(X("ZFe"), X("ZZ"), pc(10), A.mult)
+    ts(X("ZFo"), X("ZZ"), pc(1), A.mult)
+    cp(X("ZFa"), X("ZZ"))
+    cp(X("thF"), X("thI"))
+    cp(X("b8"), X("BLK", 0, 128, 16))
+    cp(X("b8h"), X("b8"))
+    cp(X("b8f"), X("b8"))
+    ts(X("r15"), X("b8"), pc(8), A.mult)
+    ts(X("SelP", 0, 16, 2), X("b8"), pc(10), A.mult)
+    ts(X("SelP", 1, 16, 2), X("b8"), pc(1), A.mult)
+    ts(pc(14), pc(0), 0.0, A.is_equal, -1.0, A.mult)
+    ts(X("b80"), X("b8"), pc(14), A.mult)
+    ts(X("u34"), X("k34"), 0.0, A.mult, X("thF", 1, 2), A.add)
+    fill(X("u34", SEG - 1, SEG), 2.0)
+    for n in range(8):
+        ts(X("TH", SEG * n, SEG * n + SEG), X("u34"), X("b80", n, n + 1), A.mult)
+    ts(X("TH", 16, NK, SEG), X("b80"), X("thF", 0, 1), A.mult)
+    cp(X("I16"), X("D0"))
+    cp(X("N16"), X("In"))
+    cp(X("I32"), X("D0"))
+    ts(X("NEG"), X("D0"), -128.0 * U, A.mult)
+    ts(X("MD"), X("rr", 0, 128), pc(0), A.is_equal)
+    tri = (T.TRI[:, :, :], "TRI", 0, 256, 256)
+    ts(X("ta"), X("rr"), pc(0), A.is_gt)
+    ts(X("tb"), X("rr"), pc(0), A.is_equal)
+    tt(tri, X("ta"), X("tb"), A.subtract)
+    cp(X("Lg"), X("iI"))
+    ts(X("LL"), X("iF"), pc(4), A.add)
+    ts(X("ii"), X("ii"), pc(0), A.add)
+    ts(X("trS"), X("ii"), W - U - OFF, A.add)
+    for n in range(8):
+        ts(X("CMP", 8 * n, 8 * n + 8), X("b8"), -1.0e9, A.mult, 1.0e9 + 2 * U, A.add)
+    fill(X("w34", 16, 17), 64.0)
+    fill(X("w34", 33, 34), 1.0)
+    ts(pc(15), pc(9), -16.0, A.mult)
+    ts(pc(16), pc(1), -2.0, A.mult, 1.0, A.add)
+    ts(pc(17), pc(0), 14.0, A.is_lt, 16.0, A.mult)
+    tt(pc(18), pc(16), pc(17), A.mult)
+    ts(X("w34"), X("w34"), pc(8), A.mult)
+    ts(X("t34"), X("k34"), pc(0), A.is_equal, pc(15), A.mult)
+    tt(X("w34"), X("w34"), X("t34"), A.add)
+    ts(X("w34", 0, 16), X("w34", 0, 16), pc(18), A.subtract)
+    ts(X("w34", 17, 33), X("w34", 17, 33), pc(18), A.add)
+    for n in range(8):
+        ts(X("WP", SEG * n, SEG * n + SEG), X("w34"), X("b8", n, n + 1), A.mult, U, A.mult)
+    for j in range(5):
+        a, b = PIECES[j], PIECES[j + 1]
+        ts(X("nbS", a, b), X("nbI", a, b), -OFF, A.add)
 
     nxt = T.cores[(rank + 1) % len(T.cores)]
     prv = T.cores[(rank - 1) % len(T.cores)]
     adr = topo.addr(nxt)
     eng = topo.engines(core, nxt)
-    half = len(eng) // 2
-    msk = sum(1 << e for e in eng[:half])
-    n_in = len(topo.engines(prv, core)) // 2
+    ne = len(eng)
+    msk = lambda es: sum(1 << e for e in es)
+    n_in = len(topo.engines(prv, core))
     loc = [0]
 
-    def send(dst, src, sem):
-        deps = {}
-        need("G", src[1], src[2], src[3], False, deps)
-        waits("G", deps)
-        g.remote_dma(dst, src[0], T.sem[sem], T.sem.loc, adr[1], adr[0], msk)
-        loc[0] += half
+    def send(items):
+        def run():
+            deps = {}
+            for dst, src, sem in items:
+                need("G", src[1], src[2], src[3], False, deps)
+            waits("G", deps)
+            if len(items) == 1:
+                dst, src, sem = items[0]
+                g.remote_dma(dst[0], src[0], T.sem[sem], T.sem.loc, adr[1], adr[0], msk(eng[:ne]))
+            else:
+                m = ne // len(items)
+                g.remote_dma_fused([RemoteDMATransfer(dst_ids=[DstId(rid=adr[0], pnc=adr[1])], dma_engine_mask=msk(eng[m * j:m * j + m]),
+                                                      remote_sem=T.sem[sem], src=src[0], dst=dst[0])
+                                    for j, (dst, src, sem) in enumerate(items)], local_sem=T.sem.loc)
+            loc[0] += ne
+        call("G", run, [it[1] for it in items], [it[0] for it in items], 150.0, lag=WAY)
 
-    def arrive(t):
-        rec["VL%d" % t] = [(0, 16, "R", "al%d" % t, n_in, True)]
-        rec["VB%d" % t] = [(0, 256, "R", "av%d" % t, n_in, True)]
-        rec["z%d" % t] = [(0, 128, "R", "ay%d" % t, n_in, True), (128, 256, "R", "az%d" % t, n_in, True)]
-
-    def expand(copy, dst, src, i0, i1):
-        a, b = 16 * i0, 16 * i1
-        copy(X(dst, a, b, 16), X(src, i0, i1))
-        for k in (8, 4, 2, 1):
-            copy(X(dst, a + k, b, 2 * k), X(dst, a, b, 2 * k))
-
-    def targets(t, c):
-        expand(scp, "zE", "z%d" % t, 64 * c, 64 * c + 64)
+    for t in range(1, 4):
+        rec["VL%d" % t] = [(8 * h, 8 * h + 8, "R", "al%d%d" % (t, h), n_in, True) for h in range(2)]
+        rec["VB%d" % t] = [(128 * h, 128 * h + 128, "R", "av%d%d" % (t, h), n_in // 2, True) for h in range(2)]
+        rec["zz%d" % t] = [(128 * h, 128 * h + 128, "R", "az%d%d" % (t, h), n_in // 2, True) for h in range(2)]
 
     def ind_x(off):
         return IND(X("xdS", 0, W), off)
@@ -289,249 +486,192 @@ def rank_program(g, core, T, topo):
     def ind_n(off):
         return IND(X("nbS", 0, W), off)
 
-    def erow(E, q):
-        return (T[E][:, q, 0:256 - 16 * q], E, 256 * q, 240 * q + 256)
+    def Hf(n, h, p=128):
+        return X(n, 128 * h, 128 * h + 128, p=p)
 
-    def count(ps, lhs, E):
-        mms([(X(ps, 16 * q, 256), lhs(q), erow(E, q)) for q in range(16)])
+    def Q(n, h):
+        return X(n, 8 * h, 8 * h + 8)
 
-    def to_list(ps, src):
-        mms([(X(ps, 480, 496), X("ZB0", 15 - r, 143 - r), X(src, r, 256, 16)) for r in range(16)])
+    def level(t, h):
+        replicate(t, h)
+        tt(Hf("dz", h), ind_x(Q("VL%d" % t, h)), Hf("zz%d" % t, h), A.subtract)
+        adz = Hf("zz%d" % t, 2 + h)
+        act(adz, Hf("dz", h), F.Abs)
+        act(Hf("far", h), adz, F.Relu, bias=pc(19))
+        mms([(Hf("pM", h), X("LT"), Hf("far", h))])
+        act(Hf("Pb", h), Hf("pM", h), F.Relu, bias=pc(7), scale=-1.0)
+        ps = "pN" if h else "pS0"
+        for c in range(4):
+            mms([(Hf(ps, c), X("M2"), Hf("Pb", h))])
+        scp(X("m4%d" % h), X(ps))
 
-    def place(ps, src, out):
-        tt(X("o1"), X(ps, 480, 496), X(src), A.add)
-        tt(X("o2"), X("o1"), X("trS"), A.min)
-        ts(X(out), X("o2"), 1536.0, A.add)
+    def ccols(h, kh, par, a=0, b=64):
+        c = 256 * h + 128 * kh + 64 * par
+        return X("cU", c + a, c + b)
 
-    def new_contacts():
-        nw = X("ps0", 0, 256)
-        tt(nw, nw, X("conF"), A.subtract)
-        tt(nw, nw, X("ohb"), A.mult)
-        tt(X("wv"), nw, X("conF"), A.add)
-
-    for t in range(4):
-        VL, VB, z, E, pk = "VL%d" % t, "VB%d" % t, "z%d" % t, "E3%d" % (t % 2), "pk%d" % t
-        last = t == 3
-
-        if t == 0:
-            targets(0, 0)
-        tt(X("dz"), ind_x(X(VL)), X(z), A.subtract)
-        ts(X("nn"), X("dz"), 1.0, A.is_gt)
-        ts(X("nm"), X("dz"), -1.0, A.is_lt)
-        mms([(X("ps6", 0, 256), X("VW"), X("nn")), (X("ps6", 0, 256), X("VW"), X("nm"))])
-        act(X("adz"), X("dz"), F.Abs)
-        mms([(X("ps5", 0, 256), X("D0"), X("adz")), (X("ps5", 0, 256), X("In"), X(z))])
-        if not last:
-            ts(X("xi"), X("dz"), 0.5, A.mult, 191.75, A.add)
-            mms([(X("ps5", 256, 512), X("D0"), X("xi")), (X("ps5", 256, 512), X("D0"), X(z))])
-        if t > 0:
-            new_contacts()
-            place("ps2", "o3", "offR")
-        else:
-            targets(0, 1)
-        targets(t, 2)
-        scp(X("dlt"), X("ps5", 0, 256))
-        if not last:
-            act(X("xn"), X("ps5", 256, 512), F.Copy, bias=-192.0)
-        ts(X("Pb"), X("ps6", 0, 256), pc(20), A.is_lt)
-        mms([(X("ps1", 0, 256), X("M2"), X("Pb"))])
-        mms([(X("ps1", 256, 512), X("M1"), X("Pb"))])
-        mms([(X("ps6", 0, 256), X("KE"), X("Pb"))])
-        mms([(X("ps6", 256, 512), X("KO"), X("Pb"))])
-        scp(X("m2"), X("ps1", 0, 256))
-        ts(X("vS"), X(VL), -1536.0, A.add)
-        if t == 0:
-            more_consts()
-            for j in range(4):
-                a, b = j * C4, (j + 1) * C4
-                ts(X("nbS", a, b), X("nbI", a, b), -1536.0, A.add)
-        else:
-            cp(IND(X("nbS", 0, WT), X("offR")), X("wv"))
-        ts(X("conU"), ind_n(X(VL)), 1536.0, A.add)
-        expand(cp, "maskE", "m2", 0, 64)
-        for c in range(1, 4):
-            expand(scp, "maskE", "m2", 64 * c, 64 * c + 64)
-            if c == 1:
-                act(X("conF"), ind_n(X(VL)), F.Copy)
-
-        def gather_nb(c):
-            s = 1024 * c
-            tt(X("mk", s, s + 1024), ind_n(X("conU", 64 * c, 64 * c + 64)), X("maskE", s, s + 1024), A.mult)
+    def candidates(t, h):
+        cp(Hf("con", h), ind_n(Q("VL%d" % t, h)))
+        for a in range(2):
+            mms([(PX(4 * h, 4 * h + 4, 16 * a, 16 * a + 16), X("W%d%d" % (a, b)), X("con", 128 * h + 64 * b, 128 * h + 64 * b + 64))
+                 for b in range(2)])
+        src, dst = PX(4 * h, 4 * h + 4), Hf("TT", h)
+        op("V", lambda e: e.transpose(dst[0], src[0]), [src], [dst], ns(dst, src))
+        ts(Hf("Tt", h), IND(Hf("TT", h), X("LP")), OFF, A.add)
+        ts(Q("vS", h), Q("VL%d" % t, h), -OFF, A.add)
+        for kh in range(2):
+            s = 2048 * h + 1024 * kh
+            for c in range(2):
+                a = 128 * h + 64 * kh + 32 * c
+                tt(X("mk", s + 512 * c, s + 512 * c + 512), ind_n(X("Tt", a, a + 32)), X("m4%d" % h), A.mult)
             for par, zz in ((0, "ZFe"), (1, "ZFo")):
-                col = par * 128 + (c % 2) * 64
-                mms([(X("ps%d" % (3 + c // 2), col, col + 64), X(zz, 15 - k, 143 - k), X("mk", s + k, s + 1024, 16))
-                     for k in range(16)])
+                slot = PX(8 + 4 * kh + 2 * par, 10 + 4 * kh + 2 * par)
+                mms([(slot, X(zz, 15 - r, 143 - r), X("mk", s + r, s + 1024, 16)) for r in range(16)])
+                if h == 0 and kh == 0:
+                    ts(ccols(h, kh, par), slot, OFF, A.add)
+            if h or kh:
+                ts(ccols(h, kh, 0, 0, 128), PX(8 + 4 * kh, 12 + 4 * kh), OFF, A.add)
 
-        def lists(h):
-            ts(X("cU", 256 * h, 256 * h + 256), X("ps%d" % (3 + h), 0, 256), 1536.0, A.add)
+    def keys(t, h):
+        mms([(X("pK", 0, NK), Hf("Pb", h), X("WP"))], stop=False)
+        for c in range(4):
+            mms([(X("pK", k, NK, 17), X("mk", 2048 * h + 128 * k, 2048 * h + 128 * k + 128), X("SelP")) for k in range(4 * c, 4 * c + 4)],
+                start=False, stop=False, part="K%d%d" % (t, h))
+        mms([(X("pK", 16, NK, SEG), Hf("co", h), X("b8h")), (X("pK", 33, NK, SEG), Hf("con", h), X("r15"))],
+            start=False, stop=False, part="K%d%d" % (t, h))
 
-        gather_nb(0)
-        gather_nb(1)
-        tt(X("co"), X("ps1", 256, 512), X("conF"), A.mult)
-        cp(X("ohb"), X("ps1", 256, 512))
-        mms([(X("ps2", 0, 16), X("ZFa", 15 - r, 143 - r), X("co", r, 256, 16)) for r in range(16)])
-        for par in range(2):
-            act((T.Wt[:, :, 128 * par:128 * par + 128], "Wt", 0, 512), X("ps6", 256 * par, 256 * par + 256), F.Exp,
-                bias=pc(28 + par), scale=-16.0 * LN2)
-        gather_nb(2)
-        lists(0)
-        ts(X("TLu"), X("ps2", 0, 16), 1536.0, A.add)
-        gather_nb(3)
-        targets(t, 3)
+    turn = [0]
 
-        def dsum(c, par):
-            s = 1024 * (2 * c + par)
-            col = par * 128 + (c % 2) * 64
-            mms([(X("ps%d" % (5 + c // 2), col, col + 64), X("ZZ", 15 - k, 143 - k), X("dd", s + k, s + 1024, 16)) for k in range(16)])
-
-        def ccols(c, par):
-            col = 256 * (c // 2) + par * 128 + (c % 2) * 64
-            return X("cU", col, col + 64)
-
-        def raw(c):
-            act(X("xg", 1024 * c, 1024 * c + 1024), ind_x(ccols(c, 1)), F.Copy)
-
-        def raw_sub(c):
-            for b in range(2):
-                a0 = 1024 * c + 512 * b
-                mms([(X("ps%d" % b), X("D0"), X("xg", a0, a0 + 512)), (X("ps%d" % b), X("In"), X("zE", a0, a0 + 512))])
-
-        def raw_abs(c):
-            s = 1024 * (2 * c + 1)
-            for b in range(2):
-                act(X("dd", s + 512 * b, s + 512 * b + 512), X("ps%d" % b), F.Abs)
-            dsum(c, 1)
-
-        def cand(c, par):
-            s = 1024 * (2 * c + par)
-            tt(X("dd", s, s + 1024), ind_x(ccols(c, par)), X("zE", 1024 * c, 1024 * c + 1024), A.subtract)
-            act(X("dd", s, s + 1024), X("dd", s, s + 1024), F.Abs)
-            dsum(c, par)
-
-        def pairs():
-            if t == 0:
-                cp(X(VB), IND(X("idW"), X(VL)))
-            for q in range(16):
-                ts(erow(E, q), X(VB, 16 * q, 256), X("vS", q, q + 1), A.is_equal)
-            diag = (T[E][:, :, 0:16], E, 0, 4096)
-            tt(diag, diag, (T.TRI[:, :, :], "TRI", 0, 256), A.mult)
-
-        def relu(h):
-            act(X("ps%d" % (5 + h), 0, 256), X("ps%d" % (5 + h), 0, 256), F.Relu, bias=X("bB"), scale=-2.0)
-
-        raw(0)
-        raw_sub(0)
-        raw(1)
-        cand(0, 0)
-        raw_abs(0)
-        raw_sub(1)
-        lists(1)
-        pairs()
-        if not last:
-            count("ps2", lambda q: X("BLKb"), E)
-        raw(2)
-        tt(X("d0"), ind_x(X("TLu")), X(z), A.subtract)
-        act(X("d0"), X("d0"), F.Abs)
-        mms([(X("ps7", 256, 512), X("BLKb"), X("d0"))])
-        raw_abs(1)
-        raw_sub(2)
-        cand(1, 0)
-        if not last:
-            scp(X("cb"), X("ps2", 0, 256))
-            to_list("ps2", "cb")
-        cand(2, 0)
-        raw_abs(2)
-        hb = X("ps7", 256, 512)
-        ts(hb, hb, X("Hc", t, t + 1), A.is_lt, 2.0, A.mult)
-        tt(X("hc"), hb, X("co"), A.mult)
-        relu(0)
-        act(X("hb2"), hb, F.Copy, acc=X("hs", t, t + 1))
-        cand(3, 0)
-
-        def tail_a(h):
-            tt(X("hw", 256 * h, 256 * h + 256), X("ps%d" % (5 + h), 0, 256), (T.Wt[:, h, :], "Wt", 256 * h, 256 * h + 256), A.min)
-            s = X("ps7", 128 * h, 128 * h + 128)
-            mms([(s, X("B7"), X("hw", 256 * h, 256 * h + 128)), (s, X("B7"), X("hw", 256 * h + 128, 256 * h + 256)),
-                 (s, X("Ih"), X("hb2", 128 * h, 128 * h + 128))])
-
-        def tail_b(h):
-            a, b = 128 * h, 128 * h + 128
-            s = X("ps7", a, b)
-            for par in range(2):
-                u = 256 * h + 128 * par
-                tt(X("fi", u, u + 128), X("hw", u, u + 128), s, A.is_gt)
-            tt(X("fc", 256 * h, 256 * h + 256), X("ps%d" % (3 + h), 0, 256), X("fi", 256 * h, 256 * h + 256), A.mult)
-            lo = X("ps1", 256 + a, 256 + b)
-            ts(lo, s, 0.0, A.is_equal)
-            tt(X("lc", a, b), lo, X("conF", a, b), A.mult)
-            o = X("ps0", a, b)
-            mms([(o, X("BFh"), X("hc", a, b)), (o, X("BF1"), X("fc", 256 * h, 256 * h + 128)),
-                 (o, X("BF1"), X("fc", 256 * h + 128, 256 * h + 256)), (o, X("BF15"), X("lc", a, b))])
-            tt(lo, lo, X("dlt", a, b), A.mult)
-            zn = X("zn%d" % t, a, b)
-            tt(zn, lo, X(z, a, b), A.add)
-            if not last:
-                send(T["z%d" % (t + 1)][:, a:b], zn, ("ay%d" if h == 0 else "az%d") % (t + 1))
+    def distances(t, h):
+        for n in range(8):
+            kh, par, s = n // 4, n // 2 % 2, n % 2
+            a = 4096 * h + 512 * n
+            dd = X("dd", a, a + 512)
+            src = ind_x(ccols(h, kh, par, 32 * s, 32 * s + 32))
+            if n < ON_SCALAR[h]:
+                ps = X("pS%d" % (turn[0] % 2))
+                turn[0] += 1
+                act(X("xg", a, a + 512), src, F.Copy)
+                mms([(ps, X("In"), X("z4%d" % h)), (ps, X("D0"), X("xg", a, a + 512))])
+                act(dd, ps, F.Abs)
             else:
-                dma("Y", T.yz[:, a:b], [], zn[0], [zn], "yz%d" % h)
-            tt(X(pk, 256 + a, 256 + b), s, X("hb2", a, b), A.is_gt)
+                tt(dd, src, X("z4%d" % h), A.subtract)
+                act(dd, dd, F.Abs)
+            mms([(X("pD%d" % h, 17 * par + 8 * kh + 4 * s + k, NK, SEG), X("dd", a + 128 * k, a + 128 * k + 128), X("b8")) for k in range(4)],
+                start=False, part="D%d%d" % (t, h))
 
-        def weigh(qs, on_scalar):
-            for q in qs:
-                if on_scalar:
-                    act(X("LQ", 128 * q, 128 * q + 128), X("BLKb"), F.Copy, scale=X("rp", q, q + 1))
-                else:
-                    ts(X("LQ", 128 * q, 128 * q + 128), X("BLKb"), X("rp", q, q + 1), A.mult)
+    def erow(q):
+        return (T.E[:, q, 0:256 - 16 * q], "E", 256 * q, 240 * q + 256, 256 - 16 * q)
 
-        tail_a(0)
-        cand(3, 1)
-        relu(1)
-        if last:
-            act(X("yn", 0, W), X("nbS", 0, W), F.Copy, bias=1536.0)
-        tail_b(0)
-        if not last:
-            place("ps2", "vS", "offA")
-            scp(X("hsb", t, t + 1), X("hs", t, t + 1))
-            mms([(X("ps4", 256, 257), X("AW"), X("hsb", t, t + 1))])
-        tail_a(1)
-        cp(X(pk, 0, 128), X("ps0", 0, 128))
-        tail_b(1)
-        cp(X(pk, 128, 256), X("ps0", 128, 256))
-        mms([(X("ps5", 256, 288), X("ZF0", 15 - r, 143 - r), X(pk, r, 512, 16)) for r in range(16)])
-        if not last:
-            ts(X("hi0", t, t + 1), X("ps4", 256, 257), -1.0, A.mult, 2048.0, A.add)
-            ts(X("hi1", t, t + 1), X("hi0", t, t + 1), 15, A.bitwise_and)
-            tt(X("Hc", t + 1, t + 2), X("hi1", t, t + 1), X("thF", 0, 1), A.add)
-        ts(X("VN%d" % t if not last else "yvS"), X("ps5", 256, 272), 1536.0, A.add)
-        if not last:
-            send(T["VL%d" % (t + 1)][:, :], X("VN%d" % t), "al%d" % (t + 1))
-            send(T["VB%d" % (t + 1)][:, :], X(pk, 0, 256), "av%d" % (t + 1))
-            arrive(t + 1)
-            targets(t + 1, 0)
+    def to_list(out, src, a, b, vs):
+        mms([(out, X("I32"), vs)] + [(out, X("ZB", 15 - r, 143 - r, p=8), X(src, a + r, b, 16, p=8)) for r in range(16)])
+
+    def place(out, ps, tmp, tr):
+        tt(tmp, ps, tr, A.min)
+        ts(out, tmp, U + OFF, A.add)
+
+    def best(t, h):
+        act(X("R%d" % h), X("pD%d" % h, 0, NK), F.Relu, bias=pc(20))
+        mms([(X("pK", 0, NK), X("NEG"), X("R%d" % h))], start=False)
+        sc, pk = X("sc%d" % h), X("pK", 0, NK)
+        op("V", lambda e: e.tensor_tensor_scan(sc[0], T.RST[:, :], pk[0], 0.0, A.mult, A.max), [X("RST"), pk], [sc], ns(sc, pk))
+        tt(Hf("Vm", h), IND(sc, X("Lg")), X("MD"), A.mult)
+        val = Q("pM", 2 + h)
+        mms([(val, Hf("Vm", h), X("b8f"))])
+        ts(Q("vi", h), val, OFF, A.add)
+        act(Q("sg", h), val, F.Sign, bias=pc(21), acc=X("hs", 2 * t + h, 2 * t + h + 1))
+        ts(Q("vc", h), Q("vi", h), int(U) - 1, A.bitwise_and)
+        ts(Q("pr", h), Q("vi", h), 63 * int(U), A.bitwise_and)
+        cp(Q("VN%d" % t, h), Q("vc", h))
+        if t < 3:
+            send([(Q("VL%d" % (t + 1), h), Q("VN%d" % t, h), "al%d%d" % (t + 1, h))])
+        tt(X("LQ", 64 * h, 64 * h + 64), IND(Q("pr", h), X("LL", 0, 4)), X("CMP"), A.is_ge)
+        lq = lambda q: X("LQ", 8 * q, 8 * q + 8)
+        if h == 0:
+            mms([(X("pN", 16 * q, 256, p=8), lq(q), erow(q)) for q in range(8)])
+            scp(X("crb", p=8), X("pN", 0, 256, p=8))
+            to_list(Q("pN", 40), "crb", 0, 128, Q("vS", 0))
         else:
-            dma("Y", T.yv[:, :], [], T.yvS[:, :], [X("yvS")], "yv")
-        scp(X("rp"), X("ps5", 272, 288))
-        weigh(range(0, 10), False)
-        weigh(range(10, 16), True)
-        count("ps2", lambda q: X("LQ", 128 * q, 128 * q + 128), E)
+            mms([(X("pN", 0, 128, p=8), X("D0", 0, 8, p=8), Hf("crb", 1, p=8))]
+                + [(X("pN", 16 * q - 128, 128, p=8), lq(q), erow(q)) for q in range(8, 16)])
+            scp(X("crc", p=8), X("pN", 0, 128, p=8))
+            to_list(Q("pN", 41), "crc", 0, 128, Q("vS", 1))
+        ts(Q("zf", h), Q("pr", h), U, A.is_equal, 256.0, A.mult)
+        tt(Q("zg", h), Q("zf", h), Q("ii", h), A.add)
+        cp(Q("zo", h), Q("zg", h))
+        zn = Hf("zn%d" % t, h)
+        act(zn, IND(X("zz%d" % t), Q("zo", h)), F.Copy)
+        cp(Hf("VO%d" % t, h), IND(X("idW"), Q("VN%d" % t, h)))
+        mms([(Hf("pM", 2 + h), X("M1"), Hf("Pb", h))])
+        tt(Hf("no", h), Hf("pM", 2 + h), Hf("VO%d" % t, h), A.mult)
+        if t < 3:
+            send([(Hf("zz%d" % (t + 1), h), zn, "az%d%d" % (t + 1, h)), (Hf("VB%d" % (t + 1), h), Hf("VO%d" % t, h), "av%d%d" % (t + 1, h))])
+        else:
+            dmas("Y", "yz%d" % h, [(T.yz[:, 128 * h:128 * h + 128], zn)], 32768)
+            cp(Q("yvS", h), Q("vc", h))
+        place(Q("offR", h), Q("pN", 40 + h), Q("o2", h), Q("trS", h))
+        tt(IND(X("nbS" if t < 3 else "yn", 0, WT), Q("offR", h)), Hf("no", h), Hf("A1", h), A.add)
+
+    cp(X("VB0"), IND(X("idW"), X("VL0")))
+    for t in range(4):
+        zz = "zz%d" % t
+        last = t == 3
+        if last:
+            act(X("yn", 0, W), X("nbS", 0, W), F.Copy, bias=OFF)
+        for h in range(2):
+            lift[0] = FIRST * (1 - h)
+            level(t, h)
+            candidates(t, h)
+            mms([(X("pD%d" % h, 0, NK), one, X("TH"))], stop=False)
+        lift[0] = FIRST
+        mms([(X("pM", 256, 512), X("M1"), X("Pb"))])
+        tt(X("co"), X("pM", 256, 512), X("con"), A.mult)
+        mms([(X("pM", 0, 16), X("ZFa", 15 - r, 143 - r), X("co", r, 256, 16)) for r in range(16)])
+        ts(X("TLu"), X("pM", 0, 16), OFF, A.add)
+        tt(X("d0"), ind_x(X("TLu")), X(zz, 0, 256), A.subtract)
+        act(X("d0"), X("d0"), F.Abs)
+        for h in range(2):
+            mms([(X("pD%d" % h, 16, NK, SEG), Hf("d0", h), X("b8"))], start=False, part="D%d%d" % (t, h))
+        mms([(X("pN", 256, 512), X("I16"), X("con")), (X("pN", 256, 512), X("N16"), X("co"))])
+        if last:
+            act(X("A1"), X("pN", 256, 512), F.Copy, bias=OFF)
+        else:
+            scp(X("A1"), X("pN", 256, 512))
+        for q in range(16):
+            ts(erow(q), X("VB%d" % t, 16 * q, 256), X("vS", q, q + 1), A.is_equal)
+        diag = (T.E[:, :, 0:16], "E", 0, 4096, 256)
+        tt(diag, diag, tri, A.mult)
+        lift[0] = 0.0
+        if not last:
+            mms([(X("pN", 16 * q, 256, p=8), X("b8"), erow(q)) for q in range(16)])
+            scp(X("cb", p=8), X("pN", 0, 256, p=8))
+            to_list(X("pN", 336, 352), "cb", 0, 256, X("vS"))
+            place(X("offA"), X("pN", 336, 352), X("o3"), X("trS"))
+            act(X("xi"), X("dz"), F.Copy, bias=191.75, scale=0.5)
+            mms([(X("pM", 256, 512), X("D0"), X("xi")), (X("pM", 256, 512), X("D0"), X(zz, 0, 256))])
+            act(X("xn"), X("pM", 256, 512), F.Copy, bias=-192.0)
+        for h in range(2):
+            lift[0] = FIRST * (1 - h)
+            keys(t, h)
+            distances(t, h)
+            best(t, h)
         if not last:
             cp(IND(X("xdS", 0, WT), X("offA")), X("xn"))
-            targets(t + 1, 1)
-        ts(X("q1"), X("rp"), -4096.0, A.mult, 4096.0, A.add)
-        tt(X("o3"), X("q1"), X("vS"), A.add)
-        scp(X("crb"), X("ps2", 0, 256))
-        to_list("ps2", "crb")
-    new_contacts()
-    place("ps2", "o3", "offR")
-    ot = IND(X("yn", 0, WT), X("offR"))
-    op("V", lambda e: e.tensor_scalar(ot[0], T.wv[:, :], 1.0, 1536.0, A.mult, A.add), [X("wv"), ot[2]], [ot[1]])
+            mms([(X("pM", 32, 33), X("on32"), X("hs", 2 * t + h, 2 * t + h + 1)) for h in range(2)])
+            ts(X("hi0", t, t + 1), X("pM", 32, 33), -0.5, A.mult, 1024.0, A.add)
+            ts(X("hi1", t, t + 1), X("hi0", t, t + 1), 15, A.bitwise_and)
+            tt(X("Hc", t, t + 1), X("hi1", t, t + 1), X("thF", 0, 1), A.add)
+            ts(X("TH", 16, NK, SEG), X("b80"), X("Hc", t, t + 1), A.mult)
+        else:
+            dmas("Y", "yv", [(T.yv[:, :], X("yvS"))], 8192)
 
+    C4 = W // 4
     for j in range(4):
         a, b = j * C4, (j + 1) * C4
-        dma("Y" if j % 2 == 0 else "S", T.ynb[:, a:b], [], T.yn[:, a:b], [X("yn", a, b)], "y%d" % j)
-    fin = {s: cnt[s] for s in cnt}
-    for d in DMAS:
-        fin["d_" + d] = 16
+        dmas("Y" if j % 2 == 0 else "S", "y%d" % j, [(T.ynb[:, a:b], X("yn", a, b))], 512 * C4)
+    for j in plan():
+        calls[j]["run"]()
+    fin = dict(cnt)
+    fin.update(dsem)
     fin["loc"] = loc[0]
     for s in fin:
         if known["G"].get(s, 0) < fin[s]:

@@ -1,3 +1,4 @@
+import numpy as np
 from concourse.bass import DstId, RemoteDMATransfer
 from concourse.mybir import dt, AluOpType, AxisListType, ActivationFunctionType
 
@@ -5,17 +6,20 @@ W = 3072
 WT = W + 256
 OFF = 1536.0
 U = 4096.0
+BIG = 128 * U
 SEG = 34
 NK = 8 * SEG
-ON_SCALAR = (6, 2)
-CYCLE, GATHER, SCATTER, HOP, DMA_LAG, DMA_RATE, WAY = 0.83, 1.3, 3.1, 280.0, 2500.0, 190.0, 4500.0
-PASSES, FIRST, BANK = 4, 0.0, 100.0
+ON_SCALAR = (7, 3)
+CYCLE, GATHER, SCATTER, HOP, DMA_LAG, DMA_RATE, WAY = 0.83, 1.3, 3.1, 280.0, 2500.0, 350.0, 4000.0
+PASSES, SHAKE, SEED, BANK, EARLY = 60, 1500.0, 1, 200.0, 1
+PLAN = []
+LOADS = "n0 n1 pv pz xa xb n2 n3 n4 th"
 
 SCRATCH = {
     "nbI": ("sbuf", [128, W], "int32"), "nbS": ("sbuf", [128, WT], "float32"), "xdS": ("sbuf", [128, WT], "bfloat16"),
     "idW": ("sbuf", [128, W], "float32"), "yn": ("sbuf", [128, WT], "float32"),
     "E": ("sbuf", [128, 16, 256], "bfloat16"), "TRI": ("sbuf", [128, 16, 16], "bfloat16"),
-    "px": ("psum", [128, 16, 32], "float32"),
+    "px0": ("psum", [128, 16, 32], "float32"), "px1": ("psum", [128, 16, 32], "float32"),
 }
 PART = {}
 
@@ -26,7 +30,7 @@ def _decl():
                            ("dz far Pb xi xn d0 cb crb zn0 zn1 zn2 zn3 ta tb tc", 256, "bfloat16"),
                            ("VB0 VB1 VB2 VB3 VO0 VO1 VO2 VO3 con co", 256, "float16"),
                            ("TT A1 no Vm rr", 256, "float32"), ("Tt", 256, "uint16"), ("cU", 512, "uint16"),
-                           ("WP TH RST R0 R1 ones", NK, "bfloat16"), ("sc0 sc1", NK, "float32"), ("w34 k34 t34 u34", SEG, "float32"),
+                           ("WP TH RST ones", NK, "bfloat16"), ("sc0 sc1 R0 R1", NK, "float32"), ("w34 k34 t34 u34", SEG, "float32"),
                            ("VL0 VL1 VL2 VL3 VN0 VN1 VN2 VN3 TLu offA offR zo", 16, "uint16"), ("Lg LP LL", 8, "uint16"),
                            ("vS o2 o3 yvS ii trS zf zg", 16, "float32"), ("pvI vi vc pr", 16, "int32"), ("sg", 16, "bfloat16"),
                            ("thI", 2, "int32"), ("thF", 2, "float32"), ("Hc", 4, "float32"), ("hs", 8, "float32"),
@@ -34,7 +38,7 @@ def _decl():
                            ("ZZ ZB", 144, "bfloat16"), ("ZFe ZFo ZFa", 144, "float16"),
                            ("BLK D0 D1 D2 CA CB D0n mt M1 M2 M2a In LT NEG Sp Sm LQ crc", 128, "bfloat16"),
                            ("I16 N16 W00 W01 W10 W11", 128, "float16"), ("I32 MD on32", 128, "float32"), ("CMP", 64, "float32"),
-                           ("b8 b80", 8, "bfloat16"), ("b8h r15", 8, "float16"), ("b8f", 8, "float32"), ("SelP", 16, "float16")):
+                           ("b8 b80 b8n b8p b8m", 8, "bfloat16"), ("b8h r15", 8, "float16"), ("b8f", 8, "float32"), ("SelP", 16, "float16")):
         for n in names.split():
             if cols > 32:
                 SCRATCH[n] = ("sbuf", [128, cols], d)
@@ -43,7 +47,7 @@ def _decl():
                 at = SCRATCH[home][1][1] if home in SCRATCH else 0
                 PART[n] = (home, at, cols)
                 SCRATCH[home] = ("sbuf", [128, at + (cols + 15) // 16 * 16], d)
-    for b in "pK pD0 pD1 pS0 pS1 pM pN".split():
+    for b in "pD0 pD1 pS0 pS1 pM pN".split():
         SCRATCH[b] = ("psum", [128, 512], "float32")
 
 
@@ -97,7 +101,6 @@ def rank_program(g, core, T, topo):
 
     calls = []
     seen = {}
-    lift = [0.0]
 
     def call(q, run, reads, writes, ns, lag=0.0, adds=False, nbytes=0):
         me = len(calls) + (1 if nbytes else 0)
@@ -137,19 +140,22 @@ def rank_program(g, core, T, topo):
                     lo, hi = 0, len(taken)
                     while lo < hi:
                         mid = (lo + hi) // 2
-                        if taken[mid][1] <= s:
+                        if taken[mid][1] + BANK <= s:
                             lo = mid + 1
                         else:
                             hi = mid
-                    if lo < len(taken) and taken[lo][0] < s + c["ns"]:
-                        s, moved = taken[lo][1], True
+                    while lo < len(taken) and taken[lo][0] < s + c["ns"] + BANK:
+                        gap = BANK if taken[lo][2] != c["uses"][0] else 0.0
+                        if taken[lo][0] < s + c["ns"] + gap and s < taken[lo][1] + gap:
+                            s, moved = taken[lo][1] + gap, True
+                        lo += 1
             at[j] = s
             for u in c["uses"]:
                 taken = busy[u]
                 k = len(taken)
                 while k and taken[k - 1][0] > s:
                     k -= 1
-                taken.insert(k, (s, s + c["ns"] + (BANK if u in SCRATCH else 0.0)))
+                taken.insert(k, (s, s + c["ns"], c["uses"][0]))
             for u in after[j]:
                 at[u] = max(at[u], s + c["ns"] + delay(j, u))
                 left[u] -= 1
@@ -158,6 +164,8 @@ def rank_program(g, core, T, topo):
         return at
 
     def plan():
+        if PLAN:
+            return PLAN
         n = len(calls)
         deps = [sorted(c["deps"]) for c in calls]
         users = [[] for c in calls]
@@ -166,14 +174,18 @@ def rank_program(g, core, T, topo):
                 users[d].append(j)
         key = list(range(n))
         best = None
-        for turn_ in range(PASSES):
+        shake = np.random.default_rng(SEED)
+        for k in range(PASSES):
             fw = place_calls(lambda j: key[j], deps, users, lambda a, b: calls[a]["lag"] + HOP)
             end = max(fw[j] + calls[j]["ns"] for j in range(n))
             if best is None or end < best[0]:
                 best = (end, fw)
-            bw = place_calls(lambda j: -(fw[j] + calls[j]["ns"]), users, deps, lambda a, b: calls[b]["lag"] + HOP)
+            src, amp = (best[1], SHAKE) if k % 3 == 2 else (fw, 0.0)
+            late = [-(src[j] + calls[j]["ns"]) + amp * float(u) for j, u in enumerate(shake.random(n))]
+            bw = place_calls(lambda j: late[j], users, deps, lambda a, b: calls[b]["lag"] + HOP)
             key = [-(bw[j] + calls[j]["ns"]) for j in range(n)]
-        return sorted(range(n), key=lambda j: (best[1][j], j))
+        PLAN.extend(sorted(range(n), key=lambda j: (best[1][j], j)))
+        return PLAN
 
     def kind(x):
         return SCRATCH[PART[x[1]][0] if x[1] in PART else x[1]]
@@ -214,8 +226,8 @@ def rank_program(g, core, T, topo):
             b = cols
         return (T[home][0:p, at + a:at + b:st] if st > 1 else T[home][0:p, at + a:at + b], n, a, b, len(range(a, b, st)))
 
-    def PX(a, b, c0=0, c1=32):
-        return (T.px[:, a:b, c0:c1], "px", 32 * a, 32 * b, (b - a) * (c1 - c0))
+    def PX(n, a, b, c0=0, c1=32):
+        return (T["px%d" % n][:, a:b, c0:c1], "px%d" % n, 32 * a, 32 * b, (b - a) * (c1 - c0))
 
     def IND(win, off):
         return (win[0].indirect(off[0]), win, off)
@@ -329,17 +341,18 @@ def rank_program(g, core, T, topo):
 
     H2 = W // 2
     PIECES = (0, 768, 1536, 2304, 2816, W)
-    lift[0] = 1.0e6
-    dmas("Y", "pv", [(X("pvI"), T.pv[:, :])], 8192)
-    dmas("S", "pz", [(X("zz0", 0, 256), T.pz[:, :])], 65536)
-    dmas("Y", "xa", [(X("xdS", 0, H2), T.xd[:, 0:H2])], 256 * H2)
-    dmas("S", "xb", [(X("xdS", H2, W), T.xd[:, H2:W])], 256 * H2)
-    dmas("Y", "th", [(X("thI"), T.th[:, :])], 1024)
-    lift[0] = 0.5e6
+    loads = {"pv": (X("pvI"), T.pv[:, :], 8192), "pz": (X("zz0", 0, 256), T.pz[:, :], 65536), "th": (X("thI"), T.th[:, :], 1024),
+             "xa": (X("xdS", 0, H2), T.xd[:, 0:H2], 256 * H2), "xb": (X("xdS", H2, W), T.xd[:, H2:W], 256 * H2)}
     for j in range(5):
         a, b = PIECES[j], PIECES[j + 1]
-        dmas("Y" if j % 2 == 0 else "S", "n%d" % j, [(X("nbI", a, b), T.nb[:, a:b])], 512 * (b - a))
-    lift[0] = 0.0
+        loads["n%d" % j] = (X("nbI", a, b), T.nb[:, a:b], 512 * (b - a))
+    done = DMA_LAG
+    for j, name in enumerate(LOADS.split()):
+        dmas("YS"[j % 2], name, [loads[name][:2]], loads[name][2])
+        calls[-2]["run"]()
+        done += calls[-1]["ns"] + 100.0
+        calls[-2].update({"run": lambda: None, "uses": [name], "lag": 0.0})
+        calls[-1].update({"ns": done, "uses": [name]})
 
     def replicate(t, h):
         src = X("zz%d" % t, 128 * h, 128 * h + 128)
@@ -410,7 +423,7 @@ def rank_program(g, core, T, topo):
     ts(X("r15"), X("b8"), pc(8), A.mult)
     ts(X("SelP", 0, 16, 2), X("b8"), pc(10), A.mult)
     ts(X("SelP", 1, 16, 2), X("b8"), pc(1), A.mult)
-    ts(pc(14), pc(0), 0.0, A.is_equal, -1.0, A.mult)
+    ts(pc(14), pc(0), 0.0, A.is_equal, BIG, A.mult)
     ts(X("b80"), X("b8"), pc(14), A.mult)
     ts(X("u34"), X("k34"), 0.0, A.mult, X("thF", 1, 2), A.add)
     fill(X("u34", SEG - 1, SEG), 2.0)
@@ -420,7 +433,8 @@ def rank_program(g, core, T, topo):
     cp(X("I16"), X("D0"))
     cp(X("N16"), X("In"))
     cp(X("I32"), X("D0"))
-    ts(X("NEG"), X("D0"), -128.0 * U, A.mult)
+    for n, v in (("b8n", -BIG), ("b8p", BIG), ("b8m", -2 * BIG)):
+        ts(X(n), X("b8"), v, A.mult)
     ts(X("MD"), X("rr", 0, 128), pc(0), A.is_equal)
     tri = (T.TRI[:, :, :], "TRI", 0, 256, 256)
     ts(X("ta"), X("rr"), pc(0), A.is_gt)
@@ -510,11 +524,14 @@ def rank_program(g, core, T, topo):
         return X("cU", c + a, c + b)
 
     def candidates(t, h):
-        cp(Hf("con", h), ind_n(Q("VL%d" % t, h)))
+        if t:
+            cp(Hf("con", h), ind_n(Q("VL%d" % t, h)))
+        else:
+            ts(Hf("con", h), IND(X("nbI"), Q("VL0", h)), -OFF, A.add)
         for a in range(2):
-            mms([(PX(4 * h, 4 * h + 4, 16 * a, 16 * a + 16), X("W%d%d" % (a, b)), X("con", 128 * h + 64 * b, 128 * h + 64 * b + 64))
+            mms([(PX(1 - h, 0, 4, 16 * a, 16 * a + 16), X("W%d%d" % (a, b)), X("con", 128 * h + 64 * b, 128 * h + 64 * b + 64))
                  for b in range(2)])
-        src, dst = PX(4 * h, 4 * h + 4), Hf("TT", h)
+        src, dst = PX(1 - h, 0, 4), Hf("TT", h)
         op("V", lambda e: e.transpose(dst[0], src[0]), [src], [dst], ns(dst, src))
         ts(Hf("Tt", h), IND(Hf("TT", h), X("LP")), OFF, A.add)
         ts(Q("vS", h), Q("VL%d" % t, h), -OFF, A.add)
@@ -524,20 +541,21 @@ def rank_program(g, core, T, topo):
                 a = 128 * h + 64 * kh + 32 * c
                 tt(X("mk", s + 512 * c, s + 512 * c + 512), ind_n(X("Tt", a, a + 32)), X("m4%d" % h), A.mult)
             for par, zz in ((0, "ZFe"), (1, "ZFo")):
-                slot = PX(8 + 4 * kh + 2 * par, 10 + 4 * kh + 2 * par)
-                mms([(slot, X(zz, 15 - r, 143 - r), X("mk", s + r, s + 1024, 16)) for r in range(16)])
-                if h == 0 and kh == 0:
-                    ts(ccols(h, kh, par), slot, OFF, A.add)
+                b = 4 + 4 * kh + 2 * par
+                cuts = ((0, 1), (1, 2)) if h + kh + par < EARLY else ((0, 2),)
+                for c0, c1 in cuts:
+                    slot = PX((c0 + par) % 2 if h + kh == 0 else kh, b + c0, b + c1)
+                    mms([(slot, X(zz, 15 - r, 143 - r), X("mk", s + 512 * c0 + r, s + 512 * c1, 16)) for r in range(16)])
+                    if h + kh == 0:
+                        ts(ccols(h, kh, par, 32 * c0, 32 * c1), slot, OFF, A.add)
             if h or kh:
-                ts(ccols(h, kh, 0, 0, 128), PX(8 + 4 * kh, 12 + 4 * kh), OFF, A.add)
+                ts(ccols(h, kh, 0, 0, 128), PX(kh, 4 + 4 * kh, 8 + 4 * kh), OFF, A.add)
 
     def keys(t, h):
-        mms([(X("pK", 0, NK), Hf("Pb", h), X("WP"))], stop=False)
-        for c in range(4):
-            mms([(X("pK", k, NK, 17), X("mk", 2048 * h + 128 * k, 2048 * h + 128 * k + 128), X("SelP")) for k in range(4 * c, 4 * c + 4)],
-                start=False, stop=False, part="K%d%d" % (t, h))
-        mms([(X("pK", 16, NK, SEG), Hf("co", h), X("b8h")), (X("pK", 33, NK, SEG), Hf("con", h), X("r15"))],
-            start=False, stop=False, part="K%d%d" % (t, h))
+        mms([(X("pM", 0, NK), Hf("Pb", h), X("WP"))]
+            + [(X("pM", k, NK, 17), X("mk", 2048 * h + 128 * k, 2048 * h + 128 * k + 128), X("SelP")) for k in range(16)]
+            + [(X("pM", 16, NK, SEG), Hf("co", h), X("b8h")), (X("pM", 33, NK, SEG), Hf("con", h), X("r15"))])
+        scp(X("R%d" % h), X("pM", 0, NK))
 
     turn = [0]
 
@@ -553,11 +571,14 @@ def rank_program(g, core, T, topo):
                 act(X("xg", a, a + 512), src, F.Copy)
                 mms([(ps, X("In"), X("z4%d" % h)), (ps, X("D0"), X("xg", a, a + 512))])
                 act(dd, ps, F.Abs)
+                terms = (("dd", "b8n"),)
             else:
                 tt(dd, src, X("z4%d" % h), A.subtract)
-                act(dd, dd, F.Abs)
-            mms([(X("pD%d" % h, 17 * par + 8 * kh + 4 * s + k, NK, SEG), X("dd", a + 128 * k, a + 128 * k + 128), X("b8")) for k in range(4)],
-                start=False, part="D%d%d" % (t, h))
+                ts(X("xg", a, a + 512), dd, 0.0, A.max)
+                terms = (("dd", "b8p"), ("xg", "b8m"))
+            for name, w in terms:
+                mms([(X("pD%d" % h, 17 * par + 8 * kh + 4 * s + k, NK, SEG), X(name, a + 128 * k, a + 128 * k + 128), X(w)) for k in range(4)],
+                    start=False, part="D%d%d" % (t, h))
 
     def erow(q):
         return (T.E[:, q, 0:256 - 16 * q], "E", 256 * q, 240 * q + 256, 256 - 16 * q)
@@ -570,12 +591,11 @@ def rank_program(g, core, T, topo):
         ts(out, tmp, U + OFF, A.add)
 
     def best(t, h):
-        act(X("R%d" % h), X("pD%d" % h, 0, NK), F.Relu, bias=pc(20))
-        mms([(X("pK", 0, NK), X("NEG"), X("R%d" % h))], start=False)
-        sc, pk = X("sc%d" % h), X("pK", 0, NK)
+        sc, pk = X("sc%d" % h), X("R%d" % h)
+        tt(pk, X("pD%d" % h, 0, NK), pk, A.min)
         op("V", lambda e: e.tensor_tensor_scan(sc[0], T.RST[:, :], pk[0], 0.0, A.mult, A.max), [X("RST"), pk], [sc], ns(sc, pk))
         tt(Hf("Vm", h), IND(sc, X("Lg")), X("MD"), A.mult)
-        val = Q("pM", 2 + h)
+        val = Q("pM", 60 + h)
         mms([(val, Hf("Vm", h), X("b8f"))])
         ts(Q("vi", h), val, OFF, A.add)
         act(Q("sg", h), val, F.Sign, bias=pc(21), acc=X("hs", 2 * t + h, 2 * t + h + 1))
@@ -589,26 +609,26 @@ def rank_program(g, core, T, topo):
         if h == 0:
             mms([(X("pN", 16 * q, 256, p=8), lq(q), erow(q)) for q in range(8)])
             scp(X("crb", p=8), X("pN", 0, 256, p=8))
-            to_list(Q("pN", 40), "crb", 0, 128, Q("vS", 0))
+            to_list(Q("pM", 58), "crb", 0, 128, Q("vS", 0))
         else:
             mms([(X("pN", 0, 128, p=8), X("D0", 0, 8, p=8), Hf("crb", 1, p=8))]
                 + [(X("pN", 16 * q - 128, 128, p=8), lq(q), erow(q)) for q in range(8, 16)])
             scp(X("crc", p=8), X("pN", 0, 128, p=8))
-            to_list(Q("pN", 41), "crc", 0, 128, Q("vS", 1))
+            to_list(Q("pM", 59), "crc", 0, 128, Q("vS", 1))
         ts(Q("zf", h), Q("pr", h), U, A.is_equal, 256.0, A.mult)
         tt(Q("zg", h), Q("zf", h), Q("ii", h), A.add)
         cp(Q("zo", h), Q("zg", h))
         zn = Hf("zn%d" % t, h)
         act(zn, IND(X("zz%d" % t), Q("zo", h)), F.Copy)
         cp(Hf("VO%d" % t, h), IND(X("idW"), Q("VN%d" % t, h)))
-        mms([(Hf("pM", 2 + h), X("M1"), Hf("Pb", h))])
-        tt(Hf("no", h), Hf("pM", 2 + h), Hf("VO%d" % t, h), A.mult)
+        mms([(Hf("pN", 2 + h), X("M1"), Hf("Pb", h))])
+        tt(Hf("no", h), Hf("pN", 2 + h), Hf("VO%d" % t, h), A.mult)
         if t < 3:
             send([(Hf("zz%d" % (t + 1), h), zn, "az%d%d" % (t + 1, h)), (Hf("VB%d" % (t + 1), h), Hf("VO%d" % t, h), "av%d%d" % (t + 1, h))])
         else:
             dmas("Y", "yz%d" % h, [(T.yz[:, 128 * h:128 * h + 128], zn)], 32768)
             cp(Q("yvS", h), Q("vc", h))
-        place(Q("offR", h), Q("pN", 40 + h), Q("o2", h), Q("trS", h))
+        place(Q("offR", h), Q("pM", 58 + h), Q("o2", h), Q("trS", h))
         tt(IND(X("nbS" if t < 3 else "yn", 0, WT), Q("offR", h)), Hf("no", h), Hf("A1", h), A.add)
 
     cp(X("VB0"), IND(X("idW"), X("VL0")))
@@ -618,19 +638,17 @@ def rank_program(g, core, T, topo):
         if last:
             act(X("yn", 0, W), X("nbS", 0, W), F.Copy, bias=OFF)
         for h in range(2):
-            lift[0] = FIRST * (1 - h)
             level(t, h)
             candidates(t, h)
             mms([(X("pD%d" % h, 0, NK), one, X("TH"))], stop=False)
-        lift[0] = FIRST
-        mms([(X("pM", 256, 512), X("M1"), X("Pb"))])
-        tt(X("co"), X("pM", 256, 512), X("con"), A.mult)
-        mms([(X("pM", 0, 16), X("ZFa", 15 - r, 143 - r), X("co", r, 256, 16)) for r in range(16)])
-        ts(X("TLu"), X("pM", 0, 16), OFF, A.add)
+        mms([(X("pM", 0, 256), X("M1"), X("Pb"))])
+        tt(X("co"), X("pM", 0, 256), X("con"), A.mult)
+        mms([(X("pM", 432, 448), X("ZFa", 15 - r, 143 - r), X("co", r, 256, 16)) for r in range(16)])
+        ts(X("TLu"), X("pM", 432, 448), OFF, A.add)
         tt(X("d0"), ind_x(X("TLu")), X(zz, 0, 256), A.subtract)
         act(X("d0"), X("d0"), F.Abs)
         for h in range(2):
-            mms([(X("pD%d" % h, 16, NK, SEG), Hf("d0", h), X("b8"))], start=False, part="D%d%d" % (t, h))
+            mms([(X("pD%d" % h, 16, NK, SEG), Hf("d0", h), X("b8n"))], start=False, part="D%d%d" % (t, h))
         mms([(X("pN", 256, 512), X("I16"), X("con")), (X("pN", 256, 512), X("N16"), X("co"))])
         if last:
             act(X("A1"), X("pN", 256, 512), F.Copy, bias=OFF)
@@ -640,24 +658,23 @@ def rank_program(g, core, T, topo):
             ts(erow(q), X("VB%d" % t, 16 * q, 256), X("vS", q, q + 1), A.is_equal)
         diag = (T.E[:, :, 0:16], "E", 0, 4096, 256)
         tt(diag, diag, tri, A.mult)
-        lift[0] = 0.0
         if not last:
+            act(X("xi"), X("dz"), F.Copy, bias=191.75, scale=0.5)
+            mms([(X("pN", 256, 512), X("D0"), X("xi")), (X("pN", 256, 512), X("D0"), X(zz, 0, 256))])
+            act(X("xn"), X("pN", 256, 512), F.Copy, bias=-192.0)
             mms([(X("pN", 16 * q, 256, p=8), X("b8"), erow(q)) for q in range(16)])
             scp(X("cb", p=8), X("pN", 0, 256, p=8))
-            to_list(X("pN", 336, 352), "cb", 0, 256, X("vS"))
-            place(X("offA"), X("pN", 336, 352), X("o3"), X("trS"))
-            act(X("xi"), X("dz"), F.Copy, bias=191.75, scale=0.5)
-            mms([(X("pM", 256, 512), X("D0"), X("xi")), (X("pM", 256, 512), X("D0"), X(zz, 0, 256))])
-            act(X("xn"), X("pM", 256, 512), F.Copy, bias=-192.0)
+            to_list(X("pM", 448, 464), "cb", 0, 256, X("vS"))
+            place(X("offA"), X("pM", 448, 464), X("o3"), X("trS"))
         for h in range(2):
-            lift[0] = FIRST * (1 - h)
             keys(t, h)
             distances(t, h)
+        for h in range(2):
             best(t, h)
         if not last:
             cp(IND(X("xdS", 0, WT), X("offA")), X("xn"))
-            mms([(X("pM", 32, 33), X("on32"), X("hs", 2 * t + h, 2 * t + h + 1)) for h in range(2)])
-            ts(X("hi0", t, t + 1), X("pM", 32, 33), -0.5, A.mult, 1024.0, A.add)
+            mms([(X("pM", 496, 497), X("on32"), X("hs", 2 * t + h, 2 * t + h + 1)) for h in range(2)])
+            ts(X("hi0", t, t + 1), X("pM", 496, 497), -0.5, A.mult, 1024.0, A.add)
             ts(X("hi1", t, t + 1), X("hi0", t, t + 1), 15, A.bitwise_and)
             tt(X("Hc", t, t + 1), X("hi1", t, t + 1), X("thF", 0, 1), A.add)
             ts(X("TH", 16, NK, SEG), X("b80"), X("Hc", t, t + 1), A.mult)

@@ -9,36 +9,34 @@ U = 4096.0
 BIG = 128 * U
 SEG = 34
 NK = 8 * SEG
-ON_SCALAR = (7, 3)
-CYCLE, GATHER, SCATTER, HOP, DMA_LAG, DMA_RATE, WAY = 0.83, 1.3, 3.1, 280.0, 2500.0, 350.0, 4000.0
-PASSES, SHAKE, SEED, BANK, EARLY = 60, 1500.0, 1, 200.0, 1
-PLAN = []
+ON_SCALAR = (6, 4)
 LOADS = "n0 n1 pv pz xa xb n2 n3 n4 th"
+CYCLE, GATHER, SCATTER, HOP, BANK, DMA_LAG, DMA_RATE, WAY = 0.83, 1.3, 3.1, 280.0, 200.0, 2500.0, 350.0, 3500.0
+PASSES, SHAKE, SPAN, SEED, EARLY = 600, 1500.0, 4000.0, 1, 1
+PLAN = []
 
 SCRATCH = {
     "nbI": ("sbuf", [128, W], "int32"), "nbS": ("sbuf", [128, WT], "float32"), "xdS": ("sbuf", [128, WT], "bfloat16"),
     "idW": ("sbuf", [128, W], "float32"), "yn": ("sbuf", [128, WT], "float32"),
-    "E": ("sbuf", [128, 16, 256], "bfloat16"), "TRI": ("sbuf", [128, 16, 16], "bfloat16"),
     "px0": ("psum", [128, 16, 32], "float32"), "px1": ("psum", [128, 16, 32], "float32"),
 }
 PART = {}
 
 
 def _decl():
-    for names, cols, d in (("mk", 4096, "float16"), ("dd xg", 8192, "bfloat16"),
-                           ("zz0 zz1 zz2 zz3 z40 z41 m40 m41", 512, "bfloat16"),
-                           ("dz far Pb xi xn d0 cb crb zn0 zn1 zn2 zn3 ta tb tc", 256, "bfloat16"),
-                           ("VB0 VB1 VB2 VB3 VO0 VO1 VO2 VO3 con co", 256, "float16"),
-                           ("TT A1 no Vm rr", 256, "float32"), ("Tt", 256, "uint16"), ("cU", 512, "uint16"),
-                           ("WP TH RST ones", NK, "bfloat16"), ("sc0 sc1 R0 R1", NK, "float32"), ("w34 k34 t34 u34", SEG, "float32"),
-                           ("VL0 VL1 VL2 VL3 VN0 VN1 VN2 VN3 TLu offA offR zo", 16, "uint16"), ("Lg LP LL", 8, "uint16"),
-                           ("vS o2 o3 yvS ii trS zf zg", 16, "float32"), ("pvI vi vc pr", 16, "int32"), ("sg", 16, "bfloat16"),
-                           ("thI", 2, "int32"), ("thF", 2, "float32"), ("Hc", 4, "float32"), ("hs", 8, "float32"),
-                           ("hi0 hi1", 4, "int32"), ("pI pB iI", 8, "int32"), ("pC", 32, "float32"), ("iF", 8, "float32"),
-                           ("ZZ ZB", 144, "bfloat16"), ("ZFe ZFo ZFa", 144, "float16"),
-                           ("BLK D0 D1 D2 CA CB D0n mt M1 M2 M2a In LT NEG Sp Sm LQ crc", 128, "bfloat16"),
-                           ("I16 N16 W00 W01 W10 W11", 128, "float16"), ("I32 MD on32", 128, "float32"), ("CMP", 64, "float32"),
-                           ("b8 b80 b8n b8p b8m", 8, "bfloat16"), ("b8h r15", 8, "float16"), ("b8f", 8, "float32"), ("SelP", 16, "float16")):
+    for names, cols, d in (("mk", 4096, "float16"), ("dd xg", 8192, "bfloat16"), ("SB E0 E1 E2 E3 EO0 EO1 EO2", W, "bfloat16"),
+                           ("zz0 zz1 zz2 zz3 z40 z41 m40 m41 far", 512, "bfloat16"),
+                           ("LOW dz Pb xi xn d0 hb zn0 zn1 zn2 zn3 FE FO ohS ta tb", 256, "bfloat16"), ("con co", 256, "float16"),
+                           ("TT A1 no Vm Wm Wa", 256, "float32"), ("Tt", 256, "uint16"), ("cU", 512, "uint16"),
+                           ("WP WH TH RST ones", NK, "bfloat16"), ("sc0 sc1 R0 R1", NK, "float32"), ("w34 k34 t34 u34 h34", SEG, "float32"),
+                           ("VL0 VL1 VL2 VL3 VN0 VN1 VN2 VN3 OA0 OA1 OA2 OO0 OO1 TLu offR zo", 16, "uint16"), ("Lg LP Lq", 8, "uint16"),
+                           ("vI0 vI1 vI2 vI3 vO0 vO1 vO2 uo ua yvS ii zf zg", 16, "float32"), ("pvI vi vc", 16, "int32"),
+                           ("thI", 2, "int32"), ("thF", 2, "float32"), ("Hc", 4, "float32"), ("hs iF b8f", 8, "float32"),
+                           ("hi0 hi1", 4, "int32"), ("pI pB iI", 8, "int32"), ("pC", 32, "float32"), ("sg12 pw12", 12, "float32"),
+                           ("ZZ", 144, "bfloat16"), ("ZFe ZFo ZFa", 144, "float16"),
+                           ("BLK D0 D1 D2 CA CB D0n mt M1 M2 M2a In LT Sp Sm tc", 128, "bfloat16"),
+                           ("I16 N16 W00 W01 W10 W11", 128, "float16"), ("I32 MD on32 rr", 128, "float32"),
+                           ("b8 b80 b8n b8p b8m wv", 8, "bfloat16"), ("rep", 16, "bfloat16"), ("b8h r15", 8, "float16"), ("SelP", 16, "float16")):
         for n in names.split():
             if cols > 32:
                 SCRATCH[n] = ("sbuf", [128, cols], d)
@@ -52,9 +50,10 @@ def _decl():
 
 
 _decl()
-DMAS = ["pv", "pz", "th", "xa", "xb", "n0", "n1", "n2", "n3", "n4", "y0", "y1", "y2", "y3", "yv", "yz0", "yz1"]
-SEMAPHORES = (["sV", "sS", "sP", "sG", "loc"] + ["d_" + d for d in DMAS] + ["d_z%d%d" % (t, h) for t in range(4) for h in range(2)]
-              + ["a%s%d%d" % (n, t, h) for n in "lzv" for t in range(1, 4) for h in range(2)])
+DMAS = LOADS.split() + ["y0", "y1", "y2", "y3", "yv", "yz0", "yz1"] + ["z%d%d" % (t, h) for t in range(4) for h in range(2)]
+SEMAPHORES = (["sV", "sS", "sP", "sG", "loc"] + ["d_" + d for d in DMAS]
+              + ["a%s%d%d" % (n, t, h) for n in "lz" for t in range(1, 4) for h in range(2)]
+              + ["ae%d%d" % (t, b) for t in range(1, 4) for b in range(3)] + ["av1", "av2", "av3", "ao1", "ao2"])
 
 
 def rank_program(g, core, T, topo):
@@ -175,15 +174,21 @@ def rank_program(g, core, T, topo):
         key = list(range(n))
         best = None
         shake = np.random.default_rng(SEED)
+        hop = lambda a, b: 0.0 if calls[a]["uses"][0] == calls[b]["uses"][0] == "P" else HOP
         for k in range(PASSES):
-            fw = place_calls(lambda j: key[j], deps, users, lambda a, b: calls[a]["lag"] + HOP)
+            fw = place_calls(lambda j: key[j], deps, users, lambda a, b: calls[a]["lag"] + hop(a, b))
             end = max(fw[j] + calls[j]["ns"] for j in range(n))
-            if best is None or end < best[0]:
+            if best is None or end <= best[0]:
                 best = (end, fw)
-            src, amp = (best[1], SHAKE) if k % 3 == 2 else (fw, 0.0)
-            late = [-(src[j] + calls[j]["ns"]) + amp * float(u) for j, u in enumerate(shake.random(n))]
-            bw = place_calls(lambda j: late[j], users, deps, lambda a, b: calls[b]["lag"] + HOP)
-            key = [-(bw[j] + calls[j]["ns"]) for j in range(n)]
+            u, mid = shake.random(n), best[0] * float(shake.random())
+            src = fw if k < 4 else best[1]
+            near = [SHAKE * float(u[j]) if k >= 4 and abs(src[j] - mid) < SPAN else 0.0 for j in range(n)]
+            if k % 2 and k >= 4:
+                key = [src[j] + near[j] for j in range(n)]
+            else:
+                late = [-(src[j] + calls[j]["ns"]) + near[j] for j in range(n)]
+                bw = place_calls(lambda j: late[j], users, deps, lambda a, b: calls[b]["lag"] + hop(a, b))
+                key = [-(bw[j] + calls[j]["ns"]) for j in range(n)]
         PLAN.extend(sorted(range(n), key=lambda j: (best[1][j], j)))
         return PLAN
 
@@ -220,14 +225,20 @@ def rank_program(g, core, T, topo):
                 note(q, x[1], x[2], x[3], s, c, True)
         call(q, run, reads, writes, t)
 
-    def X(n, a=0, b=None, st=1, p=128):
+    def X(n, a=0, b=None, st=1):
         home, at, cols = PART[n] if n in PART else (n, 0, SCRATCH[n][1][1])
         if b is None:
             b = cols
-        return (T[home][0:p, at + a:at + b:st] if st > 1 else T[home][0:p, at + a:at + b], n, a, b, len(range(a, b, st)))
+        return (T[home][:, at + a:at + b:st] if st > 1 else T[home][:, at + a:at + b], n, a, b, len(range(a, b, st)))
 
     def PX(n, a, b, c0=0, c1=32):
         return (T["px%d" % n][:, a:b, c0:c1], "px%d" % n, 32 * a, 32 * b, (b - a) * (c1 - c0))
+
+    def Hf(n, h):
+        return X(n, 128 * h, 128 * h + 128)
+
+    def Q(n, h):
+        return X(n, 8 * h, 8 * h + 8)
 
     def IND(win, off):
         return (win[0].indirect(off[0]), win, off)
@@ -354,44 +365,42 @@ def rank_program(g, core, T, topo):
         calls[-2].update({"run": lambda: None, "uses": [name], "lag": 0.0})
         calls[-1].update({"ns": done, "uses": [name]})
 
-    def replicate(t, h):
-        src = X("zz%d" % t, 128 * h, 128 * h + 128)
-        dmas("Y", "z%d%d" % (t, h), [(X("z4%d" % h, 128 * c, 128 * c + 128), src) for c in range(4)], 4 * 32768)
-
     pc = lambda j: X("pC", j, j + 1)
     one = X("ones", 0, 128)
     iota(X("pI", 0, 1), [[1, 1]], 0, 1)
     fill(X("ones"), 1.0)
     fill(X("on32"), 1.0)
     fill(X("RST"), 1.0)
-    fill(X("tc", 0, 144), U)
     fill(X("RST", 0, NK, SEG), 0.0)
+    fill(X("tc"), -2.0)
     fill(pc(19), -1.0)
-    fill(pc(20), 1.0)
-    fill(pc(21), -60.0 * U)
+    fill(pc(24), -11.0)
     sel(X("ta", 0, 128), one, [[-16, 8], [0, 16]], A.is_ge, 0, 1)
     sel(X("BLK"), X("ta", 0, 128), [[16, 8], [0, 16]], A.is_ge, 15, -1)
     sel(X("ta", 128, 256), X("BLK"), [[1, 128]], A.is_ge, 0, -1)
     sel(X("LT"), X("ta", 128, 256), [[0, 8], [-1, 16]], A.is_ge, 14, 0)
-    for n, b in (("D0", 0), ("D2", 2), ("CA", -15), ("CB", -14), ("D1", 1)):
+    sel(X("CB"), X("BLK"), [[1, 128]], A.is_ge, -2, -1)
+    for n, b in (("D0", 0), ("CA", -15), ("D1", 1)):
         sel(X(n), X("BLK"), [[-1, 128]], A.is_equal, b, 1)
     sel(X("Sp"), one, [[-1, 128]], A.is_equal, 16, 1)
     sel(X("Sm"), one, [[-1, 128]], A.is_equal, -16, 1)
-    sel(X("ZB", p=8), X("tc", 0, 144, p=8), [[1, 144]], A.is_equal, -15, -16)
     sel(X("ta", 0, 144), X("ones", 0, 144), [[-16, 9], [0, 16]], A.is_ge, 0, 1)
     sel(X("tb", 0, 144), X("ta", 0, 144), [[16, 9], [0, 16]], A.is_ge, 15, -1)
     sel(X("ZZ"), X("tb", 0, 144), [[0, 9], [1, 16]], A.is_equal, -15, 0)
-    iota(X("rr"), [[0, 16], [1, 16]], 0, 0)
+    for c in range(2):
+        sel(Hf("LOW", c), X("tc"), [[-1, 128]], A.is_ge, 0, 1)
+    iota(X("rr"), [[0, 8], [1, 16]], 0, 0)
     iota(X("iI"), [[SEG, 8]], SEG - 1, 0)
     iota(X("iF"), [[2, 8]], 0, 0)
     iota(X("ii"), [[16, 16]], 0, 0)
-    iota(X("w34"), [[-16, 2], [-1, 17]], 47, 0)
+    iota(X("w34"), [[-16, 2], [-1, 17]], 48 - 64, 0)
     iota(X("k34"), [[0, 2], [1, 17]], 0, 0)
     for j in range(4):
         iota(X("idW", 768 * j, 768 * j + 768), [[1, 768]], 768 * j - int(OFF), 0)
 
     ts(X("pI", 1, 2), X("pI", 0, 1), 15, A.bitwise_and)
     cp(pc(0), X("pI", 1, 2))
+    cp(pc(20), X("pI", 0, 1))
     for j, (sh, m) in enumerate(((0, 1), (0, 3), (2, 1), (3, 1), (4, 1))):
         ts(X("pB", j, j + 1), X("pI", 0, 1), sh, A.arith_shift_right, m, A.bitwise_and)
     cp(X("pC", 1, 6), X("pB", 0, 5))
@@ -405,14 +414,20 @@ def rank_program(g, core, T, topo):
     ts(X("In"), X("D0"), -1.0, A.mult)
     ts(X("D0n"), X("D0"), pc(9), A.mult)
     tt(X("mt"), X("CA"), X("D0n"), A.subtract)
-    tt(X("M2a"), X("D2"), X("CB"), A.add)
-    tt(X("M2"), X("M2a"), X("mt"), A.add)
     tt(X("M1"), X("D1"), X("mt"), A.add)
+    ts(X("M2a"), X("CB"), -256.0, A.mult)
+    cp(X("D2"), X("LT"))
+    fill(X("D2", 14, 128, 16), 0.0)
+    tt(X("M2"), X("M2a"), X("D2"), A.add)
+    ts(pc(28), pc(0), 14.0, A.is_ge, 400.0, A.mult)
+    ts(pc(27), pc(28), -200.0, A.add)
     for n, src, j in (("W00", "D0", 11), ("W11", "D0", 5), ("W01", "Sp", 11), ("W10", "Sm", 5)):
         ts(X(n), X(src), pc(j), A.mult)
     ts(pc(12), pc(2), 32.0, A.mult, pc(4), A.add)
     ts(pc(13), pc(3), 16.0, A.mult, pc(12), A.add)
     ts(X("LP"), X("iF"), pc(13), A.add)
+    ts(X("Lq"), X("iF"), 0.5, A.mult)
+    cp(X("Lg"), X("iI"))
     ts(X("ZFe"), X("ZZ"), pc(10), A.mult)
     ts(X("ZFo"), X("ZZ"), pc(1), A.mult)
     cp(X("ZFa"), X("ZZ"))
@@ -425,28 +440,18 @@ def rank_program(g, core, T, topo):
     ts(X("SelP", 1, 16, 2), X("b8"), pc(1), A.mult)
     ts(pc(14), pc(0), 0.0, A.is_equal, BIG, A.mult)
     ts(X("b80"), X("b8"), pc(14), A.mult)
-    ts(X("u34"), X("k34"), 0.0, A.mult, X("thF", 1, 2), A.add)
-    fill(X("u34", SEG - 1, SEG), 2.0)
-    for n in range(8):
-        ts(X("TH", SEG * n, SEG * n + SEG), X("u34"), X("b80", n, n + 1), A.mult)
-    ts(X("TH", 16, NK, SEG), X("b80"), X("thF", 0, 1), A.mult)
-    cp(X("I16"), X("D0"))
-    cp(X("N16"), X("In"))
-    cp(X("I32"), X("D0"))
     for n, v in (("b8n", -BIG), ("b8p", BIG), ("b8m", -2 * BIG)):
         ts(X(n), X("b8"), v, A.mult)
-    ts(X("MD"), X("rr", 0, 128), pc(0), A.is_equal)
-    tri = (T.TRI[:, :, :], "TRI", 0, 256, 256)
-    ts(X("ta"), X("rr"), pc(0), A.is_gt)
-    ts(X("tb"), X("rr"), pc(0), A.is_equal)
-    tt(tri, X("ta"), X("tb"), A.subtract)
-    cp(X("Lg"), X("iI"))
-    ts(X("LL"), X("iF"), pc(4), A.add)
-    ts(X("ii"), X("ii"), pc(0), A.add)
-    ts(X("trS"), X("ii"), W - U - OFF, A.add)
+    ts(X("u34"), X("k34"), 0.0, A.mult, X("thF", 1, 2), A.add)
+    fill(X("u34", 16, SEG, 17), 2.0)
+    fill(X("h34"), -0.5)
+    fill(X("h34", 16, 17), 0.5)
+    fill(X("h34", 33, 34), 0.0)
     for n in range(8):
-        ts(X("CMP", 8 * n, 8 * n + 8), X("b8"), -1.0e9, A.mult, 1.0e9 + 2 * U, A.add)
-    fill(X("w34", 16, 17), 64.0)
+        ts(X("TH", SEG * n, SEG * n + SEG), X("u34"), X("b80", n, n + 1), A.mult)
+        ts(X("WH", SEG * n, SEG * n + SEG), X("h34"), X("b80", n, n + 1), A.mult)
+    ts(X("Hc", 0, 1), X("thF", 0, 1), -0.5, A.add)
+    fill(X("w34", 16, 17), 2.0 - 64.0)
     fill(X("w34", 33, 34), 1.0)
     ts(pc(15), pc(9), -16.0, A.mult)
     ts(pc(16), pc(1), -2.0, A.mult, 1.0, A.add)
@@ -459,6 +464,24 @@ def rank_program(g, core, T, topo):
     ts(X("w34", 17, 33), X("w34", 17, 33), pc(18), A.add)
     for n in range(8):
         ts(X("WP", SEG * n, SEG * n + SEG), X("w34"), X("b8", n, n + 1), A.mult, U, A.mult)
+    cp(X("I16"), X("D0"))
+    cp(X("N16"), X("In"))
+    cp(X("I32"), X("D0"))
+    ts(X("MD"), X("rr"), pc(0), A.is_equal)
+    ts(X("ii"), X("ii"), pc(0), A.add)
+    for h in range(2):
+        ts(pc(21 + h), pc(20), W + 128 * h - U, A.add, 1.0 / U, A.mult)
+        ts(pc(25 + h), pc(20), W + 128 * h, A.add, 1.0 / U, A.mult)
+    ts(X("SB", 0, 1), pc(0), 12.0, A.is_lt, -1.0, A.mult)
+    for b in range(12):
+        ts(X("sg12", b, b + 1), pc(0), float(b), A.not_equal, 2.0, A.mult)
+        ts(X("pw12", b, b + 1), pc(0), float(b), A.is_equal, 2.0 ** (b - 1) / U, A.mult)
+    ts(X("sg12"), X("sg12"), -1.0, A.add)
+    for b in range(12):
+        n = min(2 ** b, W - 2 ** b)
+        ts(X("SB", 2 ** b, 2 ** b + n), X("SB", 0, n), X("sg12", b, b + 1), A.mult)
+    op("V", lambda e: e.tensor_reduce(pc(23)[0], X("pw12")[0], AxisListType.X, A.add), [X("pw12")], [pc(23)], 60.0)
+    ts(X("wv"), X("b8"), pc(23), A.mult)
     for j in range(5):
         a, b = PIECES[j], PIECES[j + 1]
         ts(X("nbS", a, b), X("nbI", a, b), -OFF, A.add)
@@ -466,33 +489,26 @@ def rank_program(g, core, T, topo):
     nxt = T.cores[(rank + 1) % len(T.cores)]
     prv = T.cores[(rank - 1) % len(T.cores)]
     adr = topo.addr(nxt)
-    eng = topo.engines(core, nxt)
-    ne = len(eng)
-    msk = lambda es: sum(1 << e for e in es)
+    ne = len(topo.engines(core, nxt))
     n_in = len(topo.engines(prv, core))
     loc = [0]
 
-    def send(items):
+    def send(dst, src, sem):
         def run():
             deps = {}
-            for dst, src, sem in items:
-                need("G", src[1], src[2], src[3], False, deps)
+            need("G", src[1], src[2], src[3], False, deps)
             waits("G", deps)
-            if len(items) == 1:
-                dst, src, sem = items[0]
-                g.remote_dma(dst[0], src[0], T.sem[sem], T.sem.loc, adr[1], adr[0], msk(eng[:ne]))
-            else:
-                m = ne // len(items)
-                g.remote_dma_fused([RemoteDMATransfer(dst_ids=[DstId(rid=adr[0], pnc=adr[1])], dma_engine_mask=msk(eng[m * j:m * j + m]),
-                                                      remote_sem=T.sem[sem], src=src[0], dst=dst[0])
-                                    for j, (dst, src, sem) in enumerate(items)], local_sem=T.sem.loc)
+            g.remote_dma(dst[0], src[0], T.sem[sem], T.sem.loc, adr[1], adr[0], topo.mask(core, nxt))
             loc[0] += ne
-        call("G", run, [it[1] for it in items], [it[0] for it in items], 150.0, lag=WAY)
+        call("G", run, [src], [dst], 150.0, lag=WAY)
 
     for t in range(1, 4):
         rec["VL%d" % t] = [(8 * h, 8 * h + 8, "R", "al%d%d" % (t, h), n_in, True) for h in range(2)]
-        rec["VB%d" % t] = [(128 * h, 128 * h + 128, "R", "av%d%d" % (t, h), n_in // 2, True) for h in range(2)]
-        rec["zz%d" % t] = [(128 * h, 128 * h + 128, "R", "az%d%d" % (t, h), n_in // 2, True) for h in range(2)]
+        rec["zz%d" % t] = [(128 * h, 128 * h + 128, "R", "az%d%d" % (t, h), n_in, True) for h in range(2)]
+        rec["E%d" % t] = [(1024 * b, 1024 * b + 1024, "R", "ae%d%d" % (t, b), n_in, True) for b in range(3)]
+        rec["vI%d" % t] = [(0, 16, "R", "av%d" % t, n_in, True)]
+        if t < 3:
+            rec["OA%d" % t] = [(0, 16, "R", "ao%d" % t, n_in, True)]
 
     def ind_x(off):
         return IND(X("xdS", 0, W), off)
@@ -500,24 +516,22 @@ def rank_program(g, core, T, topo):
     def ind_n(off):
         return IND(X("nbS", 0, W), off)
 
-    def Hf(n, h, p=128):
-        return X(n, 128 * h, 128 * h + 128, p=p)
-
-    def Q(n, h):
-        return X(n, 8 * h, 8 * h + 8)
+    def spare(h):
+        return X("pM", 272, 400) if h else PX(0, 12, 16)
 
     def level(t, h):
-        replicate(t, h)
-        tt(Hf("dz", h), ind_x(Q("VL%d" % t, h)), Hf("zz%d" % t, h), A.subtract)
-        adz = Hf("zz%d" % t, 2 + h)
-        act(adz, Hf("dz", h), F.Abs)
-        act(Hf("far", h), adz, F.Relu, bias=pc(19))
-        mms([(Hf("pM", h), X("LT"), Hf("far", h))])
-        act(Hf("Pb", h), Hf("pM", h), F.Relu, bias=pc(7), scale=-1.0)
-        ps = "pN" if h else "pS0"
-        for c in range(4):
-            mms([(Hf(ps, c), X("M2"), Hf("Pb", h))])
-        scp(X("m4%d" % h), X(ps))
+        z = Hf("zz%d" % t, h)
+        dmas("Y", "z%d%d" % (t, h), [(Hf("z4%d" % h, c), z) for c in range(4)], 4 * 32768)
+        tt(Hf("dz", h), ind_x(Q("VL%d" % t, h)), z, A.subtract)
+        far = [Hf("far", 2 * h + s) for s in range(2)]
+        for s in range(2):
+            act(far[s], Hf("dz", h), F.Relu, bias=pc(19), scale=1.0 - 2 * s)
+        ps = "pS%d" % h
+        mms([(Hf(ps, c), X("M2"), f) for c in range(4) for f in far])
+        act(X("m4%d" % h), X(ps), F.Sigmoid, bias=pc(27), scale=400.0)
+        mms([(spare(h), X("LT"), f) for f in far])
+        act(Hf("Pb", h), spare(h), F.Relu, bias=pc(7), scale=-1.0)
+        act(Hf("zz%d" % t, 2 + h), Hf("dz", h), F.Abs)
 
     def ccols(h, kh, par, a=0, b=64):
         c = 256 * h + 128 * kh + 64 * par
@@ -534,7 +548,6 @@ def rank_program(g, core, T, topo):
         src, dst = PX(1 - h, 0, 4), Hf("TT", h)
         op("V", lambda e: e.transpose(dst[0], src[0]), [src], [dst], ns(dst, src))
         ts(Hf("Tt", h), IND(Hf("TT", h), X("LP")), OFF, A.add)
-        ts(Q("vS", h), Q("VL%d" % t, h), -OFF, A.add)
         for kh in range(2):
             s = 2048 * h + 1024 * kh
             for c in range(2):
@@ -551,9 +564,27 @@ def rank_program(g, core, T, topo):
             if h or kh:
                 ts(ccols(h, kh, 0, 0, 128), PX(kh, 4 + 4 * kh, 8 + 4 * kh), OFF, A.add)
 
-    def keys(t, h):
-        mms([(X("pM", 0, NK), Hf("Pb", h), X("WP"))]
-            + [(X("pM", k, NK, 17), X("mk", 2048 * h + 128 * k, 2048 * h + 128 * k + 128), X("SelP")) for k in range(16)]
+    def own(t, h):
+        ps = spare(h)
+        mms([(ps, X("M1"), Hf("Pb", h))])
+        tt(Hf("co", h), ps, Hf("con", h), A.mult)
+        scp(Hf("ohS", h), ps)
+        mms([(Q("pM", 54 + h), X("ZFa", 15 - r, 143 - r), X("co", 128 * h + r, 128 * h + 128, 16)) for r in range(16)])
+        ts(Q("TLu", h), Q("pM", 54 + h), OFF, A.add)
+        tt(Hf("d0", h), ind_x(Q("TLu", h)), Hf("zz%d" % t, h), A.subtract)
+        act(Hf("d0", h), Hf("d0", h), F.Abs)
+        mms([(ps, X("BLK"), Hf("d0", h))])
+        act(Hf("hb", h), ps, F.Sign, bias=X("Hc", t, t + 1), scale=-1.0, acc=X("hs", 2 * t + h, 2 * t + h + 1))
+        mms([(ps, X("I16"), Hf("con", h)), (ps, X("N16"), Hf("co", h))])
+        act(Hf("A1", h), ps, F.Copy, bias=OFF if t == 3 else 0.0)
+        if t < 3:
+            act(Hf("xi", h), Hf("dz", h), F.Copy, bias=191.75, scale=0.5)
+            mms([(ps, X("D0"), Hf("xi", h)), (ps, X("D0"), Hf("zz%d" % t, h))])
+            act(Hf("xn", h), ps, F.Copy, bias=-192.0)
+
+    def keys(h):
+        mms([(X("pM", 0, NK), Hf("Pb", h), X("WP")), (X("pM", 0, NK), Hf("hb", h), X("WH"))]
+            + [(X("pM", k, NK, 17), Hf("mk", 16 * h + k), X("SelP")) for k in range(16)]
             + [(X("pM", 16, NK, SEG), Hf("co", h), X("b8h")), (X("pM", 33, NK, SEG), Hf("con", h), X("r15"))])
         scp(X("R%d" % h), X("pM", 0, NK))
 
@@ -566,11 +597,12 @@ def rank_program(g, core, T, topo):
             dd = X("dd", a, a + 512)
             src = ind_x(ccols(h, kh, par, 32 * s, 32 * s + 32))
             if n < ON_SCALAR[h]:
-                ps = X("pS%d" % (turn[0] % 2))
+                ps = ("pS0", "pS1", "pN")[turn[0] % 3]
                 turn[0] += 1
                 act(X("xg", a, a + 512), src, F.Copy)
-                mms([(ps, X("In"), X("z4%d" % h)), (ps, X("D0"), X("xg", a, a + 512))])
-                act(dd, ps, F.Abs)
+                mms([(Hf(ps, k), X("In"), Hf("zz%d" % t, h)) for k in range(4)], stop=False)
+                mms([(X(ps), X("D0"), X("xg", a, a + 512))], start=False)
+                act(dd, X(ps), F.Abs)
                 terms = (("dd", "b8n"),)
             else:
                 tt(dd, src, X("z4%d" % h), A.subtract)
@@ -580,111 +612,108 @@ def rank_program(g, core, T, topo):
                 mms([(X("pD%d" % h, 17 * par + 8 * kh + 4 * s + k, NK, SEG), X(name, a + 128 * k, a + 128 * k + 128), X(w)) for k in range(4)],
                     start=False, part="D%d%d" % (t, h))
 
-    def erow(q):
-        return (T.E[:, q, 0:256 - 16 * q], "E", 256 * q, 240 * q + 256, 256 - 16 * q)
+    def eb(E, b, n):
+        return Hf(E, 8 + 4 * (n // 2) + 2 * (b - 1) + n % 2 if b else n)
 
-    def to_list(out, src, a, b, vs):
-        mms([(out, X("I32"), vs)] + [(out, X("ZB", 15 - r, 143 - r, p=8), X(src, a + r, b, 16, p=8)) for r in range(16)])
+    def to_list(out, tmp, src):
+        tt(tmp, src, X("MD"), A.mult)
+        mms([(out, tmp, X("b8f"))])
 
-    def place(out, ps, tmp, tr):
-        tt(tmp, ps, tr, A.min)
-        ts(out, tmp, U + OFF, A.add)
+    def pairs(t, VL, E, vI, OA):
+        for h in range(2):
+            for F2, j in (("FE", 11), ("FO", 5)):
+                act(Hf(F2, h), IND(X("SB"), Q(VL, h)), F.Copy, scale=pc(j))
+            mms([(Q("pM", 62 + h), Hf(F2, h), X("wv")) for F2 in ("FE", "FO")])
+            act(Q(vI, h), Q("pM", 62 + h), F.Copy, bias=(U - 1) / 2 / U)
+        for blocks in (((0, 0),), ((0, 1), (1, 1))):
+            for a in range(4):
+                ps, w = ("pN", "pS1")[a % 2], 256 * len(blocks)
+                part = lambda F2, h: (T[F2][32 * a:32 * a + 32, 128 * h:128 * h + 128], F2, 128 * h, 128 * h + 128, 128)
+                mms([(X(ps, w - 256, w), X("D0"), X("LOW"))]
+                    + [(Hf(ps, 2 * k + m), part(F2, ha), part(F2, hb)) for k, (ha, hb) in enumerate(blocks) for m, F2 in enumerate(("FE", "FO"))])
+                at = 1024 * (len(blocks) - 1) + w * a
+                act(X(E, at, at + w), X(ps, 0, w), F.Relu, bias=pc(24))
+                if t and (at + w) % 1024 == 0:
+                    send(X("E%d" % t, at + w - 1024, at + w), X(E, at + w - 1024, at + w), "ae%d%d" % (t, at // 1024))
+        if t:
+            send(X("vI%d" % t), X(vI), "av%d" % t)
+        if t < 3:
+            for h in range(2):
+                mms([(Q("pM", 52 + h), X("I32"), Q(vI, h))]
+                    + [(X("pM", 416 + 8 * h + n, 417 + 8 * h + n), eb(E, b, n), X("ones", 0, 1)) for b in ((0,), (1, 2))[h] for n in range(8)])
+                ts(Q("ua", h), Q("pM", 52 + h), pc(25 + h), A.min, U, A.mult)
+                to_list(Q("pM", 56 + h), Hf("Wa", h), IND(Q("ua", h), X("Lq")))
+            cp(X(OA), X("pM", 448, 464))
+            if t:
+                send(X("OA%d" % t), X(OA), "ao%d" % t)
 
     def best(t, h):
         sc, pk = X("sc%d" % h), X("R%d" % h)
         tt(pk, X("pD%d" % h, 0, NK), pk, A.min)
         op("V", lambda e: e.tensor_tensor_scan(sc[0], T.RST[:, :], pk[0], 0.0, A.mult, A.max), [X("RST"), pk], [sc], ns(sc, pk))
-        tt(Hf("Vm", h), IND(sc, X("Lg")), X("MD"), A.mult)
+        ts(Q("rep", h), X("sc%d" % h, SEG - 1, NK, SEG), 3 * U - OFF, A.is_ge)
+        E, u = "E%d" % t, Q("pD0", 35 + h)
+        count = lambda b, ha, hb: [(X("pD0", 280 + 8 * hb + n, 281 + 8 * hb + n), eb(E, b, n), X("rep", 8 * ha + n, 8 * ha + n + 1)) for n in range(8)]
+        if h == 0:
+            mms([(u, X("I32"), Q("vI%d" % t, 0)), (u, X("In"), Q("rep", 0))] + count(0, 0, 0))
+        else:
+            mms([(u, X("In"), Q("rep", 1))] + count(2, 1, 1), start=False)
+        ts(Q("uo", h), u, pc(21 + h), A.min, U, A.mult)
+        if h == 0:
+            mms([(Q("pD0", 36), X("I32"), Q("vI%d" % t, 1))] + count(1, 0, 1), stop=False)
+            calls[-1]["deps"].add(len(calls) - 2)
+        to_list(Q("pM", 58 + h), Hf("Wm", h), IND(Q("uo", h), X("Lq")))
+        ts(Q("offR", h), Q("pM", 58 + h), U, A.add)
         val = Q("pM", 60 + h)
-        mms([(val, Hf("Vm", h), X("b8f"))])
+        to_list(val, Hf("Vm", h), IND(sc, X("Lg")))
         ts(Q("vi", h), val, OFF, A.add)
-        act(Q("sg", h), val, F.Sign, bias=pc(21), acc=X("hs", 2 * t + h, 2 * t + h + 1))
         ts(Q("vc", h), Q("vi", h), int(U) - 1, A.bitwise_and)
-        ts(Q("pr", h), Q("vi", h), 63 * int(U), A.bitwise_and)
         cp(Q("VN%d" % t, h), Q("vc", h))
         if t < 3:
-            send([(Q("VL%d" % (t + 1), h), Q("VN%d" % t, h), "al%d%d" % (t + 1, h))])
-        tt(X("LQ", 64 * h, 64 * h + 64), IND(Q("pr", h), X("LL", 0, 4)), X("CMP"), A.is_ge)
-        lq = lambda q: X("LQ", 8 * q, 8 * q + 8)
-        if h == 0:
-            mms([(X("pN", 16 * q, 256, p=8), lq(q), erow(q)) for q in range(8)])
-            scp(X("crb", p=8), X("pN", 0, 256, p=8))
-            to_list(Q("pM", 58), "crb", 0, 128, Q("vS", 0))
-        else:
-            mms([(X("pN", 0, 128, p=8), X("D0", 0, 8, p=8), Hf("crb", 1, p=8))]
-                + [(X("pN", 16 * q - 128, 128, p=8), lq(q), erow(q)) for q in range(8, 16)])
-            scp(X("crc", p=8), X("pN", 0, 128, p=8))
-            to_list(Q("pM", 59), "crc", 0, 128, Q("vS", 1))
-        ts(Q("zf", h), Q("pr", h), U, A.is_equal, 256.0, A.mult)
+            send(Q("VL%d" % (t + 1), h), Q("VN%d" % t, h), "al%d%d" % (t + 1, h))
+        ts(Q("zf", h), Q("vi", h), 2 * U, A.is_lt, 256.0, A.mult)
         tt(Q("zg", h), Q("zf", h), Q("ii", h), A.add)
         cp(Q("zo", h), Q("zg", h))
         zn = Hf("zn%d" % t, h)
         act(zn, IND(X("zz%d" % t), Q("zo", h)), F.Copy)
-        cp(Hf("VO%d" % t, h), IND(X("idW"), Q("VN%d" % t, h)))
-        mms([(Hf("pN", 2 + h), X("M1"), Hf("Pb", h))])
-        tt(Hf("no", h), Hf("pN", 2 + h), Hf("VO%d" % t, h), A.mult)
         if t < 3:
-            send([(Hf("zz%d" % (t + 1), h), zn, "az%d%d" % (t + 1, h)), (Hf("VB%d" % (t + 1), h), Hf("VO%d" % t, h), "av%d%d" % (t + 1, h))])
+            send(Hf("zz%d" % (t + 1), h), zn, "az%d%d" % (t + 1, h))
         else:
             dmas("Y", "yz%d" % h, [(T.yz[:, 128 * h:128 * h + 128], zn)], 32768)
             cp(Q("yvS", h), Q("vc", h))
-        place(Q("offR", h), Q("pM", 58 + h), Q("o2", h), Q("trS", h))
+        tt(Hf("no", h), IND(X("idW"), Q("VN%d" % t, h)), Hf("ohS", h), A.mult)
         tt(IND(X("nbS" if t < 3 else "yn", 0, WT), Q("offR", h)), Hf("no", h), Hf("A1", h), A.add)
 
-    cp(X("VB0"), IND(X("idW"), X("VL0")))
+    pairs(0, "VL0", "E0", "vI0", "OA0")
     for t in range(4):
-        zz = "zz%d" % t
         last = t == 3
         if last:
             act(X("yn", 0, W), X("nbS", 0, W), F.Copy, bias=OFF)
         for h in range(2):
             level(t, h)
             candidates(t, h)
-            mms([(X("pD%d" % h, 0, NK), one, X("TH"))], stop=False)
-        mms([(X("pM", 0, 256), X("M1"), X("Pb"))])
-        tt(X("co"), X("pM", 0, 256), X("con"), A.mult)
-        mms([(X("pM", 432, 448), X("ZFa", 15 - r, 143 - r), X("co", r, 256, 16)) for r in range(16)])
-        ts(X("TLu"), X("pM", 432, 448), OFF, A.add)
-        tt(X("d0"), ind_x(X("TLu")), X(zz, 0, 256), A.subtract)
-        act(X("d0"), X("d0"), F.Abs)
-        for h in range(2):
-            mms([(X("pD%d" % h, 16, NK, SEG), Hf("d0", h), X("b8n"))], start=False, part="D%d%d" % (t, h))
-        mms([(X("pN", 256, 512), X("I16"), X("con")), (X("pN", 256, 512), X("N16"), X("co"))])
-        if last:
-            act(X("A1"), X("pN", 256, 512), F.Copy, bias=OFF)
-        else:
-            scp(X("A1"), X("pN", 256, 512))
-        for q in range(16):
-            ts(erow(q), X("VB%d" % t, 16 * q, 256), X("vS", q, q + 1), A.is_equal)
-        diag = (T.E[:, :, 0:16], "E", 0, 4096, 256)
-        tt(diag, diag, tri, A.mult)
+            mms([(X("pD%d" % h, 0, NK)[:3] + (512, NK), one, X("TH"))], stop=False)
+            own(t, h)
+            keys(h)
         if not last:
-            act(X("xi"), X("dz"), F.Copy, bias=191.75, scale=0.5)
-            mms([(X("pN", 256, 512), X("D0"), X("xi")), (X("pN", 256, 512), X("D0"), X(zz, 0, 256))])
-            act(X("xn"), X("pN", 256, 512), F.Copy, bias=-192.0)
-            mms([(X("pN", 16 * q, 256, p=8), X("b8"), erow(q)) for q in range(16)])
-            scp(X("cb", p=8), X("pN", 0, 256, p=8))
-            to_list(X("pM", 448, 464), "cb", 0, 256, X("vS"))
-            place(X("offA"), X("pM", 448, 464), X("o3"), X("trS"))
+            mms([(X("pM", 400, 401), X("on32"), X("hs", 2 * t + h, 2 * t + h + 1)) for h in range(2)])
+            ts(X("hi0", t, t + 1), X("pM", 400, 401), -1.0 / 32, A.mult, 1024.0, A.add)
+            ts(X("hi1", t, t + 1), X("hi0", t, t + 1), 15, A.bitwise_and)
+            tt(X("Hc", t + 1, t + 2), X("hi1", t, t + 1), X("Hc", 0, 1), A.add)
         for h in range(2):
-            keys(t, h)
             distances(t, h)
         for h in range(2):
             best(t, h)
         if not last:
-            cp(IND(X("xdS", 0, WT), X("offA")), X("xn"))
-            mms([(X("pM", 496, 497), X("on32"), X("hs", 2 * t + h, 2 * t + h + 1)) for h in range(2)])
-            ts(X("hi0", t, t + 1), X("pM", 496, 497), -0.5, A.mult, 1024.0, A.add)
-            ts(X("hi1", t, t + 1), X("hi0", t, t + 1), 15, A.bitwise_and)
-            tt(X("Hc", t, t + 1), X("hi1", t, t + 1), X("thF", 0, 1), A.add)
-            ts(X("TH", 16, NK, SEG), X("b80"), X("Hc", t, t + 1), A.mult)
+            cp(IND(X("xdS", 0, WT), X("OA%d" % t)), X("xn"))
+            pairs(t + 1, "VN%d" % t, "EO%d" % t, "vO%d" % t, "OO%d" % t)
         else:
             dmas("Y", "yv", [(T.yv[:, :], X("yvS"))], 8192)
 
     C4 = W // 4
     for j in range(4):
         a, b = j * C4, (j + 1) * C4
-        dmas("Y" if j % 2 == 0 else "S", "y%d" % j, [(T.ynb[:, a:b], X("yn", a, b))], 512 * C4)
+        dmas("YS"[j % 2], "y%d" % j, [(T.ynb[:, a:b], X("yn", a, b))], 512 * C4)
     for j in plan():
         calls[j]["run"]()
     fin = dict(cnt)

@@ -1,5 +1,4 @@
 import numpy as np
-from concourse.bass import DstId, RemoteDMATransfer
 from concourse.mybir import dt, AluOpType, AxisListType, ActivationFunctionType
 
 W = 3072
@@ -9,11 +8,15 @@ U = 4096.0
 BIG = 128 * U
 SEG = 34
 NK = 8 * SEG
-ON_SCALAR = (6, 4)
-LOADS = "n0 n1 pv pz xa xb n2 n3 n4 th"
-CYCLE, GATHER, SCATTER, HOP, BANK, DMA_LAG, DMA_RATE, WAY = 0.83, 1.3, 3.1, 280.0, 200.0, 2500.0, 350.0, 3500.0
-PASSES, SHAKE, SPAN, SEED, EARLY = 600, 1500.0, 4000.0, 1, 1
+WAYS = ((("S", 1), ("S", 1), ("S", 2), ("S", 2), ("V", 1), ("V", 1)), (("S", 2), ("S", 1)) + 5 * (("V", 1),))
+MASKS = (4, 1)
+LOADS = "n0 pv pz xd n1 n2 th"
+PIECES = (0, 1536, 2560, W)
+CYCLE, GATHER, SCATTER, ACT, HOP, BANK, DMA_LAG, DMA_RATE, WAY = 0.83, 1.3, 3.1, 80.0, 280.0, 200.0, 2500.0, 350.0, 3500.0
+PASSES, SHAKE, SPAN, SLACK, SEED, EARLY = 1300, 1500.0, 3000.0, 300.0, 1, 1
 PLAN = []
+MID = 1664.0
+BY_PE = "o1 c1 a0 a1"
 
 SCRATCH = {
     "nbI": ("sbuf", [128, W], "int32"), "nbS": ("sbuf", [128, WT], "float32"), "xdS": ("sbuf", [128, WT], "bfloat16"),
@@ -26,17 +29,19 @@ PART = {}
 def _decl():
     for names, cols, d in (("mk", 4096, "float16"), ("dd xg", 8192, "bfloat16"), ("SB E0 E1 E2 E3 EO0 EO1 EO2", W, "bfloat16"),
                            ("zz0 zz1 zz2 zz3 z40 z41 m40 m41 far", 512, "bfloat16"),
-                           ("LOW dz Pb xi xn d0 hb zn0 zn1 zn2 zn3 FE FO ohS ta tb", 256, "bfloat16"), ("con co", 256, "float16"),
-                           ("TT A1 no Vm Wm Wa", 256, "float32"), ("Tt", 256, "uint16"), ("cU", 512, "uint16"),
-                           ("WP WH TH RST ones", NK, "bfloat16"), ("sc0 sc1 R0 R1", NK, "float32"), ("w34 k34 t34 u34 h34", SEG, "float32"),
-                           ("VL0 VL1 VL2 VL3 VN0 VN1 VN2 VN3 OA0 OA1 OA2 OO0 OO1 TLu offR zo", 16, "uint16"), ("Lg LP Lq", 8, "uint16"),
-                           ("vI0 vI1 vI2 vI3 vO0 vO1 vO2 uo ua yvS ii zf zg", 16, "float32"), ("pvI vi vc", 16, "int32"),
-                           ("thI", 2, "int32"), ("thF", 2, "float32"), ("Hc", 4, "float32"), ("hs iF b8f", 8, "float32"),
-                           ("hi0 hi1", 4, "int32"), ("pI pB iI", 8, "int32"), ("pC", 32, "float32"), ("sg12 pw12", 12, "float32"),
-                           ("ZZ", 144, "bfloat16"), ("ZFe ZFo ZFa", 144, "float16"),
+                           ("LOW Pb xi xn d0 hb zn0 zn1 zn2 zn3 FE EV ohS ta tb", 256, "bfloat16"), ("con co", 256, "float16"),
+                           ("TT A1 no Vm Wo Wa Wz MD2", 256, "float32"), ("Tt", 256, "uint16"), ("cU", 512, "uint16"),
+                           ("WP WH TH RST ones", NK, "bfloat16"), ("R0 R1", NK, "float32"), ("sc0 sc1", NK + 8, "float32"),
+                           ("w34 k34 t34 u34 h34", SEG, "float32"),
+                           ("VL0 VL1 VL2 VL3 VN0 VN1 VN2 VN3 OA0 OA1 OA2 OO0 OO1 TLu offR zo Lq Lg", 16, "uint16"), ("LP", 8, "uint16"),
+                           ("vI0 vI1 vI2 vI3 vO0 vO1 vO2 uo ua yvS ii zf pq", 16, "float32"), ("pvI", 16, "int32"),
+                           ("thI", 2, "int32"), ("thF", 2, "float32"), ("Hc hs", 4, "float32"), ("iF b8f b80 b8u", 8, "float32"),
+                           ("hi0 hi1", 4, "int32"), ("pI pB iI", 8, "int32"), ("pC", 32, "float32"), ("sg12 pw12 eq12", 12, "float32"),
+                           ("ZZ", 144, "bfloat16"), ("ZFe ZFo ZFa Lo0 Lo1 Lc0 Lc1 Lz0 Lz1 La0 La1", 144, "float16"),
+                           ("RQ", 128, "float16"), ("ii16", 16, "float16"), ("uu", 1, "bfloat16"), ("MD rr", 128, "float32"),
                            ("BLK D0 D1 D2 CA CB D0n mt M1 M2 M2a In LT Sp Sm tc", 128, "bfloat16"),
-                           ("I16 N16 W00 W01 W10 W11", 128, "float16"), ("I32 MD on32 rr", 128, "float32"),
-                           ("b8 b80 b8n b8p b8m wv", 8, "bfloat16"), ("rep", 16, "bfloat16"), ("b8h r15", 8, "float16"), ("SelP", 16, "float16")):
+                           ("I16 N16 W00 W01 W10 W11", 128, "float16"), ("I32 on32", 128, "float32"),
+                           ("b8 b8n b8p b8m wv", 8, "bfloat16"), ("rep", 16, "bfloat16"), ("b8h r15", 8, "float16"), ("SelP", 16, "float16")):
         for n in names.split():
             if cols > 32:
                 SCRATCH[n] = ("sbuf", [128, cols], d)
@@ -50,7 +55,7 @@ def _decl():
 
 
 _decl()
-DMAS = LOADS.split() + ["y0", "y1", "y2", "y3", "yv", "yz0", "yz1"] + ["z%d%d" % (t, h) for t in range(4) for h in range(2)]
+DMAS = LOADS.split() + ["yn", "yv", "yz0", "yz1"]
 SEMAPHORES = (["sV", "sS", "sP", "sG", "loc"] + ["d_" + d for d in DMAS]
               + ["a%s%d%d" % (n, t, h) for n in "lz" for t in range(1, 4) for h in range(2)]
               + ["ae%d%d" % (t, b) for t in range(1, 4) for b in range(3)] + ["av1", "av2", "av3", "ao1", "ao2"])
@@ -172,7 +177,7 @@ def rank_program(g, core, T, topo):
             for d in deps[j]:
                 users[d].append(j)
         key = list(range(n))
-        best = None
+        best = now = None
         shake = np.random.default_rng(SEED)
         hop = lambda a, b: 0.0 if calls[a]["uses"][0] == calls[b]["uses"][0] == "P" else HOP
         for k in range(PASSES):
@@ -180,9 +185,11 @@ def rank_program(g, core, T, topo):
             end = max(fw[j] + calls[j]["ns"] for j in range(n))
             if best is None or end <= best[0]:
                 best = (end, fw)
-            u, mid = shake.random(n), best[0] * float(shake.random())
-            src = fw if k < 4 else best[1]
-            near = [SHAKE * float(u[j]) if k >= 4 and abs(src[j] - mid) < SPAN else 0.0 for j in range(n)]
+            if now is None or end <= now[0] + SLACK * (1 - k / PASSES):
+                now = (end, fw)
+            u, mid, amp = shake.random(n), now[0] * float(shake.random()), SHAKE * (0.3 + float(shake.random()))
+            src = fw if k < 4 else now[1]
+            near = [amp * float(u[j]) if k >= 4 and abs(src[j] - mid) < SPAN else 0.0 for j in range(n)]
             if k % 2 and k >= 4:
                 key = [src[j] + near[j] for j in range(n)]
             else:
@@ -282,13 +289,14 @@ def rank_program(g, core, T, topo):
                     kw[nm] = v
         if acc is not None:
             writes = writes + [acc]; kw["accum_out"] = acc[0]
-        t = 65.0 + out[4] * GATHER if len(a) == 3 else max(60.0, 40.0 + out[4] * CYCLE)
+        t = ACT + out[4] * (GATHER if len(a) == 3 else CYCLE)
         op("S", lambda e: e.activation(out[0], a[0], f, **kw), reads, writes, t)
 
-    def scp(out, a):
-        act(out, a, F.Copy)
+    def scp(out, a, scale=None):
+        act(out, a, F.Copy, scale=scale)
 
     parts = {}
+    mark = {}
 
     def mms(items, start=True, stop=True, part=None):
         if part is not None:
@@ -321,10 +329,10 @@ def rank_program(g, core, T, topo):
 
     dsem = {}
 
-    def dmas(q, name, items, nbytes):
+    def dma(q, name, out, src, nbytes):
         s = "d_" + name
-        outs = [o for o, x in items if isinstance(o, tuple)]
-        ins = [x for o, x in items if isinstance(x, tuple)]
+        outs = [out] if isinstance(out, tuple) else []
+        ins = [src] if isinstance(src, tuple) else []
 
         def run():
             deps = {}
@@ -333,15 +341,14 @@ def rank_program(g, core, T, topo):
             for x in ins:
                 need(q, x[1], x[2], x[3], False, deps)
             waits(q, deps)
-            for o, x in items:
-                ENG[q].dma_start(o[0] if isinstance(o, tuple) else o, x[0] if isinstance(x, tuple) else x).then_inc(T.sem[s], 16)
-            c = dsem[s] = 16 * len(items)
-            snap[(s, c)] = dict(known[q])
+            ENG[q].dma_start(out[0] if outs else out, src[0] if ins else src).then_inc(T.sem[s], 16)
+            dsem[s] = 16
+            snap[(s, 16)] = dict(known[q])
             for x in ins:
-                note(q, x[1], x[2], x[3], s, c, False)
+                note(q, x[1], x[2], x[3], s, 16, False)
             for o in outs:
-                note(q, o[1], o[2], o[3], s, c, True)
-        call(q, run, ins, outs, 60.0 * len(items), lag=DMA_LAG, nbytes=nbytes)
+                note(q, o[1], o[2], o[3], s, 16, True)
+        call(q, run, ins, outs, 60.0, lag=DMA_LAG, nbytes=nbytes)
 
     def iota(x, pat, base, cm):
         kw = {} if x[1][-1] == "I" else {"allow_small_or_imprecise_dtypes": True}
@@ -350,16 +357,17 @@ def rank_program(g, core, T, topo):
     def sel(out, a, pat, o, base, cm):
         op("G", lambda e: e.affine_select(out[0], a[0], pat, o, 0.0, base, cm), [a], [out], 170.0 + 2 * CYCLE * out[4])
 
-    H2 = W // 2
-    PIECES = (0, 768, 1536, 2304, 2816, W)
+    def gcp(out, a):
+        sel(out, a, [[0, out[4]]], A.is_ge, 0, 0)
+
     loads = {"pv": (X("pvI"), T.pv[:, :], 8192), "pz": (X("zz0", 0, 256), T.pz[:, :], 65536), "th": (X("thI"), T.th[:, :], 1024),
-             "xa": (X("xdS", 0, H2), T.xd[:, 0:H2], 256 * H2), "xb": (X("xdS", H2, W), T.xd[:, H2:W], 256 * H2)}
-    for j in range(5):
+             "xd": (X("xdS", 0, W), T.xd[:, :], 256 * W)}
+    for j in range(len(PIECES) - 1):
         a, b = PIECES[j], PIECES[j + 1]
         loads["n%d" % j] = (X("nbI", a, b), T.nb[:, a:b], 512 * (b - a))
     done = DMA_LAG
     for j, name in enumerate(LOADS.split()):
-        dmas("YS"[j % 2], name, [loads[name][:2]], loads[name][2])
+        dma("YS"[j % 2], name, *loads[name])
         calls[-2]["run"]()
         done += calls[-1]["ns"] + 100.0
         calls[-2].update({"run": lambda: None, "uses": [name], "lag": 0.0})
@@ -372,9 +380,12 @@ def rank_program(g, core, T, topo):
     fill(X("on32"), 1.0)
     fill(X("RST"), 1.0)
     fill(X("RST", 0, NK, SEG), 0.0)
-    fill(X("tc"), -2.0)
+    fill(X("tc"), -32.0)
+    fill(X("xi"), -192.0)
+    fill(Hf("EV", 0), 165.0)
+    fill(Hf("EV", 1), 0.0)
     fill(pc(19), -1.0)
-    fill(pc(24), -11.0)
+    fill(pc(24), -176.0)
     sel(X("ta", 0, 128), one, [[-16, 8], [0, 16]], A.is_ge, 0, 1)
     sel(X("BLK"), X("ta", 0, 128), [[16, 8], [0, 16]], A.is_ge, 15, -1)
     sel(X("ta", 128, 256), X("BLK"), [[1, 128]], A.is_ge, 0, -1)
@@ -411,12 +422,12 @@ def rank_program(g, core, T, topo):
     ts(pc(10), pc(1), -1.0, A.mult, 1.0, A.add)
     ts(pc(11), pc(5), -1.0, A.mult, 1.0, A.add)
     cp(X("VL0"), X("pvI"))
-    ts(X("In"), X("D0"), -1.0, A.mult)
-    ts(X("D0n"), X("D0"), pc(9), A.mult)
+    scp(X("In"), X("D0"), -1.0)
+    scp(X("D0n"), X("D0"), pc(9))
     tt(X("mt"), X("CA"), X("D0n"), A.subtract)
     tt(X("M1"), X("D1"), X("mt"), A.add)
-    ts(X("M2a"), X("CB"), -256.0, A.mult)
-    cp(X("D2"), X("LT"))
+    scp(X("M2a"), X("CB"), -256.0)
+    scp(X("D2"), X("LT"))
     fill(X("D2", 14, 128, 16), 0.0)
     tt(X("M2"), X("M2a"), X("D2"), A.add)
     ts(pc(28), pc(0), 14.0, A.is_ge, 400.0, A.mult)
@@ -426,30 +437,30 @@ def rank_program(g, core, T, topo):
     ts(pc(12), pc(2), 32.0, A.mult, pc(4), A.add)
     ts(pc(13), pc(3), 16.0, A.mult, pc(12), A.add)
     ts(X("LP"), X("iF"), pc(13), A.add)
-    ts(X("Lq"), X("iF"), 0.5, A.mult)
-    cp(X("Lg"), X("iI"))
+    ts(X("Lq"), X("ii"), 1.0 / 16, A.mult)
+    cp(Q("Lg", 0), X("iI"))
+    ts(Q("Lg", 1), X("iF"), 0.5, A.mult, float(NK), A.add)
     ts(X("ZFe"), X("ZZ"), pc(10), A.mult)
     ts(X("ZFo"), X("ZZ"), pc(1), A.mult)
     cp(X("ZFa"), X("ZZ"))
     cp(X("thF"), X("thI"))
-    cp(X("b8"), X("BLK", 0, 128, 16))
+    scp(X("b8"), X("BLK", 0, 128, 16))
     cp(X("b8h"), X("b8"))
-    cp(X("b8f"), X("b8"))
+    scp(X("b8f"), X("b8"))
     ts(X("r15"), X("b8"), pc(8), A.mult)
     ts(X("SelP", 0, 16, 2), X("b8"), pc(10), A.mult)
     ts(X("SelP", 1, 16, 2), X("b8"), pc(1), A.mult)
     ts(pc(14), pc(0), 0.0, A.is_equal, BIG, A.mult)
-    ts(X("b80"), X("b8"), pc(14), A.mult)
-    for n, v in (("b8n", -BIG), ("b8p", BIG), ("b8m", -2 * BIG)):
-        ts(X(n), X("b8"), v, A.mult)
+    for n, v in (("b80", pc(14)), ("b8u", U), ("b8n", -BIG), ("b8p", BIG), ("b8m", -2 * BIG)):
+        scp(X(n), X("b8"), v)
     ts(X("u34"), X("k34"), 0.0, A.mult, X("thF", 1, 2), A.add)
     fill(X("u34", 16, SEG, 17), 2.0)
     fill(X("h34"), -0.5)
     fill(X("h34", 16, 17), 0.5)
     fill(X("h34", 33, 34), 0.0)
     for n in range(8):
-        ts(X("TH", SEG * n, SEG * n + SEG), X("u34"), X("b80", n, n + 1), A.mult)
-        ts(X("WH", SEG * n, SEG * n + SEG), X("h34"), X("b80", n, n + 1), A.mult)
+        scp(X("TH", SEG * n, SEG * n + SEG), X("u34"), X("b80", n, n + 1))
+        scp(X("WH", SEG * n, SEG * n + SEG), X("h34"), X("b80", n, n + 1))
     ts(X("Hc", 0, 1), X("thF", 0, 1), -0.5, A.add)
     fill(X("w34", 16, 17), 2.0 - 64.0)
     fill(X("w34", 33, 34), 1.0)
@@ -463,28 +474,41 @@ def rank_program(g, core, T, topo):
     ts(X("w34", 0, 16), X("w34", 0, 16), pc(18), A.subtract)
     ts(X("w34", 17, 33), X("w34", 17, 33), pc(18), A.add)
     for n in range(8):
-        ts(X("WP", SEG * n, SEG * n + SEG), X("w34"), X("b8", n, n + 1), A.mult, U, A.mult)
+        scp(X("WP", SEG * n, SEG * n + SEG), X("w34"), X("b8u", n, n + 1))
     cp(X("I16"), X("D0"))
     cp(X("N16"), X("In"))
-    cp(X("I32"), X("D0"))
+    scp(X("I32"), X("D0"))
     ts(X("MD"), X("rr"), pc(0), A.is_equal)
     ts(X("ii"), X("ii"), pc(0), A.add)
+    scp(Hf("MD2", 0), Hf("MD", 0))
+    scp(Hf("MD2", 1), Hf("MD", 0), -1.0)
     for h in range(2):
-        ts(pc(21 + h), pc(20), W + 128 * h - U, A.add, 1.0 / U, A.mult)
-        ts(pc(25 + h), pc(20), W + 128 * h, A.add, 1.0 / U, A.mult)
-    ts(X("SB", 0, 1), pc(0), 12.0, A.is_lt, -1.0, A.mult)
-    for b in range(12):
-        ts(X("sg12", b, b + 1), pc(0), float(b), A.not_equal, 2.0, A.mult)
-        ts(X("pw12", b, b + 1), pc(0), float(b), A.is_equal, 2.0 ** (b - 1) / U, A.mult)
-    ts(X("sg12"), X("sg12"), -1.0, A.add)
+        ts(pc(21 + h), pc(20), W + 128 * h - MID, A.add)
+    for n in BY_PE.split():
+        fill(X("L" + n), 0.0)
+    fill(X("uu"), U)
+    sel(X("tb", 0, 128), one, [[-1, 16], [-16, 8]], A.is_equal, 0, 1)
+    cp(X("RQ"), X("tb", 0, 128))
+    cp(X("ii16"), X("ii"))
+    ts(pc(25), pc(5), -3.0, A.mult, -1.0, A.add)
+    ts(pc(26), pc(5), -0.75, A.mult, 1.0, A.add)
+    ts(X("SB", 0, 1), pc(0), 12.0, A.is_lt, pc(25), A.mult)
+    ts(X("eq12"), X("k34", 0, 12), pc(0), A.is_equal)
+    act(X("sg12"), X("eq12"), F.Copy, scale=-2.0, bias=1.0)
+    fill(X("pw12", 0, 1), 0.5)
+    for b in (1, 2, 4, 8):
+        scp(X("pw12", b, min(2 * b, 12)), X("pw12", 0, min(b, 12 - b)), 2.0 ** b)
+    tt(X("pw12"), X("pw12"), X("eq12"), A.mult)
     for b in range(12):
         n = min(2 ** b, W - 2 ** b)
-        ts(X("SB", 2 ** b, 2 ** b + n), X("SB", 0, n), X("sg12", b, b + 1), A.mult)
+        scp(X("SB", 2 ** b, 2 ** b + n), X("SB", 0, n), X("sg12", b, b + 1))
     op("V", lambda e: e.tensor_reduce(pc(23)[0], X("pw12")[0], AxisListType.X, A.add), [X("pw12")], [pc(23)], 60.0)
-    ts(X("wv"), X("b8"), pc(23), A.mult)
-    for j in range(5):
-        a, b = PIECES[j], PIECES[j + 1]
-        ts(X("nbS", a, b), X("nbI", a, b), -OFF, A.add)
+    tt(pc(29), pc(23), pc(26), A.mult)
+    scp(X("wv"), X("b8"), pc(29))
+    tt(X("LOW"), X("LOW"), X("EV"), A.add)
+    scp(X("EV"), X("EV"), 1.0 / 128)
+    for a in range(0, W, 512):
+        ts(X("nbS", a, a + 512), X("nbI", a, a + 512), -OFF, A.add)
 
     nxt = T.cores[(rank + 1) % len(T.cores)]
     prv = T.cores[(rank - 1) % len(T.cores)]
@@ -516,22 +540,29 @@ def rank_program(g, core, T, topo):
     def ind_n(off):
         return IND(X("nbS", 0, W), off)
 
-    def spare(h):
-        return X("pM", 272, 400) if h else PX(0, 12, 16)
-
     def level(t, h):
-        z = Hf("zz%d" % t, h)
-        dmas("Y", "z%d%d" % (t, h), [(Hf("z4%d" % h, c), z) for c in range(4)], 4 * 32768)
-        tt(Hf("dz", h), ind_x(Q("VL%d" % t, h)), z, A.subtract)
+        z, z4, m4, n = Hf("zz%d" % t, h), "z4%d" % h, "m4%d" % h, MASKS[h]
+        for out, src in ((Hf(z4, 0), z), (Hf(z4, 1), z), (X(z4, 256, 512), X(z4, 0, 256))):
+            gcp(out, src)
+        dz = Hf("zz%d" % t, 2 + h)
+        tt(dz, ind_x(Q("VL%d" % t, h)), z, A.subtract)
         far = [Hf("far", 2 * h + s) for s in range(2)]
         for s in range(2):
-            act(far[s], Hf("dz", h), F.Relu, bias=pc(19), scale=1.0 - 2 * s)
+            act(far[s], dz, F.Relu, bias=pc(19), scale=1.0 - 2 * s)
         ps = "pS%d" % h
-        mms([(Hf(ps, c), X("M2"), f) for c in range(4) for f in far])
-        act(X("m4%d" % h), X(ps), F.Sigmoid, bias=pc(27), scale=400.0)
-        mms([(spare(h), X("LT"), f) for f in far])
-        act(Hf("Pb", h), spare(h), F.Relu, bias=pc(7), scale=-1.0)
-        act(Hf("zz%d" % t, 2 + h), Hf("dz", h), F.Abs)
+        mms([(Hf(ps, c), X("M2"), f) for c in range(n) for f in far])
+        act(X(m4, 0, 128 * n), X(ps, 0, 128 * n), F.Sigmoid, bias=pc(27), scale=400.0)
+        while n < 4:
+            gcp(X(m4, 128 * n, 256 * n), X(m4, 0, 128 * n))
+            n *= 2
+        ps = X("pM", 272, 400) if h else PX(0, 12, 16)
+        mms([(ps, X("LT"), f) for f in far])
+        act(Hf("Pb", h), ps, F.Relu, bias=pc(7), scale=-1.0)
+        mms([(ps, X("M1"), Hf("Pb", h))])
+        scp(Hf("ohS", h), ps)
+        if t < 3:
+            mms([(ps, X("D0"), dz), (ps, X("D0"), z), (ps, X("D0"), z)])
+            act(Hf("xn", h), ps, F.Copy, bias=191.75, scale=0.5)
 
     def ccols(h, kh, par, a=0, b=64):
         c = 256 * h + 128 * kh + 64 * par
@@ -564,23 +595,16 @@ def rank_program(g, core, T, topo):
             if h or kh:
                 ts(ccols(h, kh, 0, 0, 128), PX(kh, 4 + 4 * kh, 8 + 4 * kh), OFF, A.add)
 
-    def own(t, h):
-        ps = spare(h)
-        mms([(ps, X("M1"), Hf("Pb", h))])
-        tt(Hf("co", h), ps, Hf("con", h), A.mult)
-        scp(Hf("ohS", h), ps)
-        mms([(Q("pM", 54 + h), X("ZFa", 15 - r, 143 - r), X("co", 128 * h + r, 128 * h + 128, 16)) for r in range(16)])
-        ts(Q("TLu", h), Q("pM", 54 + h), OFF, A.add)
-        tt(Hf("d0", h), ind_x(Q("TLu", h)), Hf("zz%d" % t, h), A.subtract)
-        act(Hf("d0", h), Hf("d0", h), F.Abs)
-        mms([(ps, X("BLK"), Hf("d0", h))])
-        act(Hf("hb", h), ps, F.Sign, bias=X("Hc", t, t + 1), scale=-1.0, acc=X("hs", 2 * t + h, 2 * t + h + 1))
-        mms([(ps, X("I16"), Hf("con", h)), (ps, X("N16"), Hf("co", h))])
-        act(Hf("A1", h), ps, F.Copy, bias=OFF if t == 3 else 0.0)
-        if t < 3:
-            act(Hf("xi", h), Hf("dz", h), F.Copy, bias=191.75, scale=0.5)
-            mms([(ps, X("D0"), Hf("xi", h)), (ps, X("D0"), Hf("zz%d" % t, h))])
-            act(Hf("xn", h), ps, F.Copy, bias=-192.0)
+    def healthy(t):
+        ps = X("pM", 0, 256)
+        mms([(ps, X("M1"), X("Pb"))])
+        tt(X("co"), ps, X("con"), A.mult)
+        mms([(X("pM", 432, 448), X("ZFa", 15 - r, 143 - r), X("co", r, 256, 16)) for r in range(16)])
+        ts(X("TLu"), X("pM", 432, 448), OFF, A.add)
+        tt(X("d0"), ind_x(X("TLu")), X("zz%d" % t, 0, 256), A.subtract)
+        act(X("d0"), X("d0"), F.Abs)
+        mms([(ps, X("BLK"), X("d0"))])
+        act(X("hb"), ps, F.Sign, bias=X("Hc", t, t + 1), scale=-1.0, acc=X("hs", t, t + 1))
 
     def keys(h):
         mms([(X("pM", 0, NK), Hf("Pb", h), X("WP")), (X("pM", 0, NK), Hf("hb", h), X("WH"))]
@@ -591,96 +615,113 @@ def rank_program(g, core, T, topo):
     turn = [0]
 
     def distances(t, h):
-        for n in range(8):
+        n = 0
+        for way, w in WAYS[h]:
             kh, par, s = n // 4, n // 2 % 2, n % 2
             a = 4096 * h + 512 * n
-            dd = X("dd", a, a + 512)
-            src = ind_x(ccols(h, kh, par, 32 * s, 32 * s + 32))
-            if n < ON_SCALAR[h]:
-                ps = ("pS0", "pS1", "pN")[turn[0] % 3]
-                turn[0] += 1
-                act(X("xg", a, a + 512), src, F.Copy)
-                mms([(Hf(ps, k), X("In"), Hf("zz%d" % t, h)) for k in range(4)], stop=False)
-                mms([(X(ps), X("D0"), X("xg", a, a + 512))], start=False)
-                act(dd, X(ps), F.Abs)
+            n += w
+            dd, xg = X("dd", a, a + 512 * w), X("xg", a, a + 512 * w)
+            src = ind_x(ccols(h, kh, par, 32 * s, 32 * (s + w)))
+            if way == "S":
+                act(xg, src, F.Copy)
+                for b in range(a, a + 512 * w, 512):
+                    ps = ("pS0", "pS1", "pN")[turn[0] % 3]
+                    turn[0] += 1
+                    mms([(Hf(ps, k), X("In"), Hf("zz%d" % t, h)) for k in range(4)], stop=False)
+                    mms([(X(ps), X("D0"), X("xg", b, b + 512))], start=False)
+                    act(X("dd", b, b + 512), X(ps), F.Abs)
                 terms = (("dd", "b8n"),)
             else:
                 tt(dd, src, X("z4%d" % h), A.subtract)
-                ts(X("xg", a, a + 512), dd, 0.0, A.max)
+                ts(xg, dd, 0.0, A.max)
                 terms = (("dd", "b8p"), ("xg", "b8m"))
-            for name, w in terms:
-                mms([(X("pD%d" % h, 17 * par + 8 * kh + 4 * s + k, NK, SEG), X(name, a + 128 * k, a + 128 * k + 128), X(w)) for k in range(4)],
-                    start=False, part="D%d%d" % (t, h))
+            for c in range(w):
+                for name, wt in terms:
+                    mms([(X("pD%d" % h, 17 * par + 8 * kh + 4 * (s + c) + k, NK, SEG), Hf(name, a // 128 + 4 * c + k), X(wt)) for k in range(4)],
+                        start=False, part="D%d%d" % (t, h))
 
     def eb(E, b, n):
         return Hf(E, 8 + 4 * (n // 2) + 2 * (b - 1) + n % 2 if b else n)
 
-    def to_list(out, tmp, src):
-        tt(tmp, src, X("MD"), A.mult)
-        mms([(out, tmp, X("b8f"))])
+    def listed(name, small):
+        return X("L" + name, 15, 143, 16) if name in BY_PE else small
+
+    def to_list(name, out, small, more=()):
+        if name in BY_PE:
+            mms(list(more) + [(out, X("L" + name, 15 - r, 143 - r), Q("RQ", r)) for r in range(16)])
+        else:
+            tmp = Hf("W" + name[0], int(name[1]))
+            tt(tmp, IND(small, Q("Lq", 0)), X("MD"), A.mult)
+            mms(list(more) + [(out, tmp, X("b8f"))])
 
     def pairs(t, VL, E, vI, OA):
         for h in range(2):
-            for F2, j in (("FE", 11), ("FO", 5)):
-                act(Hf(F2, h), IND(X("SB"), Q(VL, h)), F.Copy, scale=pc(j))
-            mms([(Q("pM", 62 + h), Hf(F2, h), X("wv")) for F2 in ("FE", "FO")])
-            act(Q(vI, h), Q("pM", 62 + h), F.Copy, bias=(U - 1) / 2 / U)
+            act(Hf("FE", h), IND(X("SB"), Q(VL, h)), F.Copy)
+            mms([(Q("pM", 62 + h), Hf("FE", h), X("wv"))])
+            act(Q(vI, h), Q("pM", 62 + h), F.Copy, bias=(U - 1) / 2 - MID)
         for blocks in (((0, 0),), ((0, 1), (1, 1))):
             for a in range(4):
                 ps, w = ("pN", "pS1")[a % 2], 256 * len(blocks)
-                part = lambda F2, h: (T[F2][32 * a:32 * a + 32, 128 * h:128 * h + 128], F2, 128 * h, 128 * h + 128, 128)
-                mms([(X(ps, w - 256, w), X("D0"), X("LOW"))]
-                    + [(Hf(ps, 2 * k + m), part(F2, ha), part(F2, hb)) for k, (ha, hb) in enumerate(blocks) for m, F2 in enumerate(("FE", "FO"))])
+                part = lambda m, h: (T.FE[32 * a:32 * a + 16 * (m + 1), 128 * h:128 * h + 128], "FE", 128 * h, 128 * h + 128, 128)
+                mms([(X(ps, w - 256, w), X("D0"), X("LOW"))] + [(Hf(ps, 0), one, Hf("EV", 0))] * (len(blocks) - 1)
+                    + [(Hf(ps, 2 * k + m), part(m, ha), part(m, hb)) for k, (ha, hb) in enumerate(blocks) for m in range(2)])
                 at = 1024 * (len(blocks) - 1) + w * a
                 act(X(E, at, at + w), X(ps, 0, w), F.Relu, bias=pc(24))
                 if t and (at + w) % 1024 == 0:
                     send(X("E%d" % t, at + w - 1024, at + w), X(E, at + w - 1024, at + w), "ae%d%d" % (t, at // 1024))
+                    calls[-1]["deps"].add(mark["z"])
         if t:
             send(X("vI%d" % t), X(vI), "av%d" % t)
         if t < 3:
             for h in range(2):
                 mms([(Q("pM", 52 + h), X("I32"), Q(vI, h))]
-                    + [(X("pM", 416 + 8 * h + n, 417 + 8 * h + n), eb(E, b, n), X("ones", 0, 1)) for b in ((0,), (1, 2))[h] for n in range(8)])
-                ts(Q("ua", h), Q("pM", 52 + h), pc(25 + h), A.min, U, A.mult)
-                to_list(Q("pM", 56 + h), Hf("Wa", h), IND(Q("ua", h), X("Lq")))
-            cp(X(OA), X("pM", 448, 464))
+                    + [(X("pM", 416 + 8 * h + n, 417 + 8 * h + n), eb(E, b, n), X("uu")) for b in ((0,), (1, 2))[h] for n in range(8)])
+                ts(listed("a%d" % h, Q("ua", h)), Q("pM", 52 + h), pc(21 + h), A.min)
+                to_list("a%d" % h, Q("pM", 56 + h), Q("ua", h))
+            ts(X(OA), X("pM", 448, 464), MID, A.add)
             if t:
                 send(X("OA%d" % t), X(OA), "ao%d" % t)
 
     def best(t, h):
-        sc, pk = X("sc%d" % h), X("R%d" % h)
+        sc, pk, top = X("sc%d" % h, 0, NK), X("R%d" % h), X("sc%d" % h, SEG - 1, NK, SEG)
         tt(pk, X("pD%d" % h, 0, NK), pk, A.min)
         op("V", lambda e: e.tensor_tensor_scan(sc[0], T.RST[:, :], pk[0], 0.0, A.mult, A.max), [X("RST"), pk], [sc], ns(sc, pk))
-        ts(Q("rep", h), X("sc%d" % h, SEG - 1, NK, SEG), 3 * U - OFF, A.is_ge)
+        ts(Q("rep", h), top, 3 * U - OFF, A.is_ge, U, A.mult)
         E, u = "E%d" % t, Q("pD0", 35 + h)
         count = lambda b, ha, hb: [(X("pD0", 280 + 8 * hb + n, 281 + 8 * hb + n), eb(E, b, n), X("rep", 8 * ha + n, 8 * ha + n + 1)) for n in range(8)]
         if h == 0:
             mms([(u, X("I32"), Q("vI%d" % t, 0)), (u, X("In"), Q("rep", 0))] + count(0, 0, 0))
         else:
             mms([(u, X("In"), Q("rep", 1))] + count(2, 1, 1), start=False)
-        ts(Q("uo", h), u, pc(21 + h), A.min, U, A.mult)
+        ts(listed("o%d" % h, Q("uo", h)), u, U, A.add, pc(21 + h), A.min)
         if h == 0:
             mms([(Q("pD0", 36), X("I32"), Q("vI%d" % t, 1))] + count(1, 0, 1), stop=False)
             calls[-1]["deps"].add(len(calls) - 2)
-        to_list(Q("pM", 58 + h), Hf("Wm", h), IND(Q("uo", h), X("Lq")))
-        ts(Q("offR", h), Q("pM", 58 + h), U, A.add)
+        to_list("o%d" % h, Q("pM", 58 + h), Q("uo", h))
+        ts(Q("offR", h), Q("pM", 58 + h), MID, A.add)
         val = Q("pM", 60 + h)
-        to_list(val, Hf("Vm", h), IND(sc, X("Lg")))
-        ts(Q("vi", h), val, OFF, A.add)
-        ts(Q("vc", h), Q("vi", h), int(U) - 1, A.bitwise_and)
-        cp(Q("VN%d" % t, h), Q("vc", h))
+        ts(X("sc%d" % h, NK, NK + 8), top, 1.5 * 2.0 ** 35, A.add, 1.5 * 2.0 ** 35, A.subtract)
+        if "c%d" % h in BY_PE:
+            tt(listed("c%d" % h, None), top, X("sc%d" % h, NK, NK + 8), A.subtract)
+            to_list("c%d" % h, val, None)
+        else:
+            tt(X("Vm"), IND(X("sc%d" % h), X("Lg")), X("MD2"), A.mult)
+            mms([(val, Hf("Vm", k), X("b8f")) for k in range(2)])
+        ts(Q("VN%d" % t, h), val, OFF, A.add)
         if t < 3:
             send(Q("VL%d" % (t + 1), h), Q("VN%d" % t, h), "al%d%d" % (t + 1, h))
-        ts(Q("zf", h), Q("vi", h), 2 * U, A.is_lt, 256.0, A.mult)
-        tt(Q("zg", h), Q("zf", h), Q("ii", h), A.add)
-        cp(Q("zo", h), Q("zg", h))
+        else:
+            act(Q("yvS", h), val, F.Copy, bias=OFF)
+        ts(listed("z%d" % h, Q("zf", h)), top, 2 * U - OFF, A.is_lt, 256.0, A.mult)
+        to_list("z%d" % h, Q("pM", 51), Q("zf", h), [(Q("pM", 51), X("I16"), Q("ii16", h))])
+        cp(Q("zo", h), Q("pM", 51))
         zn = Hf("zn%d" % t, h)
-        act(zn, IND(X("zz%d" % t), Q("zo", h)), F.Copy)
+        act(zn, IND(X("zz%d" % t), Q("zo", h)), F.Abs)
+        mark["z"] = len(calls) - 1
         if t < 3:
             send(Hf("zz%d" % (t + 1), h), zn, "az%d%d" % (t + 1, h))
         else:
-            dmas("Y", "yz%d" % h, [(T.yz[:, 128 * h:128 * h + 128], zn)], 32768)
-            cp(Q("yvS", h), Q("vc", h))
+            dma("Y", "yz%d" % h, T.yz[:, 128 * h:128 * h + 128], zn, 32768)
         tt(Hf("no", h), IND(X("idW"), Q("VN%d" % t, h)), Hf("ohS", h), A.mult)
         tt(IND(X("nbS" if t < 3 else "yn", 0, WT), Q("offR", h)), Hf("no", h), Hf("A1", h), A.add)
 
@@ -693,10 +734,13 @@ def rank_program(g, core, T, topo):
             level(t, h)
             candidates(t, h)
             mms([(X("pD%d" % h, 0, NK)[:3] + (512, NK), one, X("TH"))], stop=False)
-            own(t, h)
-            keys(h)
+        healthy(t)
+        keys(0)
+        mms([(X("pM", 0, 256), X("I16"), X("con")), (X("pM", 0, 256), X("N16"), X("co"))])
+        act(X("A1"), X("pM", 0, 256), F.Copy, bias=OFF if last else 0.0)
+        keys(1)
         if not last:
-            mms([(X("pM", 400, 401), X("on32"), X("hs", 2 * t + h, 2 * t + h + 1)) for h in range(2)])
+            mms([(X("pM", 400, 401), X("on32"), X("hs", t, t + 1))])
             ts(X("hi0", t, t + 1), X("pM", 400, 401), -1.0 / 32, A.mult, 1024.0, A.add)
             ts(X("hi1", t, t + 1), X("hi0", t, t + 1), 15, A.bitwise_and)
             tt(X("Hc", t + 1, t + 2), X("hi1", t, t + 1), X("Hc", 0, 1), A.add)
@@ -705,15 +749,12 @@ def rank_program(g, core, T, topo):
         for h in range(2):
             best(t, h)
         if not last:
-            cp(IND(X("xdS", 0, WT), X("OA%d" % t)), X("xn"))
+            tt(IND(X("xdS", 0, WT), X("OA%d" % t)), X("xn"), X("xi"), A.add)
             pairs(t + 1, "VN%d" % t, "EO%d" % t, "vO%d" % t, "OO%d" % t)
         else:
-            dmas("Y", "yv", [(T.yv[:, :], X("yvS"))], 8192)
+            dma("Y", "yv", T.yv[:, :], X("yvS"), 8192)
 
-    C4 = W // 4
-    for j in range(4):
-        a, b = j * C4, (j + 1) * C4
-        dmas("YS"[j % 2], "y%d" % j, [(T.ynb[:, a:b], X("yn", a, b))], 512 * C4)
+    dma("S", "yn", T.ynb[:, :], X("yn", 0, W), 512 * W)
     for j in plan():
         calls[j]["run"]()
     fin = dict(cnt)

import numpy as np
from concourse.mybir import dt, AluOpType, AxisListType, ActivationFunctionType

W = 3072
WT = W + 256
OFF = 1536.0
U = 4096.0
BIG = 128 * U
SEG = 34
NK = 8 * SEG
WAYS = ((("S", 1), ("S", 1), ("S", 2), ("S", 2), ("V", 1), ("V", 1)), (("S", 2), ("S", 1)) + 5 * (("V", 1),))
MASKS = (4, 1)
LOADS = "n0 pv pz xd n1 n2 th"
PIECES = (0, 1536, 2560, W)
CYCLE, GATHER, SCATTER, ACT, HOP, BANK, DMA_LAG, DMA_RATE, WAY = 0.83, 1.3, 3.1, 80.0, 280.0, 200.0, 2500.0, 350.0, 3500.0
PASSES, SHAKE, SPAN, SLACK, SEED, EARLY = 1300, 1500.0, 3000.0, 300.0, 1, 1
PLAN = []
MID = 1664.0
BY_PE = "o1 c1 a0 a1"

SCRATCH = {
    "nbI": ("sbuf", [128, W], "int32"), "nbS": ("sbuf", [128, WT], "float32"), "xdS": ("sbuf", [128, WT], "bfloat16"),
    "idW": ("sbuf", [128, W], "float32"), "yn": ("sbuf", [128, WT], "float32"),
    "px0": ("psum", [128, 16, 32], "float32"), "px1": ("psum", [128, 16, 32], "float32"),
}
PART = {}


def _decl():
    for names, cols, d in (("mk", 4096, "float16"), ("dd xg", 8192, "bfloat16"), ("SB E0 E1 E2 E3 EO0 EO1 EO2", W, "bfloat16"),
                           ("zz0 zz1 zz2 zz3 z40 z41 m40 m41 far", 512, "bfloat16"),
                           ("LOW Pb xi xn d0 hb zn0 zn1 zn2 zn3 FE EV ohS ta tb", 256, "bfloat16"), ("con co", 256, "float16"),
                           ("TT A1 no Vm Wo Wa Wz MD2", 256, "float32"), ("Tt", 256, "uint16"), ("cU", 512, "uint16"),
                           ("WP WH TH RST ones", NK, "bfloat16"), ("R0 R1", NK, "float32"), ("sc0 sc1", NK + 8, "float32"),
                           ("w34 k34 t34 u34 h34", SEG, "float32"),
                           ("VL0 VL1 VL2 VL3 VN0 VN1 VN2 VN3 OA0 OA1 OA2 OO0 OO1 TLu offR zo Lq Lg", 16, "uint16"), ("LP", 8, "uint16"),
                           ("vI0 vI1 vI2 vI3 vO0 vO1 vO2 uo ua yvS ii zf pq", 16, "float32"), ("pvI", 16, "int32"),
                           ("thI", 2, "int32"), ("thF", 2, "float32"), ("Hc hs", 4, "float32"), ("iF b8f b80 b8u", 8, "float32"),
                           ("hi0 hi1", 4, "int32"), ("pI pB iI", 8, "int32"), ("pC", 32, "float32"), ("sg12 pw12 eq12", 12, "float32"),
                           ("ZZ", 144, "bfloat16"), ("ZFe ZFo ZFa Lo0 Lo1 Lc0 Lc1 Lz0 Lz1 La0 La1", 144, "float16"),
                           ("RQ", 128, "float16"), ("ii16", 16, "float16"), ("uu", 1, "bfloat16"), ("MD rr", 128, "float32"),
                           ("BLK D0 D1 D2 CA CB D0n mt M1 M2 M2a In LT Sp Sm tc", 128, "bfloat16"),
                           ("I16 N16 W00 W01 W10 W11", 128, "float16"), ("I32 on32", 128, "float32"),
                           ("b8 b8n b8p b8m wv", 8, "bfloat16"), ("rep", 16, "bfloat16"), ("b8h r15", 8, "float16"), ("SelP", 16, "float16")):
        for n in names.split():
            if cols > 32:
                SCRATCH[n] = ("sbuf", [128, cols], d)
            else:
                home = "few_" + d
                at = SCRATCH[home][1][1] if home in SCRATCH else 0
                PART[n] = (home, at, cols)
                SCRATCH[home] = ("sbuf", [128, at + (cols + 15) // 16 * 16], d)
    for b in "pD0 pD1 pS0 pS1 pM pN".split():
        SCRATCH[b] = ("psum", [128, 512], "float32")


_decl()
DMAS = LOADS.split() + ["yn", "yv", "yz0", "yz1"]
SEMAPHORES = (["sV", "sS", "sP", "sG", "loc"] + ["d_" + d for d in DMAS]
              + ["a%s%d%d" % (n, t, h) for n in "lz" for t in range(1, 4) for h in range(2)]
              + ["ae%d%d" % (t, b) for t in range(1, 4) for b in range(3)] + ["av1", "av2", "av3", "ao1", "ao2"])


def rank_program(g, core, T, topo):
    rank = T.rank_of(core)
    if rank is None:
        return
    A, F = AluOpType, ActivationFunctionType
    ENG = {"V": g.vector, "S": g.scalar, "P": g.tensor, "G": g, "Y": g.sync}
    cnt = {"sV": 0, "sS": 0, "sP": 0, "sG": 0}
    known = {q: {} for q in ENG}
    snap = {}
    rec = {}

    def need(q, name, lo, hi, wr, out):
        ps = name in SCRATCH and SCRATCH[name][0] == "psum"
        for (a, b, q2, s, c, w2) in rec.get(name, ()):
            if ps and q == q2 == "P":
                continue
            if (ps and q2 != q) or (a < hi and lo < b and (wr or w2)):
                if out.get(s, 0) < c:
                    out[s] = c

    def note(q, name, lo, hi, s, c, wr):
        keep = []
        for x in rec.get(name, []):
            inside = lo <= x[0] and x[1] <= hi
            if inside and (wr or (x[2] == q and not x[5] and x[3] == s)):
                continue
            keep.append(x)
        keep.append((lo, hi, q, s, c, wr))
        rec[name] = keep

    def waits(q, deps):
        k = known[q]
        for s in sorted(deps, key=lambda s: -len(snap.get((s, deps[s]), ()))):
            c = deps[s]
            if k.get(s, 0) >= c:
                continue
            ENG[q].wait_ge(T.sem[s], c)
            for s2, c2 in snap.get((s, c), {}).items():
                if k.get(s2, 0) < c2:
                    k[s2] = c2
            k[s] = max(k.get(s, 0), c)

    calls = []
    seen = {}

    def call(q, run, reads, writes, ns, lag=0.0, adds=False, nbytes=0):
        me = len(calls) + (1 if nbytes else 0)
        deps = set()
        for xs, wr in ((reads, False), (writes, True)):
            for x in xs:
                for (a, b, c, w2, ad) in seen.get(x[1], ()):
                    if a < x[3] and x[2] < b and (wr or w2) and not (wr and adds and ad):
                        deps.add(c)
        for xs, wr in ((reads, False), (writes, True)):
            for x in xs:
                old = seen.get(x[1], [])
                if wr and not adds:
                    old = [y for y in old if not (x[2] <= y[0] and y[1] <= x[3])]
                seen[x[1]] = old + [(x[2], x[3], me, wr, wr and adds)]
        deps.discard(me)
        uses = [q] + sorted({x[1] for x in reads + writes if in_psum(x)})
        calls.append({"uses": uses, "run": run, "deps": deps, "ns": ns, "lag": lag})
        if nbytes:
            calls.append({"uses": ["engines"], "run": lambda: None, "deps": {me - 1}, "ns": nbytes / DMA_RATE, "lag": 0.0})

    def place_calls(rank_of, before, after, delay):
        n = len(calls)
        left = [len(b) for b in before]
        at = [0.0] * n
        busy = {}
        ready = [j for j in range(n) if left[j] == 0]
        while ready:
            j = min(ready, key=rank_of)
            ready.remove(j)
            c = calls[j]
            s, moved = at[j], True
            while moved:
                moved = False
                for u in c["uses"]:
                    taken = busy.setdefault(u, [])
                    lo, hi = 0, len(taken)
                    while lo < hi:
                        mid = (lo + hi) // 2
                        if taken[mid][1] + BANK <= s:
                            lo = mid + 1
                        else:
                            hi = mid
                    while lo < len(taken) and taken[lo][0] < s + c["ns"] + BANK:
                        gap = BANK if taken[lo][2] != c["uses"][0] else 0.0
                        if taken[lo][0] < s + c["ns"] + gap and s < taken[lo][1] + gap:
                            s, moved = taken[lo][1] + gap, True
                        lo += 1
            at[j] = s
            for u in c["uses"]:
                taken = busy[u]
                k = len(taken)
                while k and taken[k - 1][0] > s:
                    k -= 1
                taken.insert(k, (s, s + c["ns"], c["uses"][0]))
            for u in after[j]:
                at[u] = max(at[u], s + c["ns"] + delay(j, u))
                left[u] -= 1
                if left[u] == 0:
                    ready.append(u)
        return at

    def plan():
        if PLAN:
            return PLAN
        n = len(calls)
        deps = [sorted(c["deps"]) for c in calls]
        users = [[] for c in calls]
        for j in range(n):
            for d in deps[j]:
                users[d].append(j)
        key = list(range(n))
        best = now = None
        shake = np.random.default_rng(SEED)
        hop = lambda a, b: 0.0 if calls[a]["uses"][0] == calls[b]["uses"][0] == "P" else HOP
        for k in range(PASSES):
            fw = place_calls(lambda j: key[j], deps, users, lambda a, b: calls[a]["lag"] + hop(a, b))
            end = max(fw[j] + calls[j]["ns"] for j in range(n))
            if best is None or end <= best[0]:
                best = (end, fw)
            if now is None or end <= now[0] + SLACK * (1 - k / PASSES):
                now = (end, fw)
            u, mid, amp = shake.random(n), now[0] * float(shake.random()), SHAKE * (0.3 + float(shake.random()))
            src = fw if k < 4 else now[1]
            near = [amp * float(u[j]) if k >= 4 and abs(src[j] - mid) < SPAN else 0.0 for j in range(n)]
            if k % 2 and k >= 4:
                key = [src[j] + near[j] for j in range(n)]
            else:
                late = [-(src[j] + calls[j]["ns"]) + near[j] for j in range(n)]
                bw = place_calls(lambda j: late[j], users, deps, lambda a, b: calls[b]["lag"] + hop(a, b))
                key = [-(bw[j] + calls[j]["ns"]) for j in range(n)]
        PLAN.extend(sorted(range(n), key=lambda j: (best[1][j], j)))
        return PLAN

    def kind(x):
        return SCRATCH[PART[x[1]][0] if x[1] in PART else x[1]]

    def in_psum(x):
        return kind(x)[0] == "psum"

    def ns(out, a, two=False):
        if len(out) == 3:
            return 50.0 + 16 * out[2][4] * SCATTER
        if len(a) == 3:
            return 50.0 + out[4] * GATHER
        narrow = all(kind(x)[2] in ("bfloat16", "float16", "uint16") for x in (out, a))
        return max(55.0, 35.0 + out[4] * CYCLE * (2.0 if two else 0.5 if narrow else 1.0))

    def op(q, emit, reads, writes, t):
        def run():
            deps = {}
            for x in reads:
                need(q, x[1], x[2], x[3], False, deps)
            for x in writes:
                need(q, x[1], x[2], x[3], True, deps)
            waits(q, deps)
            s = "s" + q
            cnt[s] += 1
            c = cnt[s]
            emit(ENG[q]).then_inc(T.sem[s], 1)
            snap[(s, c)] = dict(known[q])
            for x in reads:
                note(q, x[1], x[2], x[3], s, c, False)
            for x in writes:
                note(q, x[1], x[2], x[3], s, c, True)
        call(q, run, reads, writes, t)

    def X(n, a=0, b=None, st=1):
        home, at, cols = PART[n] if n in PART else (n, 0, SCRATCH[n][1][1])
        if b is None:
            b = cols
        return (T[home][:, at + a:at + b:st] if st > 1 else T[home][:, at + a:at + b], n, a, b, len(range(a, b, st)))

    def PX(n, a, b, c0=0, c1=32):
        return (T["px%d" % n][:, a:b, c0:c1], "px%d" % n, 32 * a, 32 * b, (b - a) * (c1 - c0))

    def Hf(n, h):
        return X(n, 128 * h, 128 * h + 128)

    def Q(n, h):
        return X(n, 8 * h, 8 * h + 8)

    def IND(win, off):
        return (win[0].indirect(off[0]), win, off)

    def rd(x):
        return [x[1], x[2]] if len(x) == 3 else [x]

    def wr(out):
        return ([out[2]], [out[1]]) if len(out) == 3 else ([], [out])

    def tt(out, a, b, o):
        two = len(a) > 3 and not in_psum(a) and not in_psum(b)
        op("V", lambda e: e.tensor_tensor(out[0], a[0], b[0], o), rd(a) + rd(b) + wr(out)[0], wr(out)[1], ns(out, a, two))

    def ts(out, a, s1, o0, s2=None, o1=None):
        reads = rd(a)
        v1, v2 = s1, s2
        if isinstance(s1, tuple):
            reads = reads + [s1]; v1 = s1[0]
        if isinstance(s2, tuple):
            reads = reads + [s2]; v2 = s2[0]
        if o1 is None:
            op("V", lambda e: e.tensor_scalar(out[0], a[0], v1, None, o0), reads, [out], ns(out, a))
        else:
            op("V", lambda e: e.tensor_scalar(out[0], a[0], v1, v2, o0, o1), reads, [out], ns(out, a))

    def cp(out, a):
        op("V", lambda e: e.tensor_copy(out[0], a[0]), rd(a) + wr(out)[0], wr(out)[1], ns(out, a))

    def fill(x, v):
        op("V", lambda e: e.memset(x[0], v), [], [x], ns(x, x))

    def act(out, a, f, bias=None, scale=None, acc=None):
        kw = {}
        reads, writes = rd(a), [out]
        for nm, v in (("bias", bias), ("scale", scale)):
            if v is not None:
                if isinstance(v, tuple):
                    reads = reads + [v]; kw[nm] = v[0]
                else:
                    kw[nm] = v
        if acc is not None:
            writes = writes + [acc]; kw["accum_out"] = acc[0]
        t = ACT + out[4] * (GATHER if len(a) == 3 else CYCLE)
        op("S", lambda e: e.activation(out[0], a[0], f, **kw), reads, writes, t)

    def scp(out, a, scale=None):
        act(out, a, F.Copy, scale=scale)

    parts = {}
    mark = {}

    def mms(items, start=True, stop=True, part=None):
        if part is not None:
            parts[part] = parts.get(part, 0) + 1

        def run():
            deps = {}
            for (o, l, r) in items:
                need("P", o[1], o[2], o[3], True, deps)
                need("P", l[1], l[2], l[3], False, deps)
                need("P", r[1], r[2], r[3], False, deps)
            waits("P", deps)
            n = len(items)
            end = stop
            if part is not None:
                parts[part] -= 1
                end = stop and parts[part] == 0
            for j, (o, l, r) in enumerate(items):
                g.tensor.matmul(o[0], l[0], r[0], start and j == 0, end and j == n - 1).then_inc(T.sem.sP, 1)
            cnt["sP"] += n
            c = cnt["sP"]
            snap[("sP", c)] = dict(known["P"])
            for (o, l, r) in items:
                note("P", l[1], l[2], l[3], "sP", c, False)
                note("P", r[1], r[2], r[3], "sP", c, False)
            for (o, l, r) in items:
                note("P", o[1], o[2], o[3], "sP", c, True)
        t = sum(max(min(64, l[4]), r[4]) * (4 if kind(l)[2] == "float32" else 1) for (o, l, r) in items) * CYCLE / 2
        call("P", run, [x for it in items for x in it[1:]], [it[0] for it in items], t, adds=part is not None)

    dsem = {}

    def dma(q, name, out, src, nbytes):
        s = "d_" + name
        outs = [out] if isinstance(out, tuple) else []
        ins = [src] if isinstance(src, tuple) else []

        def run():
            deps = {}
            for o in outs:
                need(q, o[1], o[2], o[3], True, deps)
            for x in ins:
                need(q, x[1], x[2], x[3], False, deps)
            waits(q, deps)
            ENG[q].dma_start(out[0] if outs else out, src[0] if ins else src).then_inc(T.sem[s], 16)
            dsem[s] = 16
            snap[(s, 16)] = dict(known[q])
            for x in ins:
                note(q, x[1], x[2], x[3], s, 16, False)
            for o in outs:
                note(q, o[1], o[2], o[3], s, 16, True)
        call(q, run, ins, outs, 60.0, lag=DMA_LAG, nbytes=nbytes)

    def iota(x, pat, base, cm):
        kw = {} if x[1][-1] == "I" else {"allow_small_or_imprecise_dtypes": True}
        op("G", lambda e: e.iota(x[0], pat, base, cm, **kw), [], [x], 130.0 + 2 * CYCLE * x[4])

    def sel(out, a, pat, o, base, cm):
        op("G", lambda e: e.affine_select(out[0], a[0], pat, o, 0.0, base, cm), [a], [out], 170.0 + 2 * CYCLE * out[4])

    def gcp(out, a):
        sel(out, a, [[0, out[4]]], A.is_ge, 0, 0)

    loads = {"pv": (X("pvI"), T.pv[:, :], 8192), "pz": (X("zz0", 0, 256), T.pz[:, :], 65536), "th": (X("thI"), T.th[:, :], 1024),
             "xd": (X("xdS", 0, W), T.xd[:, :], 256 * W)}
    for j in range(len(PIECES) - 1):
        a, b = PIECES[j], PIECES[j + 1]
        loads["n%d" % j] = (X("nbI", a, b), T.nb[:, a:b], 512 * (b - a))
    done = DMA_LAG
    for j, name in enumerate(LOADS.split()):
        dma("YS"[j % 2], name, *loads[name])
        calls[-2]["run"]()
        done += calls[-1]["ns"] + 100.0
        calls[-2].update({"run": lambda: None, "uses": [name], "lag": 0.0})
        calls[-1].update({"ns": done, "uses": [name]})

    pc = lambda j: X("pC", j, j + 1)
    one = X("ones", 0, 128)
    iota(X("pI", 0, 1), [[1, 1]], 0, 1)
    fill(X("ones"), 1.0)
    fill(X("on32"), 1.0)
    fill(X("RST"), 1.0)
    fill(X("RST", 0, NK, SEG), 0.0)
    fill(X("tc"), -32.0)
    fill(X("xi"), -192.0)
    fill(Hf("EV", 0), 165.0)
    fill(Hf("EV", 1), 0.0)
    fill(pc(19), -1.0)
    fill(pc(24), -176.0)
    sel(X("ta", 0, 128), one, [[-16, 8], [0, 16]], A.is_ge, 0, 1)
    sel(X("BLK"), X("ta", 0, 128), [[16, 8], [0, 16]], A.is_ge, 15, -1)
    sel(X("ta", 128, 256), X("BLK"), [[1, 128]], A.is_ge, 0, -1)
    sel(X("LT"), X("ta", 128, 256), [[0, 8], [-1, 16]], A.is_ge, 14, 0)
    sel(X("CB"), X("BLK"), [[1, 128]], A.is_ge, -2, -1)
    for n, b in (("D0", 0), ("CA", -15), ("D1", 1)):
        sel(X(n), X("BLK"), [[-1, 128]], A.is_equal, b, 1)
    sel(X("Sp"), one, [[-1, 128]], A.is_equal, 16, 1)
    sel(X("Sm"), one, [[-1, 128]], A.is_equal, -16, 1)
    sel(X("ta", 0, 144), X("ones", 0, 144), [[-16, 9], [0, 16]], A.is_ge, 0, 1)
    sel(X("tb", 0, 144), X("ta", 0, 144), [[16, 9], [0, 16]], A.is_ge, 15, -1)
    sel(X("ZZ"), X("tb", 0, 144), [[0, 9], [1, 16]], A.is_equal, -15, 0)
    for c in range(2):
        sel(Hf("LOW", c), X("tc"), [[-1, 128]], A.is_ge, 0, 1)
    iota(X("rr"), [[0, 8], [1, 16]], 0, 0)
    iota(X("iI"), [[SEG, 8]], SEG - 1, 0)
    iota(X("iF"), [[2, 8]], 0, 0)
    iota(X("ii"), [[16, 16]], 0, 0)
    iota(X("w34"), [[-16, 2], [-1, 17]], 48 - 64, 0)
    iota(X("k34"), [[0, 2], [1, 17]], 0, 0)
    for j in range(4):
        iota(X("idW", 768 * j, 768 * j + 768), [[1, 768]], 768 * j - int(OFF), 0)

    ts(X("pI", 1, 2), X("pI", 0, 1), 15, A.bitwise_and)
    cp(pc(0), X("pI", 1, 2))
    cp(pc(20), X("pI", 0, 1))
    for j, (sh, m) in enumerate(((0, 1), (0, 3), (2, 1), (3, 1), (4, 1))):
        ts(X("pB", j, j + 1), X("pI", 0, 1), sh, A.arith_shift_right, m, A.bitwise_and)
    cp(X("pC", 1, 6), X("pB", 0, 5))
    ts(pc(6), pc(0), 14.0, A.not_equal, 2.0, A.mult)
    ts(pc(7), pc(6), -1.0, A.add)
    ts(pc(8), pc(0), 15.0, A.is_equal)
    ts(pc(9), pc(0), 15.0, A.is_lt)
    ts(pc(10), pc(1), -1.0, A.mult, 1.0, A.add)
    ts(pc(11), pc(5), -1.0, A.mult, 1.0, A.add)
    cp(X("VL0"), X("pvI"))
    scp(X("In"), X("D0"), -1.0)
    scp(X("D0n"), X("D0"), pc(9))
    tt(X("mt"), X("CA"), X("D0n"), A.subtract)
    tt(X("M1"), X("D1"), X("mt"), A.add)
    scp(X("M2a"), X("CB"), -256.0)
    scp(X("D2"), X("LT"))
    fill(X("D2", 14, 128, 16), 0.0)
    tt(X("M2"), X("M2a"), X("D2"), A.add)
    ts(pc(28), pc(0), 14.0, A.is_ge, 400.0, A.mult)
    ts(pc(27), pc(28), -200.0, A.add)
    for n, src, j in (("W00", "D0", 11), ("W11", "D0", 5), ("W01", "Sp", 11), ("W10", "Sm", 5)):
        ts(X(n), X(src), pc(j), A.mult)
    ts(pc(12), pc(2), 32.0, A.mult, pc(4), A.add)
    ts(pc(13), pc(3), 16.0, A.mult, pc(12), A.add)
    ts(X("LP"), X("iF"), pc(13), A.add)
    ts(X("Lq"), X("ii"), 1.0 / 16, A.mult)
    cp(Q("Lg", 0), X("iI"))
    ts(Q("Lg", 1), X("iF"), 0.5, A.mult, float(NK), A.add)
    ts(X("ZFe"), X("ZZ"), pc(10), A.mult)
    ts(X("ZFo"), X("ZZ"), pc(1), A.mult)
    cp(X("ZFa"), X("ZZ"))
    cp(X("thF"), X("thI"))
    scp(X("b8"), X("BLK", 0, 128, 16))
    cp(X("b8h"), X("b8"))
    scp(X("b8f"), X("b8"))
    ts(X("r15"), X("b8"), pc(8), A.mult)
    ts(X("SelP", 0, 16, 2), X("b8"), pc(10), A.mult)
    ts(X("SelP", 1, 16, 2), X("b8"), pc(1), A.mult)
    ts(pc(14), pc(0), 0.0, A.is_equal, BIG, A.mult)
    for n, v in (("b80", pc(14)), ("b8u", U), ("b8n", -BIG), ("b8p", BIG), ("b8m", -2 * BIG)):
        scp(X(n), X("b8"), v)
    ts(X("u34"), X("k34"), 0.0, A.mult, X("thF", 1, 2), A.add)
    fill(X("u34", 16, SEG, 17), 2.0)
    fill(X("h34"), -0.5)
    fill(X("h34", 16, 17), 0.5)
    fill(X("h34", 33, 34), 0.0)
    for n in range(8):
        scp(X("TH", SEG * n, SEG * n + SEG), X("u34"), X("b80", n, n + 1))
        scp(X("WH", SEG * n, SEG * n + SEG), X("h34"), X("b80", n, n + 1))
    ts(X("Hc", 0, 1), X("thF", 0, 1), -0.5, A.add)
    fill(X("w34", 16, 17), 2.0 - 64.0)
    fill(X("w34", 33, 34), 1.0)
    ts(pc(15), pc(9), -16.0, A.mult)
    ts(pc(16), pc(1), -2.0, A.mult, 1.0, A.add)
    ts(pc(17), pc(0), 14.0, A.is_lt, 16.0, A.mult)
    tt(pc(18), pc(16), pc(17), A.mult)
    ts(X("w34"), X("w34"), pc(8), A.mult)
    ts(X("t34"), X("k34"), pc(0), A.is_equal, pc(15), A.mult)
    tt(X("w34"), X("w34"), X("t34"), A.add)
    ts(X("w34", 0, 16), X("w34", 0, 16), pc(18), A.subtract)
    ts(X("w34", 17, 33), X("w34", 17, 33), pc(18), A.add)
    for n in range(8):
        scp(X("WP", SEG * n, SEG * n + SEG), X("w34"), X("b8u", n, n + 1))
    cp(X("I16"), X("D0"))
    cp(X("N16"), X("In"))
    scp(X("I32"), X("D0"))
    ts(X("MD"), X("rr"), pc(0), A.is_equal)
    ts(X("ii"), X("ii"), pc(0), A.add)
    scp(Hf("MD2", 0), Hf("MD", 0))
    scp(Hf("MD2", 1), Hf("MD", 0), -1.0)
    for h in range(2):
        ts(pc(21 + h), pc(20), W + 128 * h - MID, A.add)
    for n in BY_PE.split():
        fill(X("L" + n), 0.0)
    fill(X("uu"), U)
    sel(X("tb", 0, 128), one, [[-1, 16], [-16, 8]], A.is_equal, 0, 1)
    cp(X("RQ"), X("tb", 0, 128))
    cp(X("ii16"), X("ii"))
    ts(pc(25), pc(5), -3.0, A.mult, -1.0, A.add)
    ts(pc(26), pc(5), -0.75, A.mult, 1.0, A.add)
    ts(X("SB", 0, 1), pc(0), 12.0, A.is_lt, pc(25), A.mult)
    ts(X("eq12"), X("k34", 0, 12), pc(0), A.is_equal)
    act(X("sg12"), X("eq12"), F.Copy, scale=-2.0, bias=1.0)
    fill(X("pw12", 0, 1), 0.5)
    for b in (1, 2, 4, 8):
        scp(X("pw12", b, min(2 * b, 12)), X("pw12", 0, min(b, 12 - b)), 2.0 ** b)
    tt(X("pw12"), X("pw12"), X("eq12"), A.mult)
    for b in range(12):
        n = min(2 ** b, W - 2 ** b)
        scp(X("SB", 2 ** b, 2 ** b + n), X("SB", 0, n), X("sg12", b, b + 1))
    op("V", lambda e: e.tensor_reduce(pc(23)[0], X("pw12")[0], AxisListType.X, A.add), [X("pw12")], [pc(23)], 60.0)
    tt(pc(29), pc(23), pc(26), A.mult)
    scp(X("wv"), X("b8"), pc(29))
    tt(X("LOW"), X("LOW"), X("EV"), A.add)
    scp(X("EV"), X("EV"), 1.0 / 128)
    for a in range(0, W, 512):
        ts(X("nbS", a, a + 512), X("nbI", a, a + 512), -OFF, A.add)

    nxt = T.cores[(rank + 1) % len(T.cores)]
    prv = T.cores[(rank - 1) % len(T.cores)]
    adr = topo.addr(nxt)
    ne = len(topo.engines(core, nxt))
    n_in = len(topo.engines(prv, core))
    loc = [0]

    def send(dst, src, sem):
        def run():
            deps = {}
            need("G", src[1], src[2], src[3], False, deps)
            waits("G", deps)
            g.remote_dma(dst[0], src[0], T.sem[sem], T.sem.loc, adr[1], adr[0], topo.mask(core, nxt))
            loc[0] += ne
        call("G", run, [src], [dst], 150.0, lag=WAY)

    for t in range(1, 4):
        rec["VL%d" % t] = [(8 * h, 8 * h + 8, "R", "al%d%d" % (t, h), n_in, True) for h in range(2)]
        rec["zz%d" % t] = [(128 * h, 128 * h + 128, "R", "az%d%d" % (t, h), n_in, True) for h in range(2)]
        rec["E%d" % t] = [(1024 * b, 1024 * b + 1024, "R", "ae%d%d" % (t, b), n_in, True) for b in range(3)]
        rec["vI%d" % t] = [(0, 16, "R", "av%d" % t, n_in, True)]
        if t < 3:
            rec["OA%d" % t] = [(0, 16, "R", "ao%d" % t, n_in, True)]

    def ind_x(off):
        return IND(X("xdS", 0, W), off)

    def ind_n(off):
        return IND(X("nbS", 0, W), off)

    def level(t, h):
        z, z4, m4, n = Hf("zz%d" % t, h), "z4%d" % h, "m4%d" % h, MASKS[h]
        for out, src in ((Hf(z4, 0), z), (Hf(z4, 1), z), (X(z4, 256, 512), X(z4, 0, 256))):
            gcp(out, src)
        dz = Hf("zz%d" % t, 2 + h)
        tt(dz, ind_x(Q("VL%d" % t, h)), z, A.subtract)
        far = [Hf("far", 2 * h + s) for s in range(2)]
        for s in range(2):
            act(far[s], dz, F.Relu, bias=pc(19), scale=1.0 - 2 * s)
        ps = "pS%d" % h
        mms([(Hf(ps, c), X("M2"), f) for c in range(n) for f in far])
        act(X(m4, 0, 128 * n), X(ps, 0, 128 * n), F.Sigmoid, bias=pc(27), scale=400.0)
        while n < 4:
            gcp(X(m4, 128 * n, 256 * n), X(m4, 0, 128 * n))
            n *= 2
        ps = X("pM", 272, 400) if h else PX(0, 12, 16)
        mms([(ps, X("LT"), f) for f in far])
        act(Hf("Pb", h), ps, F.Relu, bias=pc(7), scale=-1.0)
        mms([(ps, X("M1"), Hf("Pb", h))])
        scp(Hf("ohS", h), ps)
        if t < 3:
            mms([(ps, X("D0"), dz), (ps, X("D0"), z), (ps, X("D0"), z)])
            act(Hf("xn", h), ps, F.Copy, bias=191.75, scale=0.5)

    def ccols(h, kh, par, a=0, b=64):
        c = 256 * h + 128 * kh + 64 * par
        return X("cU", c + a, c + b)

    def candidates(t, h):
        if t:
            cp(Hf("con", h), ind_n(Q("VL%d" % t, h)))
        else:
            ts(Hf("con", h), IND(X("nbI"), Q("VL0", h)), -OFF, A.add)
        for a in range(2):
            mms([(PX(1 - h, 0, 4, 16 * a, 16 * a + 16), X("W%d%d" % (a, b)), X("con", 128 * h + 64 * b, 128 * h + 64 * b + 64))
                 for b in range(2)])
        src, dst = PX(1 - h, 0, 4), Hf("TT", h)
        op("V", lambda e: e.transpose(dst[0], src[0]), [src], [dst], ns(dst, src))
        ts(Hf("Tt", h), IND(Hf("TT", h), X("LP")), OFF, A.add)
        for kh in range(2):
            s = 2048 * h + 1024 * kh
            for c in range(2):
                a = 128 * h + 64 * kh + 32 * c
                tt(X("mk", s + 512 * c, s + 512 * c + 512), ind_n(X("Tt", a, a + 32)), X("m4%d" % h), A.mult)
            for par, zz in ((0, "ZFe"), (1, "ZFo")):
                b = 4 + 4 * kh + 2 * par
                cuts = ((0, 1), (1, 2)) if h + kh + par < EARLY else ((0, 2),)
                for c0, c1 in cuts:
                    slot = PX((c0 + par) % 2 if h + kh == 0 else kh, b + c0, b + c1)
                    mms([(slot, X(zz, 15 - r, 143 - r), X("mk", s + 512 * c0 + r, s + 512 * c1, 16)) for r in range(16)])
                    if h + kh == 0:
                        ts(ccols(h, kh, par, 32 * c0, 32 * c1), slot, OFF, A.add)
            if h or kh:
                ts(ccols(h, kh, 0, 0, 128), PX(kh, 4 + 4 * kh, 8 + 4 * kh), OFF, A.add)

    def healthy(t):
        ps = X("pM", 0, 256)
        mms([(ps, X("M1"), X("Pb"))])
        tt(X("co"), ps, X("con"), A.mult)
        mms([(X("pM", 432, 448), X("ZFa", 15 - r, 143 - r), X("co", r, 256, 16)) for r in range(16)])
        ts(X("TLu"), X("pM", 432, 448), OFF, A.add)
        tt(X("d0"), ind_x(X("TLu")), X("zz%d" % t, 0, 256), A.subtract)
        act(X("d0"), X("d0"), F.Abs)
        mms([(ps, X("BLK"), X("d0"))])
        act(X("hb"), ps, F.Sign, bias=X("Hc", t, t + 1), scale=-1.0, acc=X("hs", t, t + 1))

    def keys(h):
        mms([(X("pM", 0, NK), Hf("Pb", h), X("WP")), (X("pM", 0, NK), Hf("hb", h), X("WH"))]
            + [(X("pM", k, NK, 17), Hf("mk", 16 * h + k), X("SelP")) for k in range(16)]
            + [(X("pM", 16, NK, SEG), Hf("co", h), X("b8h")), (X("pM", 33, NK, SEG), Hf("con", h), X("r15"))])
        scp(X("R%d" % h), X("pM", 0, NK))

    turn = [0]

    def distances(t, h):
        n = 0
        for way, w in WAYS[h]:
            kh, par, s = n // 4, n // 2 % 2, n % 2
            a = 4096 * h + 512 * n
            n += w
            dd, xg = X("dd", a, a + 512 * w), X("xg", a, a + 512 * w)
            src = ind_x(ccols(h, kh, par, 32 * s, 32 * (s + w)))
            if way == "S":
                act(xg, src, F.Copy)
                for b in range(a, a + 512 * w, 512):
                    ps = ("pS0", "pS1", "pN")[turn[0] % 3]
                    turn[0] += 1
                    mms([(Hf(ps, k), X("In"), Hf("zz%d" % t, h)) for k in range(4)], stop=False)
                    mms([(X(ps), X("D0"), X("xg", b, b + 512))], start=False)
                    act(X("dd", b, b + 512), X(ps), F.Abs)
                terms = (("dd", "b8n"),)
            else:
                tt(dd, src, X("z4%d" % h), A.subtract)
                ts(xg, dd, 0.0, A.max)
                terms = (("dd", "b8p"), ("xg", "b8m"))
            for c in range(w):
                for name, wt in terms:
                    mms([(X("pD%d" % h, 17 * par + 8 * kh + 4 * (s + c) + k, NK, SEG), Hf(name, a // 128 + 4 * c + k), X(wt)) for k in range(4)],
                        start=False, part="D%d%d" % (t, h))

    def eb(E, b, n):
        return Hf(E, 8 + 4 * (n // 2) + 2 * (b - 1) + n % 2 if b else n)

    def listed(name, small):
        return X("L" + name, 15, 143, 16) if name in BY_PE else small

    def to_list(name, out, small, more=()):
        if name in BY_PE:
            mms(list(more) + [(out, X("L" + name, 15 - r, 143 - r), Q("RQ", r)) for r in range(16)])
        else:
            tmp = Hf("W" + name[0], int(name[1]))
            tt(tmp, IND(small, Q("Lq", 0)), X("MD"), A.mult)
            mms(list(more) + [(out, tmp, X("b8f"))])

    def pairs(t, VL, E, vI, OA):
        for h in range(2):
            act(Hf("FE", h), IND(X("SB"), Q(VL, h)), F.Copy)
            mms([(Q("pM", 62 + h), Hf("FE", h), X("wv"))])
            act(Q(vI, h), Q("pM", 62 + h), F.Copy, bias=(U - 1) / 2 - MID)
        for blocks in (((0, 0),), ((0, 1), (1, 1))):
            for a in range(4):
                ps, w = ("pN", "pS1")[a % 2], 256 * len(blocks)
                part = lambda m, h: (T.FE[32 * a:32 * a + 16 * (m + 1), 128 * h:128 * h + 128], "FE", 128 * h, 128 * h + 128, 128)
                mms([(X(ps, w - 256, w), X("D0"), X("LOW"))] + [(Hf(ps, 0), one, Hf("EV", 0))] * (len(blocks) - 1)
                    + [(Hf(ps, 2 * k + m), part(m, ha), part(m, hb)) for k, (ha, hb) in enumerate(blocks) for m in range(2)])
                at = 1024 * (len(blocks) - 1) + w * a
                act(X(E, at, at + w), X(ps, 0, w), F.Relu, bias=pc(24))
                if t and (at + w) % 1024 == 0:
                    send(X("E%d" % t, at + w - 1024, at + w), X(E, at + w - 1024, at + w), "ae%d%d" % (t, at // 1024))
                    calls[-1]["deps"].add(mark["z"])
        if t:
            send(X("vI%d" % t), X(vI), "av%d" % t)
        if t < 3:
            for h in range(2):
                mms([(Q("pM", 52 + h), X("I32"), Q(vI, h))]
                    + [(X("pM", 416 + 8 * h + n, 417 + 8 * h + n), eb(E, b, n), X("uu")) for b in ((0,), (1, 2))[h] for n in range(8)])
                ts(listed("a%d" % h, Q("ua", h)), Q("pM", 52 + h), pc(21 + h), A.min)
                to_list("a%d" % h, Q("pM", 56 + h), Q("ua", h))
            ts(X(OA), X("pM", 448, 464), MID, A.add)
            if t:
                send(X("OA%d" % t), X(OA), "ao%d" % t)

    def best(t, h):
        sc, pk, top = X("sc%d" % h, 0, NK), X("R%d" % h), X("sc%d" % h, SEG - 1, NK, SEG)
        tt(pk, X("pD%d" % h, 0, NK), pk, A.min)
        op("V", lambda e: e.tensor_tensor_scan(sc[0], T.RST[:, :], pk[0], 0.0, A.mult, A.max), [X("RST"), pk], [sc], ns(sc, pk))
        ts(Q("rep", h), top, 3 * U - OFF, A.is_ge, U, A.mult)
        E, u = "E%d" % t, Q("pD0", 35 + h)
        count = lambda b, ha, hb: [(X("pD0", 280 + 8 * hb + n, 281 + 8 * hb + n), eb(E, b, n), X("rep", 8 * ha + n, 8 * ha + n + 1)) for n in range(8)]
        if h == 0:
            mms([(u, X("I32"), Q("vI%d" % t, 0)), (u, X("In"), Q("rep", 0))] + count(0, 0, 0))
        else:
            mms([(u, X("In"), Q("rep", 1))] + count(2, 1, 1), start=False)
        ts(listed("o%d" % h, Q("uo", h)), u, U, A.add, pc(21 + h), A.min)
        if h == 0:
            mms([(Q("pD0", 36), X("I32"), Q("vI%d" % t, 1))] + count(1, 0, 1), stop=False)
            calls[-1]["deps"].add(len(calls) - 2)
        to_list("o%d" % h, Q("pM", 58 + h), Q("uo", h))
        ts(Q("offR", h), Q("pM", 58 + h), MID, A.add)
        val = Q("pM", 60 + h)
        ts(X("sc%d" % h, NK, NK + 8), top, 1.5 * 2.0 ** 35, A.add, 1.5 * 2.0 ** 35, A.subtract)
        if "c%d" % h in BY_PE:
            tt(listed("c%d" % h, None), top, X("sc%d" % h, NK, NK + 8), A.subtract)
            to_list("c%d" % h, val, None)
        else:
            tt(X("Vm"), IND(X("sc%d" % h), X("Lg")), X("MD2"), A.mult)
            mms([(val, Hf("Vm", k), X("b8f")) for k in range(2)])
        ts(Q("VN%d" % t, h), val, OFF, A.add)
        if t < 3:
            send(Q("VL%d" % (t + 1), h), Q("VN%d" % t, h), "al%d%d" % (t + 1, h))
        else:
            act(Q("yvS", h), val, F.Copy, bias=OFF)
        ts(listed("z%d" % h, Q("zf", h)), top, 2 * U - OFF, A.is_lt, 256.0, A.mult)
        to_list("z%d" % h, Q("pM", 51), Q("zf", h), [(Q("pM", 51), X("I16"), Q("ii16", h))])
        cp(Q("zo", h), Q("pM", 51))
        zn = Hf("zn%d" % t, h)
        act(zn, IND(X("zz%d" % t), Q("zo", h)), F.Abs)
        mark["z"] = len(calls) - 1
        if t < 3:
            send(Hf("zz%d" % (t + 1), h), zn, "az%d%d" % (t + 1, h))
        else:
            dma("Y", "yz%d" % h, T.yz[:, 128 * h:128 * h + 128], zn, 32768)
        tt(Hf("no", h), IND(X("idW"), Q("VN%d" % t, h)), Hf("ohS", h), A.mult)
        tt(IND(X("nbS" if t < 3 else "yn", 0, WT), Q("offR", h)), Hf("no", h), Hf("A1", h), A.add)

    pairs(0, "VL0", "E0", "vI0", "OA0")
    for t in range(4):
        last = t == 3
        if last:
            act(X("yn", 0, W), X("nbS", 0, W), F.Copy, bias=OFF)
        for h in range(2):
            level(t, h)
            candidates(t, h)
            mms([(X("pD%d" % h, 0, NK)[:3] + (512, NK), one, X("TH"))], stop=False)
        healthy(t)
        keys(0)
        mms([(X("pM", 0, 256), X("I16"), X("con")), (X("pM", 0, 256), X("N16"), X("co"))])
        act(X("A1"), X("pM", 0, 256), F.Copy, bias=OFF if last else 0.0)
        keys(1)
        if not last:
            mms([(X("pM", 400, 401), X("on32"), X("hs", t, t + 1))])
            ts(X("hi0", t, t + 1), X("pM", 400, 401), -1.0 / 32, A.mult, 1024.0, A.add)
            ts(X("hi1", t, t + 1), X("hi0", t, t + 1), 15, A.bitwise_and)
            tt(X("Hc", t + 1, t + 2), X("hi1", t, t + 1), X("Hc", 0, 1), A.add)
        for h in range(2):
            distances(t, h)
        for h in range(2):
            best(t, h)
        if not last:
            tt(IND(X("xdS", 0, WT), X("OA%d" % t)), X("xn"), X("xi"), A.add)
            pairs(t + 1, "VN%d" % t, "EO%d" % t, "vO%d" % t, "OO%d" % t)
        else:
            dma("Y", "yv", T.yv[:, :], X("yvS"), 8192)

    dma("S", "yn", T.ynb[:, :], X("yn", 0, W), 512 * W)
    for j in plan():
        calls[j]["run"]()
    fin = dict(cnt)
    fin.update(dsem)
    fin["loc"] = loc[0]
    for s in fin:
        if known["G"].get(s, 0) < fin[s]:
            g.wait_ge(T.sem[s], fin[s])
